import numpy as np, ml_dtypes
CORES = [3,7,11,15,131,135,139,143]
N = 8
BF = ml_dtypes.bfloat16
def gentries(a):
    return np.ascontiguousarray(a.reshape(8, 16, -1).transpose(0, 2, 1)).reshape(8, -1)
def gtable(e):
    e = np.asarray(e); return np.ascontiguousarray(e.reshape(8, -1, 16).transpose(0, 2, 1)).reshape(128, -1).astype(np.int32)
V, G, B, L, RO = 1024, 256, 3, 64, 3
W = V + B * G
def numbers(rng, ghost):
    s = (N, 8, V, 16)
    return np.where(rng.random(s) < ghost, rng.integers(V, W, s), rng.integers(0, V, s))
def image(t, nb):
    tw = np.concatenate([t, np.broadcast_to(np.arange(V, W), (N, 8, W - V))], axis=2)
    e = np.take_along_axis(tw, nb.reshape(N, 8, -1), 2).reshape(nb.shape)
    return np.take_along_axis(e, np.argsort(t, axis=-1)[..., None], 2)
def parts(rng, z, wild, mix):
    t = np.argsort(rng.random((N, 8, V)), axis=-1); nb = numbers(rng, 0.125)
    nz = np.where(rng.random(nb.shape) < wild, numbers(rng, 0.125), image(t, nb))
    x = np.clip(np.take_along_axis(z, t[:, :, None, :], 3) + rng.integers(-2, 3, z.shape), 0, 255)
    x = np.where(rng.random(z.shape) < 0.1, rng.integers(0, 256, z.shape), x)
    o = np.argsort(rng.random((N, 8, V)), axis=-1); m = t.copy()
    for r in range(N):
        for g in range(8):
            j = o[r, g, :int(V * mix[r, g])]; m[r, g, j] = t[r, g, np.roll(j, 1)]
    bx = np.ascontiguousarray(np.argsort(rng.random((N, 8, V)), axis=-1)[..., :G]); bz = np.take_along_axis(t, bx, 2)
    return {"x": x, "z": z, "nb": nb, "nz": nz, "m": m, "bx": bx, "bz": bz}
def pack(d):
    return {"x": np.ascontiguousarray(d["x"].reshape(N, 128, V)).astype(np.float32).astype(BF), "z": np.ascontiguousarray(d["z"].reshape(N, 128, V)).astype(np.float32).astype(BF),
            "nb": np.stack([gtable(a.reshape(8, -1)) for a in d["nb"]]), "nz": np.stack([gtable(a.reshape(8, -1)) for a in d["nz"]]),
            "m": d["m"].astype(np.int32), "im": np.argsort(d["m"], axis=-1).astype(np.int32),
            "bx": np.stack([gtable(a) for a in d["bx"]]), "bz": np.stack([gtable(a) for a in d["bz"]])}
def setup_inputs(rng):
    size = rng.permuted(np.tile(np.array([1, 1, 3, 3, 15, 63, 255, 255]), (N, 1)), axis=1)[:, :, None, None]
    z = rng.integers(0, size + 1, (N, 8, 16, V))
    wild = rng.choice(np.array([0.05, 0.2, 0.5, 1.0]), (N, 8, 1, 1)); mix = rng.choice(np.array([0.1, 0.3, 0.6, 1.0]), (N, 8))
    h = int(rng.integers(0, 8)); wild[:, h] = 0.0; mix[:, h] = 0.05
    return pack(parts(rng, z, wild, mix))
def setup_inputs_ties(rng):
    z = rng.integers(0, 2, (N, 8, 16, V)) * (rng.random((N, 8, 1, V)) < 0.5); z[:, 1, 1:] = 0
    d = parts(rng, z, rng.choice(np.array([0.2, 1.0]), (N, 8, 1, 1)), np.full((N, 8), 0.8))
    u = (np.arange(L) * (V // L))[1::2]
    for r in range(N):
        for g in (0, 2, 4, 6):
            s0 = np.flatnonzero(np.all(z[r, g] == 0, axis=0)); im = np.argsort(d["m"][r, g])
            d["nb"][r, g, u] = im[rng.choice(s0, (len(u), 16))]; d["nz"][r, g, d["m"][r, g, u]] = rng.choice(s0, (len(u), 16))
    d["nb"][:, 5] = rng.integers(0, V, (N, 1, 16))
    return pack(d)
def setup_inputs_crowd(rng):
    z = rng.integers(0, rng.choice(np.array([3, 15, 255]), (N, 8, 1, 1)) + 1, (N, 8, 16, V))
    d = parts(rng, z, np.ones((N, 8, 1, 1)), np.ones((N, 8)))
    for r in range(N):
        for g in range(8):
            n = (24, 160)[g % 2]
            s = np.concatenate([np.array([0, V - 1]), 1 + rng.permutation(V - 2)[:n - 2]]); e = np.concatenate([np.array([0, V - 1]), 1 + rng.permutation(V - 2)[:n - 2]])
            if g < 4: e = d["m"][r, g, s]
            ends = np.array([V, W - 1])
            d["nb"][r, g] = np.where(rng.random((V, 16)) < 0.05, rng.choice(ends, (V, 16)), rng.choice(s, (V, 16)))
            d["nz"][r, g] = np.where(rng.random((V, 16)) < 0.05, rng.choice(ends, (V, 16)), rng.choice(e, (V, 16)))
            d["bx"][r, g] = rng.choice(s, G); d["bz"][r, g] = rng.choice(e, G)
    return pack(d)
def setup_inputs_border(rng):
    z = rng.integers(0, rng.choice(np.array([3, 15, 255]), (N, 8, 1, 1)) + 1, (N, 8, 16, V))
    d = parts(rng, z, np.ones((N, 8, 1, 1)), np.ones((N, 8)))
    for r in range(N):
        for g in range(8):
            s = rng.permutation(V)[:160]; e = d["m"][r, g, s]
            d["nb"][r, g] = np.where(rng.random((V, 16)) < 0.3, rng.integers(V, W, (V, 16)), rng.choice(s, (V, 16)))
            d["nz"][r, g] = np.where(rng.random((V, 16)) < 0.3, rng.integers(V, W, (V, 16)), rng.choice(e, (V, 16)))
            d["bx"][r, g] = rng.choice(s, G); d["bz"][r, g] = rng.choice(e, G)
    d["bx"][:, :, 0] = 0; d["bx"][:, :, G - 1] = V - 1; d["bz"][:, :, 0] = V - 1; d["bz"][:, :, G - 1] = 0
    q = rng.permutation(8); d["nb"][:, q[0]] = rng.integers(V, W, (N, V, 16)); d["nz"][:, q[1]] = rng.integers(V, W, (N, V, 16))
    d["nb"][:, :, 0, :2] = np.array([V, W - 1])
    return pack(d)
def agree(d, r, g):
    t = np.concatenate([d["m"][r, g], np.arange(V, W)]); d["nz"][r, g, t[:V]] = t[d["nb"][r, g]]
def early(rng, d, r, g, n):
    st = np.arange(L) * (V // L); o = rng.permutation(np.setdiff1d(np.arange(V), np.concatenate([st, d["bx"][r, g]])))
    p = o[:2 * n]; a = d["nb"][r, g][st]; a[np.isin(a, p)] = o[2 * n]
    a[rng.permutation(L)[:n], rng.integers(0, 16, n)] = p[:n]; d["nb"][r, g, st] = a
    agree(d, r, g); t = d["m"][r, g].copy(); d["m"][r, g, p] = t[np.roll(p, n)]
def late(rng, d, r, g):
    st = np.arange(L) * (V // L); o = rng.permutation(np.setdiff1d(np.arange(V), np.concatenate([st, d["bx"][r, g], np.array([819, V - 1])])))
    p = o[:6].copy(); s = p[:3]; f = int(o[6]); b = o[7:7 + L].copy(); c = o[7 + L:7 + 2 * L].copy(); rest = o[7 + 2 * L:]
    j = 1 + rng.permutation(L - 1)[:3]; b[j[0]] = 819
    nb = d["nb"][r, g]; nb[np.isin(nb, p)] = f
    nb[p] = rng.choice(rest, (6, 16)); nb[s, rng.integers(0, 16, 3)] = f
    nb[st, 0] = b; nb[b, 0] = c; nb[819, 0] = rng.integers(V, W)
    nb[np.array([b[j[1]], c[j[2]], V - 1]), rng.integers(1, 16, 3)] = s
    agree(d, r, g); t = d["m"][r, g].copy(); z = d["z"][r, g]
    z[:] = rng.integers(0, 200, (16, 1)); z[:, t[s]] += rng.integers(1, 5, (16, 3)); z[int(rng.integers(0, 16)), t[f]] += rng.integers(1, 16)
    d["m"][r, g, p] = t[np.roll(p, 3)]
def setup_inputs_still(rng):
    z = rng.integers(0, 256, (N, 8, 16, V)); d = parts(rng, z, np.zeros((N, 8, 1, 1)), np.zeros((N, 8)))
    q, q2, q3 = [int(i) for i in rng.permutation(N)[:3]]; h, h2 = [int(i) for i in rng.permutation(8)[:2]]; st = np.arange(L) * (V // L)
    room = [L] + [(287 - L + i) // 5 for i in range(5)]
    for r in range(N):
        for g in range(8):
            if r == q or g == h: continue
            if r in (q2, q3):
                if g == h2: late(rng, d, r, g)
                elif r == q3: early(rng, d, r, g, room.pop())
                continue
            c = np.unique(d["nb"][r, g, st]); c = np.setdiff1d(c[c < V], np.concatenate([st, d["bx"][r, g]]))
            p = rng.permutation(c)[:2 * int(rng.integers(1, 4))]
            d["m"][r, g, p] = d["m"][r, g, p.reshape(-1, 2)[:, ::-1].reshape(-1)]
    return pack(d)
def setup_inputs_spread(rng):
    z = (np.exp2(8 * rng.random((N, 8, 1, V))) * rng.random((N, 8, 16, V)) * (rng.random((N, 8, 1, V)) > 0.0625)).astype(np.int64)
    wild = rng.choice(np.array([0.05, 0.3, 1.0]), (N, 8, 1, 1)); mix = rng.choice(np.array([0.2, 0.5, 1.0]), (N, 8))
    for h in rng.permutation(8)[:2]:
        u = rng.integers(0, 4, (N, 16, V)); z[:, h] = np.where(rng.random((N, 1, V)) < 0.5, u, 255 - u); wild[:, h] = 1.0; mix[:, h] = 1.0
    return pack(parts(rng, z, wild, mix))
def check_inputs(d):
    bad = []
    for k in ("x", "z"):
        a = np.asarray(d[k]).astype(np.float32)
        if not np.all((a >= 0) & (a <= 255) & (a == np.floor(a))): bad.append("whole numbers 0 to 255 in " + k)
    for k, hi in (("nb", W - 1), ("nz", W - 1), ("m", V - 1), ("im", V - 1), ("bx", V - 1), ("bz", V - 1)):
        if np.min(d[k]) < 0 or np.max(d[k]) > hi: bad.append("range of " + k)
    if not np.all(np.sort(d["m"], axis=-1) == np.arange(V)): bad.append("m is a bijection")
    elif not np.all(np.argsort(d["m"], axis=-1) == d["im"]): bad.append("im is the inverse of m")
    return bad
def reference(x, z, nb, nz, m, im, bx, bz):
    X = x.astype(np.float32).astype(np.int64).reshape(N, 8, 16, V); Z = z.astype(np.float32).astype(np.int64).reshape(N, 8, 16, V)
    nv = np.stack([gentries(a) for a in nb]).astype(np.int64).reshape(N, 8, V, 16); ns = np.stack([gentries(a) for a in nz]).astype(np.int64).reshape(N, 8, V, 16)
    M = m.astype(np.int64); I = im.astype(np.int64)
    b1 = np.stack([gentries(a) for a in bx]).astype(np.int64); b2 = np.stack([gentries(a) for a in bz]).astype(np.int64)
    lane = np.arange(L); v = np.tile(lane * (V // L), (N, 8, 1)); last = np.zeros(N, np.int64)
    for rnd in range(RO):
        Y = np.take_along_axis(Z, M[:, :, None, :], 3)
        ey = np.take_along_axis(Y, b1[:, :, None, :], 3); ez = np.take_along_axis(Z, b2[:, :, None, :], 3)
        YW = np.concatenate([Y] + [np.roll(ey, -d, axis=0) for d in range(1, B + 1)], axis=3)
        ZW = np.concatenate([Z] + [np.roll(ez, -d, axis=0) for d in range(1, B + 1)], axis=3)
        th = last & 31; last = np.zeros(N, np.int64)
        for r in range(N):
            for g in range(8):
                Yg, Zg, n1, n2, at = YW[r, g], ZW[r, g], nv[r, g], ns[r, g], v[r, g].copy()
                na = n1[at]; nq = n2[M[r, g, at]]
                D = np.add.reduce(np.abs(Yg[:, na] - Zg[:, nq]), axis=0); k = np.argmax(D, axis=1)
                a = na[lane, k]; q = nq[lane, k]; live = (D[lane, k] > 0) & (a < V) & (q < V)
                ac = np.minimum(a, V - 1); qc = np.minimum(q, V - 1); w = I[r, g, qc]; p = M[r, g, ac]
                Aa = Yg[:, n1[ac]]; Aw = Yg[:, n1[w]]; Ba = Zg[:, n2[p]]; Bw = Zg[:, n2[qc]]
                gain = np.add.reduce(np.abs(Aa - Ba) + np.abs(Aw - Bw) - np.abs(Aa - Bw) - np.abs(Aw - Ba), axis=(0, 2))
                prop = live & (gain > th[r])
                first = np.full(V, L); np.minimum.at(first, ac[prop], lane[prop]); np.minimum.at(first, w[prop], lane[prop])
                com = prop & (first[ac] >= lane) & (first[w] >= lane)
                last[r] += np.count_nonzero(com)
                v[r, g] = np.where(com, a, np.where(q < V, w, (5 * at + 1) & (V - 1)))
                a, w, p, q = a[com], w[com], p[com], q[com]
                M[r, g, a] = q; M[r, g, w] = p; I[r, g, q] = a; I[r, g, p] = w
                for vert, site in ((a, q), (w, p)):
                    old = Z[r, g][:, site]; Z[r, g][:, site] = old + np.clip(X[r, g][:, vert] - old, -1, 1)
    return {"mo": M.astype(np.float32), "zo": Z.reshape(N, 128, V).astype(np.float32).astype(BF)}

@@ -1,0 +1,492 @@
+from concourse.mybir import AluOpType as O, AxisListType, ActivationFunctionType as AF
+
+F4, B2, I4, U2 = "float32", "bfloat16", "int32", "uint16"
+_W = {
+    B2: dict(ZW=1920, YW=1920, tX=1024, SY=768, SZ=768, Yt=1024, Zt=1024, ng=512, AD=1024, At=1024, Bt=1024, Bp=1024, T1=1024,
+             T2=1024, R1=1024, R2=1024, zz=128, xx=128, cl=128, nzv=128, EQ=640, gh=128, kz2=64, npr=64, WT=512, cnt=2,
+             identb=128, identn=128, biasd=128, blkp=128, blkm=128, blkV=128, idV=128, idN=128, Es=144, W4=512, ones64=64,
+             onesb=128),
+    F4: dict(MF=1152, mlf=256, nf=128, KT=64, Fs=64, OHt=64, pr=128, mk=128, sc=128, WP=128, AQ=128, NR=128, mk2=128,
+             sc2=128, NLc=16, kz=64, TH=64, x1=64, sp=64, cm=64, cl2=64, VL=4, V5=4, oq=4, d1=4, d2=4, alt=4, da=4,
+             d3=4, cn=2, thc=2, onesf=128, b1=128, blkf=128, ff=2, f15=2, itf=128, mask=128, reset=128, identf=128, q25=16,
+             s0=16, pwr=16, pm=16, pwc=2, c25=64, c00=64, thr=64, t1=64, mm1=64, thrM=64, nmB=64, c16f=4, lane4=4),
+    I4: dict(tNB=1024, tNZ=1024, tNZM=1152, tNBI=1152, tM=1152, tIM=1152, ml=256, bl=32, v5a=4, v5b=4, thi=2, thj=2, c_it=128,
+             c_p=2, c_c16=4, fI=2),
+    U2: dict(ML=128, BL=32, L1=128, LAQ=8, L2=256, LWP=8, OFF=16, vl=4),
+}
+SCRATCH = {n: ("sbuf", [128, w], d) for d in _W for n, w in _W[d].items()}
+for _i in range(8):
+    SCRATCH["pb%d" % _i] = ("psum", [128, 512], F4)
+SEMAPHORES = ["cv", "cs", "cp", "cg", "ld_z", "ld_b", "ld_m", "ld_im", "ld_nz", "ld_nb", "ld_x", "ld_M", "ld_IM", "st_z", "st_m",
+              "rdy1", "rdy2", "sl"] + ["%s%s%d" % (a, w, e) for a in "ab" for w in "YZ" for e in range(3)]
+N = 8
+OWN = 128
+CFG = dict(CH=[(0, 24), (24, 44), (44, 64)],
+           YS=24,
+           AS=32)
+
+
+def rank_program(g, core, T, topo):
+    rank = T.rank_of(core)
+    if rank is None:
+        return
+    QUEUE = {"V": g.vector, "S": g.scalar, "P": g.tensor, "G": g, "Y": g.sync}
+    SEM = {"V": "cv", "S": "cs", "P": "cp", "G": "cg"}
+    cnt = {"cv": 0, "cs": 0, "cp": 0, "cg": 0}
+    total = {}
+    seen = {q: {} for q in QUEUE}
+    acc = {}
+    CH, YS, AS = CFG["CH"], CFG["YS"], CFG["AS"]
+
+    def need(q, sem, val):
+        if seen[q].get(sem, 0) < val:
+            QUEUE[q].wait_ge(T.sem[sem], val)
+            seen[q][sem] = val
+
+    def order(q, reads, writes):
+        w = {}
+        for kind, regs in (("r", reads), ("w", writes)):
+            for (n, a, b) in regs:
+                ps = n[:2] == "pb"
+                for (a2, b2, k2, q2, s2, v2) in acc.get(n, ()):
+                    if ps:
+                        if q2 == q and (q == "P" or (kind == "r" and k2 == "r")):
+                            continue
+                    else:
+                        if (kind == "r" and k2 == "r") or b2 <= a or b <= a2:
+                            continue
+                    w[s2] = max(w.get(s2, 0), v2)
+        for s, v in w.items():
+            need(q, s, v)
+
+    def record(q, reads, writes, sem, val):
+        for kind, regs in (("r", reads), ("w", writes)):
+            for (n, a, b) in regs:
+                l = [e for e in acc.get(n, []) if not (e[0] == a and e[1] == b and e[2] == kind and e[3] == q)]
+                l.append((a, b, kind, q, sem, val))
+                acc[n] = l
+
+    def emit(q, calls, outs, ins):
+        reads = [r for i in ins for r in i[1] + i[2]] + [r for o in outs for r in o[2]]
+        writes = [r for o in outs for r in o[1]]
+        order(q, reads, writes)
+        for c in calls:
+            last = c()
+        s = SEM[q]
+        cnt[s] += 1
+        last.then_inc(T.sem[s], 1)
+        record(q, reads, writes, s, cnt[s])
+
+    def R(n, a, b, s=1):
+        return (T[n][:, a:b] if s == 1 else T[n][:, a:b:s], [(n, a, b)], [])
+
+    def C(n, c=0):
+        return R(n, c, c + 1)
+
+    def IND(n, a, b, off):
+        return (T[n][:, a:b].indirect(off[0]), [(n, a, b)], off[1])
+
+    def tup(*xs):
+        return [x for x in xs if isinstance(x, tuple)]
+
+    def raw(x):
+        return x[0] if isinstance(x, tuple) else x
+
+    def vcopy(o, i):
+        emit("V", [lambda: g.vector.tensor_copy(out=o[0], in_=i[0])], [o], [i])
+
+    def vtt(o, a, b, op):
+        emit("V", [lambda: g.vector.tensor_tensor(out=o[0], in0=a[0], in1=b[0], op=op)], [o], [a, b])
+
+    def vts(o, a, s1, s2, op0, op1=None):
+        if op1 is None:
+            f = lambda: g.vector.tensor_scalar(out=o[0], in0=a[0], scalar1=raw(s1), scalar2=None, op0=op0)
+        else:
+            f = lambda: g.vector.tensor_scalar(out=o[0], in0=a[0], scalar1=raw(s1), scalar2=raw(s2), op0=op0, op1=op1)
+        emit("V", [f], [o], [a] + tup(s1, s2))
+
+    def vscan(o, d0, d1, init, op0, op1):
+        emit("V", [lambda: g.vector.tensor_tensor_scan(out=o[0], data0=d0[0], data1=d1[0], initial=init, op0=op0, op1=op1)],
+             [o], [d0, d1])
+
+    def vset(o, c):
+        emit("V", [lambda: g.vector.memset(o[0], c)], [o], [])
+
+    def vtr(o, i):
+        emit("V", [lambda: g.vector.transpose(out=o[0], in_=i[0])], [o], [i])
+
+    def vsum(o, i):
+        emit("V", [lambda: g.vector.tensor_reduce(out=o[0], in_=i[0], axis=AxisListType.X, op=O.add)], [o], [i])
+
+    def sact(o, i, func=AF.Copy, scale=1.0):
+        emit("S", [lambda: g.scalar.activation(out=o[0], in_=i[0], func=func, scale=raw(scale))], [o], [i] + tup(scale))
+
+    def mm(o, l, r, st, sp):
+        return (lambda: g.tensor.matmul(o[0], l[0], r[0], st, sp)), o, l, r
+
+    def pe(ms):
+        emit("P", [m[0] for m in ms], [m[1] for m in ms], [x for m in ms for x in (m[2], m[3])])
+
+    def load(q, sem, o, in_ap, tot):
+        order(q, [], o[1])
+        QUEUE[q].dma_start(out=o[0], in_=in_ap).then_inc(T.sem[sem], 16)
+        total[sem] = 16 * tot
+        record("D" + sem, [], o[1], sem, 16 * tot)
+
+    def store(q, sem, out_ap, i):
+        order(q, i[1], [])
+        QUEUE[q].dma_start(out=out_ap, in_=i[0]).then_inc(T.sem[sem], 16)
+        total[sem] = 16
+
+    def lists(a, sem, src):
+        for k in range(8):
+            c = a + 16 * k
+            load("Y", sem, (T.ml[0:64, c:c + 16], [("ml", c, c + 16)], []), src[k:k + 1, :], 8)
+
+    def spread(sem, n, src):
+        for f in range(16):
+            load("Y", sem, (T[n][f:128:16, OWN:OWN + 1024], [(n + "_" + str(f), 0, 1)], []), src[:], 16)
+        record("D" + sem, [], [(n, OWN, OWN + 1024)], sem, 256)
+    load("S", "ld_b", R("bl", 0, 16), T.bx[:], 2)
+    load("S", "ld_b", R("bl", 16, 32), T.bz[:], 2)
+    lists(0, "ld_m", T.m)
+    load("S", "ld_z", R("ZW", OWN, OWN + 1024), T.z[:], 1)
+    load("Y", "ld_nz", R("tNZ", 0, 1024), T.nz[:], 1)
+    lists(128, "ld_im", T.im)
+    load("Y", "ld_nb", R("tNB", 0, 1024), T.nb[:], 1)
+
+    def giota(o, pat, ch):
+        emit("G", [lambda: g.iota(o[0], pat, 0, ch)], [o], [])
+
+    def gsel(o, i, pat, base, ch):
+        emit("G", [lambda: g.affine_select(o[0], i[0], pat, O.is_ge, 0.0, base, ch)], [o], [i])
+    a128 = lambda n: R(n, 0, 128)
+    a64 = lambda n: R(n, 0, 64)
+    MP = R("pb6", 256, 384)
+    vset(a128("onesf"), 1.0)
+    giota(R("c_p", 0, 2), [[0, 2]], 1)
+    giota(a128("c_it"), [[0, 8], [1, 16]], 0)
+    gsel(a128("b1"), a128("onesf"), [[-16, 8], [0, 16]], 0, 1)
+    gsel(a128("blkf"), a128("b1"), [[16, 8], [0, 16]], 15, -1)
+    giota(R("c_c16", 0, 4), [[16, 4]], 0)
+    vset(a64("ones64"), 1.0)
+    vset(R("Es", 0, 144), 0.0)
+    vset(a64("c25"), 0.25)
+    vset(a64("c00"), 0.0)
+    vts(R("fI", 0, 2), R("c_p", 0, 2), 15, None, O.bitwise_and)
+    vcopy(a128("itf"), a128("c_it"))
+    vcopy(R("ff", 0, 2), R("fI", 0, 2))
+    vts(a128("reset"), a128("itf"), 0.0, None, O.is_gt)
+    vts(a128("mask"), a128("itf"), C("ff"), None, O.is_equal)
+    vts(C("f15"), C("ff"), -1.0, 15.0, O.mult, O.add)
+    vscan(a64("thr"), a64("c25"), a64("c00"), 3.0 * 4.0 ** 33, O.mult, O.add)
+    vtt(a128("identf"), a128("blkf"), a128("mask"), O.mult)
+    vcopy(MP, a128("mask"))
+    vts(R("Es", 15, 143, 16), R("blkf", 0, 128, 16), 16.0, None, O.mult)
+    vts(a128("identn"), a128("identf"), -1.0, None, O.mult)
+    vcopy(a128("identb"), a128("identf"))
+    vcopy(R("BL", 0, 32), R("bl", 0, 32))
+    vts(a128("biasd"), a128("identf"), C("f15"), None, O.mult)
+    vts(R("q25", 0, 16), R("reset", 0, 16), 0.25, None, O.mult)
+    vts(R("s0", 0, 16), R("reset", 0, 16), -1.0, 1.0, O.mult, O.add)
+    vts(a64("mm1"), a64("mask"), -1.0, None, O.add)
+    vscan(R("pwr", 0, 16), R("q25", 0, 16), R("s0", 0, 16), 0.0, O.mult, O.add)
+    vtt(a64("t1"), a64("thr"), a64("mask"), O.mult)
+    vtt(R("pm", 0, 16), R("pwr", 0, 16), R("mask", 0, 16), O.mult)
+    vts(a64("nmB"), a64("mask"), -float(2 ** 24), float(2 ** 24), O.mult, O.add)
+    vsum(C("pwc"), R("pm", 0, 16))
+    vtt(a64("thrM"), a64("t1"), a64("mm1"), O.add)
+    vcopy(R("c16f", 0, 4), R("c_c16", 0, 4))
+    vts(R("lane4", 0, 4), R("c16f", 0, 4), C("ff"), None, O.add)
+    for c in range(4):
+        vts(R("W4", 128 * c, 128 * c + 128), a128("blkf"), C("pwc"), 4.0 ** (32 - 16 * c), O.mult, O.mult)
+    vts(R("VL", 0, 4), R("lane4", 0, 4), 16.0, None, O.mult)
+    sact(a128("blkp"), a128("blkf"), AF.Copy, 2.0)
+    sact(a128("blkm"), a128("blkf"), AF.Copy, -2.0)
+    sact(a128("blkV"), a128("blkf"), AF.Copy, -float(2 ** 20))
+    sact(a128("idV"), a128("identf"), AF.Copy, -float(2 ** 20))
+    sact(a128("idN"), a128("identf"), AF.Copy, float(2 ** 70))
+    sact(a128("onesb"), a128("onesf"))
+
+    def near(c):
+        return topo.cores_of(c)
+
+    def wmask(c, d):
+        m = topo.mask(c, d)
+        if d in near(c):
+            for o in T.cores:
+                if o not in near(c):
+                    m &= ~topo.mask(c, o)
+        return m
+
+    def ones(m):
+        return bin(m).count("1")
+
+    def plan(s):
+        ds = [(d, T.cores[(T.rank_of(s) - d) % N]) for d in (1, 2, 3)]
+        rel = []
+        for (d, t) in ds:
+            twin = [(e, u) for (e, u) in ds if u != t and u in near(t)]
+            if t not in near(s) and twin and topo.die(t) != topo.die(s):
+                rel.append((twin[0][1], twin[0][0], t, d))
+        far = [x[2] for x in rel]
+        lead = [x[0] for x in rel]
+        direct = [(d, t, t in lead) for (d, t) in ds if t not in far]
+        return sorted(direct, key=lambda x: not x[2]), rel
+    plans = {s: plan(s) for s in T.cores}
+    duty = [(e, t, d) for s in T.cores for (u, e, t, d) in plans[s][1] if u == core]
+
+    def targets(s):
+        return [t for (d, t, l) in plans[s][0]] + [t for p in plans.values() for (u, e, t, d) in p[1] if u == s]
+    writers = [s for s in T.cores if core in targets(s)]
+    tell = len(set(targets(core)))
+    come = []
+    for s in T.cores:
+        for (d, t, l) in plans[s][0]:
+            if t == core:
+                come.append(("b" if l else "a", d, ones(wmask(s, core))))
+        for (u, e, t, d) in plans[s][1]:
+            if t == core:
+                come.append(("a", d, ones(wmask(u, core))))
+    nsl = [0]
+    block = lambda d: (OWN + 1024 + 256 * (d - 1), OWN + 1280 + 256 * (d - 1))
+
+    def put(dst, win, d, src, sem):
+        order("G", src[1], [])
+        rid, pid = topo.addr(dst, core)
+        a, b = block(d)
+        m = wmask(core, dst)
+        g.remote_dma(out_ap=T[win][:, a:b], in_ap=src[0], remote_sem=T.sem[sem], local_sem=T.sem.sl, pid=pid, routing_id=rid,
+                     dma_engine_mask=m)
+        nsl[0] += ones(m)
+
+    Zown, Zall = ("ZW", OWN, OWN + 1024), ("ZW", OWN, OWN + 1792)
+    Yown, Yall = ("YW", OWN, OWN + 1024), ("YW", OWN, OWN + 1792)
+
+    def borders(e):
+        vcopy(R("SY", 256 * e, 256 * e + 128), IND(*Yown, R("BL", 0, 8)))
+        sact(R("SY", 256 * e + 128, 256 * e + 256), IND(*Yown, R("BL", 8, 16)))
+        two = (("SZ", "ZW", "Z%d" % e), ("SY", "YW", "Y%d" % e))
+        todo = [(w, x) for x in plans[core][0] for w in two]
+        if e == 0:
+            todo = [(w, x) for w in two for x in plans[core][0]]
+        for (n, win, s), (d, t, l) in todo:
+            put(t, win, d, R(n, 256 * e, 256 * e + 256), ("b" if l else "a") + s)
+        for (n, win, s) in two:
+            for k in "ab":
+                v = sum(x[2] for x in come if x[0] == k)
+                total[k + s] = v
+                for x in come:
+                    if x[0] == k:
+                        record("A", [], [(win,) + block(x[1])], k + s, v)
+            for (b, t, d) in duty:
+                put(t, win, d, R(win, *block(b)), "a" + s)
+
+    sact(R("SZ", 0, 256), IND(*Zown, R("BL", 16, 32)))
+    mlp = lambda n, a: (T[n][0:64, a:a + 128], [(n, a, a + 128)], [])
+    id64 = (T.identf[0:64, 0:64], [("identf", 0, 128)], [])
+
+    def mlist(a, bank):
+        vcopy(mlp("mlf", a), mlp("ml", a))
+        o, i = R(bank, 0, 64), mlp("mlf", a)
+        emit("P", [lambda: g.tensor.transpose(o[0], i[0], id64[0])], [o], [i, id64])
+        vcopy(R("ML", a // 2, a // 2 + 64), o)
+    mlist(0, "pb0")
+    vcopy(R("YW", OWN, OWN + 512), IND(*Zown, R("ML", 0, 32)))
+    sact(R("YW", OWN + 512, OWN + 1024), IND(*Zown, R("ML", 32, 64)))
+    borders(0)
+    need("Y", "aZ0", total["aZ0"])
+    spread("ld_IM", "tIM", T.im)
+    spread("ld_M", "tM", T.m)
+    load("Y", "ld_x", R("tX", 0, 1024), T.x[:], 1)
+    vcopy(R("tNZM", OWN, OWN + 1024), IND("tNZ", 0, 1024, R("ML", 0, 64)))
+    mlist(128, "pb1")
+    vcopy(R("L1", 64, 128), R("tNZM", OWN, OWN + 1024, 16))
+    vcopy(R("L1", 0, 64), R("tNB", 0, 1024, 16))
+    vcopy(R("tNBI", OWN, OWN + 1024), IND("tNB", 0, 1024, R("ML", 64, 128)))
+
+    def step_lists():
+        vcopy(a128("nf"), a128("L1"))
+        vts(R("v5a", 0, 4), R("VL", 0, 4), 5.0, 1.0, O.mult, O.add)
+        vts(R("v5b", 0, 4), R("v5a", 0, 4), 1023, None, O.bitwise_and)
+        vcopy(R("V5", 0, 4), R("v5b", 0, 4))
+    step_lists()
+
+    for r in range(3):
+        mt = "tM" if r == 0 else "MF"
+        more = r < 2
+        for (a, b) in CH:
+            sact(R("Zt", 16 * a, 16 * b), IND(*Zall, R("L1", 64 + a, 64 + b)))
+            b = min(b, 64 - YS)
+            if a < b:
+                vcopy(R("Yt", 16 * a, 16 * b), IND(*Yall, R("L1", a, b)))
+        sact(R("Yt", 1024 - 16 * YS, 1024), IND(*Yall, R("L1", 64 - YS, 64)))
+        for j, (a, b) in enumerate(CH):
+            o = R("pb%d" % j, 0, 16 * (b - a))
+            pe([mm(o, a128("identb"), R("Yt", 16 * a, 16 * b), True, False),
+                mm(o, a128("identn"), R("Zt", 16 * a, 16 * b), False, True)])
+        c0 = 16 * CH[0][1]
+        vts(R("ng", 0, c0), R("pb0", 0, c0), -1.0, None, O.mult)
+        vtt(R("AD", 0, c0), R("pb0", 0, c0), R("ng", 0, c0), O.max)
+        for j in (1, 2):
+            a, b = CH[j]
+            sact(R("AD", 16 * a, 16 * b), R("pb%d" % j, 0, 16 * (b - a)), AF.Abs)
+        K = R("pb3", 0, 64)
+        pe([mm(K, a128("biasd"), a64("ones64"), True, False)] +
+           [mm(K, R("Es", 15 - k, 143 - k), R("AD", k, 1024, 16), False, k == 15) for k in range(16)])
+        OH = R("pb5", 0, 64)
+        vtr(a64("KT"), K)
+        vscan(a64("Fs"), a64("reset"), a64("KT"), 0.0, O.mult, O.max)
+        for s in range(4):
+            vts(R("OHt", 16 * s, 16 * s + 16), R("KT", 16 * s, 16 * s + 16), C("Fs", 16 * s + 15), None, O.is_equal)
+        vtr(OH, a64("OHt"))
+        vtt(R("pr", 0, 64), OH, R("nf", 0, 64), O.mult)
+        vtt(R("pr", 64, 128), OH, R("nf", 64, 128), O.mult)
+        ROW = R("pb4", 0, 128)
+        pe([mm(ROW, a128("blkf"), a128("pr"), True, True)])
+        vts(a64("kz"), K, 16.0, None, O.is_lt)
+        vtt(a64("kz2"), a64("kz"), OH, O.mult)
+        vtt(a128("mk"), ROW, a128("mask"), O.mult)
+        vscan(a128("sc"), a128("reset"), a128("mk"), 0.0, O.mult, O.add)
+        vts(R("LAQ", 0, 8), R("sc", 15, 128, 16), 1023.0, None, O.min)
+        la, lq = R("LAQ", 0, 4), R("LAQ", 4, 8)
+        vcopy(R("L2", 0, 64), IND("tNZM", OWN, OWN + 1024, la))
+        vcopy(R("L2", 64, 128), IND("tNBI", OWN, OWN + 1024, lq))
+        vcopy(R("L2", 128, 192), IND("tNZ", 0, 1024, lq))
+        for n, c in (("Bt", 0), ("Bp", 128)):
+            for h in (0, 1):
+                sact(R(n, 512 * h, 512 * h + 512), IND(*Zall, R("L2", c + 32 * h, c + 32 * h + 32)))
+        sact(R("At", 1024 - 16 * AS, 1024), IND(*Yall, R("L2", 128 - AS, 128)))
+        vcopy(R("At", 0, 1024 - 16 * AS), IND(*Yall, R("L2", 64, 128 - AS)))
+        vcopy(R("L2", 192, 256), IND("tNB", 0, 1024, la))
+        vcopy(R("WP", 0, 64), IND("tIM", OWN, OWN + 1024, lq))
+        vcopy(R("WP", 64, 128), IND(mt, OWN, OWN + 1024, la))
+        vts(a128("gh"), ROW, 1024.0, None, O.is_ge)
+        vtt(a128("mk2"), a128("WP"), MP, O.mult)
+        sact(a128("AQ"), ROW)
+        sact(R("NR", 0, 128, 2), R("AQ", 0, 64))
+        sact(R("NR", 1, 128, 2), R("WP", 0, 64))
+        vtt(R("T1", 0, 1024), IND(*Yall, R("L2", 192, 256)), R("Bt", 0, 1024), O.max)
+        vscan(a128("sc2"), a128("reset"), a128("mk2"), 0.0, O.mult, O.add)
+        vts(R("NLc", 0, 8), R("sc", 15, 128, 16), 1023.0, float(OWN), O.min, O.add)
+        vts(R("NLc", 8, 16), R("sc2", 15, 128, 16), float(OWN), None, O.add)
+        vcopy(R("LWP", 0, 8), R("sc2", 15, 128, 16))
+        vtt(R("T2", 0, 1024), IND(*Yall, R("L2", 192, 256)), R("Bp", 0, 1024), O.max)
+        if more:
+            need("G", "cv", cnt["cv"])
+            need("G", "cs", max(e[5] for w in ("ZW", "YW") for e in acc[w] if e[3] == "S"))
+            need("G", "sl", nsl[0])
+            for d in writers:
+                rid, pid = topo.addr(d, core)
+                g.remote_sem_update(T.sem["rdy%d" % (r + 1)], T.sem.sl, pid, rid, 1 << topo.engines(core, d)[0])
+                nsl[0] += 1
+            total["rdy%d" % (r + 1)] = tell
+        Gn = R("pb6", 0, 64)
+        dif = {}
+
+        def diff(bk, src, h):
+            a, b = 512 * h, 512 * h + 512
+            o = R(bk, 0, 512)
+            pe([mm(o, a128("identb"), R(src, a, b), True, False), mm(o, a128("identn"), R("At", a, b), False, True)])
+            dif[src, h] = o
+
+        def term(n, l):
+            pe([mm(Gn, a128(l), R(n, k, 1024, 16), False, n == "R2" and k == 15) for k in range(16)])
+        diff("pb0", "Bt", 0)
+        diff("pb2", "Bp", 0)
+        pe([mm(Gn, a128("idV"), R("gh", 0, 64), True, False), mm(Gn, a128("idV"), R("gh", 64, 128), False, False),
+            mm(Gn, a128("blkV"), a64("kz2"), False, False)])
+        term("T1", "blkp")
+        diff("pb1", "Bt", 1)
+        diff("pb5", "Bp", 1)
+        for (n, src, h) in (("R1", "Bt", 0), ("R2", "Bp", 0), ("R1", "Bt", 1), ("R2", "Bp", 1)):
+            o = R(n, 512 * h, 512 * h + 512)
+            if n == "R1" and h == 0:
+                vts(o, dif[src, h], 0.0, None, O.max)
+            else:
+                sact(o, dif[src, h], AF.Relu)
+        term("T2", "blkm")
+        term("R1", "blkm")
+        term("R2", "blkp")
+        sact(R("zz", 0, 64), IND(*Zown, lq))
+        sact(R("xx", 0, 64), IND("tX", 0, 1024, la))
+        sact(R("zz", 64, 128), IND(*Zown, R("LWP", 4, 8)))
+        sact(R("xx", 64, 128), IND("tX", 0, 1024, R("LWP", 0, 4)))
+        eqs, at = [], 0
+        for c in range(4):
+            for col in (C("sc", 16 * c + 15), C("sc2", 16 * c + 15)):
+                w = 128 - 32 * c
+                vts(R("EQ", at, at + w), R("NR", 32 * c, 128), col, None, O.is_equal)
+                eqs.append((c, at, w))
+                at += w
+        vtt(a64("x1"), Gn, a64("TH") if r else a64("nmB"), O.is_gt)
+        vscan(a64("sp"), a64("reset"), a64("x1"), 0.0, O.mult, O.add)
+        for c in range(4):
+            vts(R("WT", 128 * c, 128 * c + 128), R("W4", 128 * c, 128 * c + 128), C("sp", 16 * c + 15), None, O.mult)
+        vts(a64("npr"), Gn, C("thc") if r else 0.0, None, O.is_le)
+        xz = R("pb4", 128, 256)
+        pe([mm(xz, a128("identb"), a128("xx"), True, False), mm(xz, a128("identn"), a128("zz"), False, True)])
+        vts(a128("cl"), xz, -1.0, 1.0, O.max, O.min)
+        CS = R("pb7", 0, 64)
+        for c in range(4):
+            pe([mm(R("pb7", 16 * c, 64), R("WT", 128 * c, 128 * c + 128), R("EQ", at + nm, at + w, 2),
+                   c == 0 and (at, nm) == (0, 0), False) for (c2, at, w) in eqs if c2 == c for nm in (0, 1)])
+        pe([mm(CS, a128("idN"), a64("npr"), False, True)])
+        nzp = R("pb3", 128, 256)
+        pe([mm(nzp, a128("identb"), a128("zz"), True, False), mm(nzp, a128("identb"), a128("cl"), False, True)])
+        sact(a128("nzv"), nzp)
+        if more:
+            vts(R("oq", 0, 4), R("sc", 79, 128, 16), 1024.0, None, O.is_lt)
+            vtt(R("d1", 0, 4), R("sc2", 15, 64, 16), R("V5", 0, 4), O.subtract)
+            vtt(R("d2", 0, 4), R("d1", 0, 4), R("oq", 0, 4), O.mult)
+            vtt(R("alt", 0, 4), R("d2", 0, 4), R("V5", 0, 4), O.add)
+            vtt(R("da", 0, 4), R("sc", 15, 64, 16), R("alt", 0, 4), O.subtract)
+        vtt(a64("cm"), CS, a64("thrM"), O.is_le)
+        vscan(a64("cl2"), a64("reset"), a64("cm"), 0.0, O.mult, O.add)
+        for c in range(4):
+            vts(R("OFF", c, 16, 4), R("NLc", c, 16, 4), C("cl2", 16 * c + 15), C("lane4", c), O.mult, O.max)
+        oa, oqq, ow, op = [R("OFF", 4 * n, 4 * n + 4) for n in range(4)]
+        sca = lambda n, off, d: vcopy(IND(n, 0, OWN + 1024, off), d)
+        sca("ZW", oqq, R("nzv", 0, 64))
+        sca("ZW", op, R("nzv", 64, 128))
+        if not more:
+            store("Y", "st_z", T.zo[:], R("ZW", OWN, OWN + 1024))
+            sca("MF", oa, R("AQ", 64, 128))
+            sca("MF", ow, R("WP", 64, 128))
+            store("Y", "st_m", T.mo[:], (T.MF[0:128:16, OWN:OWN + 1024], [("MF", OWN, OWN + 1024)], []))
+            break
+        e = r + 1
+        sact(R("SZ", 256 * e, 256 * e + 256), IND(*Zown, R("BL", 16, 32)))
+        sca("YW", oa, R("nzv", 0, 64))
+        sca("YW", ow, R("nzv", 64, 128))
+        need("G", "rdy%d" % e, tell)
+        borders(e)
+        vtt(R("d3", 0, 4), R("da", 0, 4), R("cl2", 15, 64, 16), O.mult)
+        sca("tNZM", oa, R("L2", 128, 192))
+        sca("tNZM", ow, R("L2", 0, 64))
+        vtt(R("VL", 0, 4), R("d3", 0, 4), R("alt", 0, 4), O.add)
+        vsum(C("cn"), a64("cm"))
+        vcopy(R("vl", 0, 4), R("VL", 0, 4))
+        vcopy(C("cnt"), C("cn"))
+        vcopy(R("L1", 0, 64), IND("tNB", 0, 1024, R("vl", 0, 4)))
+        pe([mm(R("pb7", 256, 257), a128("onesb"), C("cnt"), True, True)])
+        vcopy(R("L1", 64, 128), IND("tNZM", OWN, OWN + 1024, R("vl", 0, 4)))
+        sca("tNBI", oqq, R("L2", 192, 256))
+        sca("tNBI", op, R("L2", 64, 128))
+        vcopy(C("thi"), R("pb7", 256, 257))
+        step_lists()
+        vts(C("thj"), C("thi"), 31, None, O.bitwise_and)
+        sca(mt, oa, R("AQ", 64, 128))
+        vcopy(C("thc"), C("thj"))
+        sca(mt, ow, R("WP", 64, 128))
+        vts(a64("TH"), a64("nmB"), C("thc"), None, O.add)
+        sca("tIM", oqq, R("AQ", 0, 64))
+        sca("tIM", op, R("WP", 0, 64))
+        if r == 0:
+            vcopy(R("MF", OWN, OWN + 1024), R("tM", OWN, OWN + 1024))
+
+    total.update(cnt)
+    total["sl"] = nsl[0]
+    for s, v in total.items():
+        if max(seen[q].get(s, 0) for q in seen) < v:
+            g.wait_ge(T.sem[s], v)

@@ -1,29 +1,31 @@
-from concourse.mybir import AluOpType as O, AxisListType, ActivationFunctionType as AF
+from concourse.bass import DstId, RemoteDMATransfer
+from concourse.mybir import AluOpType as O, ActivationFunctionType as AF
 
 F4, B2, I4, U2 = "float32", "bfloat16", "int32", "uint16"
 _W = {
-    B2: dict(ZW=1920, YW=1920, tX=1024, SY=768, SZ=768, Yt=1024, Zt=1024, ng=512, AD=1024, At=1024, Bt=1024, Bp=1024, T1=1024,
-             T2=1024, R1=1024, R2=1024, zz=128, xx=128, cl=128, nzv=128, EQ=640, gh=128, kz2=64, npr=64, WT=512, cnt=2,
-             identb=128, identn=128, biasd=128, blkp=128, blkm=128, blkV=128, idV=128, idN=128, Es=144, W4=512, ones64=64,
-             onesb=128),
-    F4: dict(MF=1152, mlf=256, nf=128, KT=64, Fs=64, OHt=64, pr=128, mk=128, sc=128, WP=128, AQ=128, NR=128, mk2=128,
-             sc2=128, NLc=16, kz=64, TH=64, x1=64, sp=64, cm=64, cl2=64, VL=4, V5=4, oq=4, d1=4, d2=4, alt=4, da=4,
-             d3=4, cn=2, thc=2, onesf=128, b1=128, blkf=128, ff=2, f15=2, itf=128, mask=128, reset=128, identf=128, q25=16,
-             s0=16, pwr=16, pm=16, pwc=2, c25=64, c00=64, thr=64, t1=64, mm1=64, thrM=64, nmB=64, c16f=4, lane4=4),
-    I4: dict(tNB=1024, tNZ=1024, tNZM=1152, tNBI=1152, tM=1152, tIM=1152, ml=256, bl=32, v5a=4, v5b=4, thi=2, thj=2, c_it=128,
-             c_p=2, c_c16=4, fI=2),
-    U2: dict(ML=128, BL=32, L1=128, LAQ=8, L2=256, LWP=8, OFF=16, vl=4),
+    B2: dict(ZW0=1920, ZW1=1920, ZW2=1920, YW0=1920, YW1=1920, YW2=1920, tX=1024, SY=768, SZ=768, Zt=1024, Dt=1024, AD=1024,
+             At=1024, Bt=1024, Bp=1024, T1=1024, T2=1024, R1=1024, R2=1024, zz=128, xx=128, cl=128, nzv=128, EQ=640, rv=16,
+             WT=512, identb=128, identn=128, blkp=128, blkm=128, blkH=128, Es=432, brow=64, cst4=4, offG=64, stepG=64,
+             offC=128, thrC=128, selfC=32),
+    F4: dict(IOTA=1024, tM=1152, tIM=1152, mlf=128, mlt=128, nf=160, TT=296, Tn=128, DL=128, Fs=64, ns=64, SC=256, mk2=128,
+             E1=64, GS=64, BS=128, NR=128, QP=128, NLc=16, s6a=12, s6b=12, s6o=12, VL=4, mkv=64, scv=64, nth=2, onesf=128,
+             itf=128, gf=128, ff=2, gp=2, mask=128, blkf=128, identf=128, reset=128, reset32=128, half=64, wrow=64, wm=64,
+             WL=64, lane4=4, pbase=8, f2=2, ps=2, fv=8, b16=8, foldf=8, n15=2, n16=2),
+    I4: dict(tNB=1024, tNZ=1024, ml=128, bl=32, v5a=4, v5b=4, thi=2, thj=2, c_p=2, fI=2, gI=2, f3I=2, f2I=2, pa=8, pb=8),
+    U2: dict(ML=128, BL=32, L1=128, LL=16, L2=256, OFF=16, vl=4, mvl=4, PERM=8, FOLD=8, NEXT=8),
 }
 SCRATCH = {n: ("sbuf", [128, w], d) for d in _W for n, w in _W[d].items()}
 for _i in range(8):
-    SCRATCH["pb%d" % _i] = ("psum", [128, 512], F4)
-SEMAPHORES = ["cv", "cs", "cp", "cg", "ld_z", "ld_b", "ld_m", "ld_im", "ld_nz", "ld_nb", "ld_x", "ld_M", "ld_IM", "st_z", "st_m",
-              "rdy1", "rdy2", "sl"] + ["%s%s%d" % (a, w, e) for a in "ab" for w in "YZ" for e in range(3)]
+    SCRATCH["ps%d" % _i] = ("psum", [128, 512], F4)
 N = 8
+SEMAPHORES = ["cv", "cs", "cp", "cg", "ld_z", "ld_b", "ld_m", "ld_im", "ld_nz", "ld_nb", "ld_x", "cp_Z0", "cp_Z1", "cp_Y0", "cp_Y1",
+              "st_z", "st_m", "sl"] + ["%s%d_%d" % (w, e, s) for w in "YZ" for e in range(3) for s in range(N)]
 OWN = 128
-CFG = dict(CH=[(0, 24), (24, 44), (44, 64)],
-           YS=24,
-           AS=32)
+STEP, FAR, VOID = 2.0 ** 19, 2.0 ** 23, 2.0 ** 18
+WTOP, HUGE = 2.0 ** 75, 2.0 ** 80
+CFG = dict(CH=[(0, 2, "S"), (2, 6, "S"), (6, 11, "V"), (11, 16, "V")],
+           AS=16,
+           RV=1)
 
 
 def rank_program(g, core, T, topo):
@@ -36,34 +38,38 @@ def rank_program(g, core, T, topo):
     total = {}
     seen = {q: {} for q in QUEUE}
     acc = {}
-    CH, YS, AS = CFG["CH"], CFG["YS"], CFG["AS"]
+    CH, AS, RV = CFG["CH"], CFG["AS"], CFG["RV"]
 
     def need(q, sem, val):
         if seen[q].get(sem, 0) < val:
             QUEUE[q].wait_ge(T.sem[sem], val)
             seen[q][sem] = val
 
+    def meet(a, b, s, a2, b2, s2):
+        if b2 <= a or b <= a2:
+            return False
+        return s != s2 or (a - a2) % s == 0
+
     def order(q, reads, writes):
         w = {}
         for kind, regs in (("r", reads), ("w", writes)):
-            for (n, a, b) in regs:
-                ps = n[:2] == "pb"
-                for (a2, b2, k2, q2, s2, v2) in acc.get(n, ()):
+            for (n, a, b, s) in regs:
+                ps = n[:2] == "ps" and n != "ps"
+                for (a2, b2, st2, k2, q2, s2, v2) in acc.get(n, ()):
                     if ps:
                         if q2 == q and (q == "P" or (kind == "r" and k2 == "r")):
                             continue
-                    else:
-                        if (kind == "r" and k2 == "r") or b2 <= a or b <= a2:
-                            continue
+                    elif (kind == "r" and k2 == "r") or not meet(a, b, s, a2, b2, st2):
+                        continue
                     w[s2] = max(w.get(s2, 0), v2)
         for s, v in w.items():
             need(q, s, v)
 
     def record(q, reads, writes, sem, val):
         for kind, regs in (("r", reads), ("w", writes)):
-            for (n, a, b) in regs:
-                l = [e for e in acc.get(n, []) if not (e[0] == a and e[1] == b and e[2] == kind and e[3] == q)]
-                l.append((a, b, kind, q, sem, val))
+            for (n, a, b, s) in regs:
+                l = [e for e in acc.get(n, []) if e[:5] != (a, b, s, kind, q)]
+                l.append((a, b, s, kind, q, sem, val))
                 acc[n] = l
 
     def emit(q, calls, outs, ins):
@@ -78,13 +84,13 @@ def rank_program(g, core, T, topo):
         record(q, reads, writes, s, cnt[s])
 
     def R(n, a, b, s=1):
-        return (T[n][:, a:b] if s == 1 else T[n][:, a:b:s], [(n, a, b)], [])
+        return (T[n][:, a:b] if s == 1 else T[n][:, a:b:s], [(n, a, b, s)], [])
 
     def C(n, c=0):
         return R(n, c, c + 1)
 
     def IND(n, a, b, off):
-        return (T[n][:, a:b].indirect(off[0]), [(n, a, b)], off[1])
+        return (T[n][:, a:b].indirect(off[0]), [(n, a, b, 1)], off[1])
 
     def tup(*xs):
         return [x for x in xs if isinstance(x, tuple)]
@@ -115,11 +121,12 @@ def rank_program(g, core, T, topo):
     def vtr(o, i):
         emit("V", [lambda: g.vector.transpose(out=o[0], in_=i[0])], [o], [i])
 
-    def vsum(o, i):
-        emit("V", [lambda: g.vector.tensor_reduce(out=o[0], in_=i[0], axis=AxisListType.X, op=O.add)], [o], [i])
-
-    def sact(o, i, func=AF.Copy, scale=1.0):
-        emit("S", [lambda: g.scalar.activation(out=o[0], in_=i[0], func=func, scale=raw(scale))], [o], [i] + tup(scale))
+    def sact(o, i, func=AF.Copy, scale=1.0, bias=None):
+        if bias is None:
+            f = lambda: g.scalar.activation(out=o[0], in_=i[0], func=func, scale=scale)
+        else:
+            f = lambda: g.scalar.activation(out=o[0], in_=i[0], func=func, scale=scale, bias=raw(bias))
+        emit("S", [f], [o], [i] + tup(bias))
 
     def mm(o, l, r, st, sp):
         return (lambda: g.tensor.matmul(o[0], l[0], r[0], st, sp)), o, l, r
@@ -127,86 +134,57 @@ def rank_program(g, core, T, topo):
     def pe(ms):
         emit("P", [m[0] for m in ms], [m[1] for m in ms], [x for m in ms for x in (m[2], m[3])])
 
-    def load(q, sem, o, in_ap, tot):
-        order(q, [], o[1])
-        QUEUE[q].dma_start(out=o[0], in_=in_ap).then_inc(T.sem[sem], 16)
+    def giota(o, pat, base, ch):
+        emit("G", [lambda: g.iota(o[0], pat, base, ch, allow_small_or_imprecise_dtypes=True)], [o], [])
+
+    def dma(q, sem, o, i, tot=1):
+        order(q, i[1] if tup(i) else [], o[1] if tup(o) else [])
+        QUEUE[q].dma_start(out=raw(o), in_=raw(i)).then_inc(T.sem[sem], 16)
         total[sem] = 16 * tot
-        record("D" + sem, [], o[1], sem, 16 * tot)
+        record("D" + sem, i[1] if tup(i) else [], o[1] if tup(o) else [], sem, 16 * tot)
 
-    def store(q, sem, out_ap, i):
-        order(q, i[1], [])
-        QUEUE[q].dma_start(out=out_ap, in_=i[0]).then_inc(T.sem[sem], 16)
-        total[sem] = 16
-
-    def lists(a, sem, src):
-        for k in range(8):
-            c = a + 16 * k
-            load("Y", sem, (T.ml[0:64, c:c + 16], [("ml", c, c + 16)], []), src[k:k + 1, :], 8)
-
-    def spread(sem, n, src):
-        for f in range(16):
-            load("Y", sem, (T[n][f:128:16, OWN:OWN + 1024], [(n + "_" + str(f), 0, 1)], []), src[:], 16)
-        record("D" + sem, [], [(n, OWN, OWN + 1024)], sem, 256)
-    load("S", "ld_b", R("bl", 0, 16), T.bx[:], 2)
-    load("S", "ld_b", R("bl", 16, 32), T.bz[:], 2)
-    lists(0, "ld_m", T.m)
-    load("S", "ld_z", R("ZW", OWN, OWN + 1024), T.z[:], 1)
-    load("Y", "ld_nz", R("tNZ", 0, 1024), T.nz[:], 1)
-    lists(128, "ld_im", T.im)
-    load("Y", "ld_nb", R("tNB", 0, 1024), T.nb[:], 1)
-
-    def giota(o, pat, ch):
-        emit("G", [lambda: g.iota(o[0], pat, 0, ch)], [o], [])
-
-    def gsel(o, i, pat, base, ch):
-        emit("G", [lambda: g.affine_select(o[0], i[0], pat, O.is_ge, 0.0, base, ch)], [o], [i])
     a128 = lambda n: R(n, 0, 128)
     a64 = lambda n: R(n, 0, 64)
-    MP = R("pb6", 256, 384)
-    vset(a128("onesf"), 1.0)
-    giota(R("c_p", 0, 2), [[0, 2]], 1)
-    giota(a128("c_it"), [[0, 8], [1, 16]], 0)
-    gsel(a128("b1"), a128("onesf"), [[-16, 8], [0, 16]], 0, 1)
-    gsel(a128("blkf"), a128("b1"), [[16, 8], [0, 16]], 15, -1)
-    giota(R("c_c16", 0, 4), [[16, 4]], 0)
-    vset(a64("ones64"), 1.0)
-    vset(R("Es", 0, 144), 0.0)
-    vset(a64("c25"), 0.25)
-    vset(a64("c00"), 0.0)
+    ends = lambda n, a, k, s=16: R(n, a + s - 1, a + s * k, s)
+
+    def lists(a, sem, src):
+        for h in (0, 1):
+            for b in (0, 1):
+                c = a + 32 * b + 16 * h
+                dma("Y", sem, R("ml", c, c + 16), src[h:8:2, 512 * b:512 * b + 512], 4)
+    dma("S", "ld_b", R("bl", 0, 16), T.bx[:], 2)
+    dma("S", "ld_b", R("bl", 16, 32), T.bz[:], 2)
+    lists(0, "ld_m", T.m)
+    dma("S", "ld_z", R("ZW0", OWN, OWN + 1024), T.z[:])
+    dma("Y", "ld_nz", R("tNZ", 0, 1024), T.nz[:])
+    dma("Y", "ld_nb", R("tNB", 0, 1024), T.nb[:])
+    lists(64, "ld_im", T.im)
+
+    emit("G", [lambda: g.iota(T.c_p[:, 0:2], [[0, 2]], 0, 1)], [R("c_p", 0, 2)], [])
+    giota(a128("itf"), [[0, 8], [1, 16]], 0, 0)
+    giota(a128("gf"), [[1, 8], [0, 16]], 0, 0)
+    giota(R("pbase", 0, 8), [[64, 2], [4, 4]], 0, 0)
+    giota(a64("brow"), [[0, 4], [-1, 16]], 15, 0)
+    giota(R("IOTA", 0, 512), [[1, 512]], 0, 0)
+    vset(a64("E1"), 0.0)
+    vset(a64("half"), 0.5)
     vts(R("fI", 0, 2), R("c_p", 0, 2), 15, None, O.bitwise_and)
-    vcopy(a128("itf"), a128("c_it"))
+    vts(R("gI", 0, 2), R("c_p", 0, 2), 4, None, O.arith_shift_right)
+    vset(R("Es", 0, 432), 0.0)
     vcopy(R("ff", 0, 2), R("fI", 0, 2))
-    vts(a128("reset"), a128("itf"), 0.0, None, O.is_gt)
+    vcopy(R("gp", 0, 2), R("gI", 0, 2))
+    vts(R("f3I", 0, 2), R("fI", 0, 2), 3, None, O.bitwise_and)
+    vts(R("f2I", 0, 2), R("fI", 0, 2), 2, None, O.arith_shift_right)
     vts(a128("mask"), a128("itf"), C("ff"), None, O.is_equal)
-    vts(C("f15"), C("ff"), -1.0, 15.0, O.mult, O.add)
-    vscan(a64("thr"), a64("c25"), a64("c00"), 3.0 * 4.0 ** 33, O.mult, O.add)
-    vtt(a128("identf"), a128("blkf"), a128("mask"), O.mult)
-    vcopy(MP, a128("mask"))
-    vts(R("Es", 15, 143, 16), R("blkf", 0, 128, 16), 16.0, None, O.mult)
-    vts(a128("identn"), a128("identf"), -1.0, None, O.mult)
-    vcopy(a128("identb"), a128("identf"))
+    vts(a128("reset"), a128("itf"), 0.0, None, O.is_gt)
+    vcopy(R("f2", 0, 2), R("f2I", 0, 2))
+    vts(a128("blkf"), a128("gf"), C("gp"), None, O.is_equal)
+    vscan(a64("wrow"), a64("half"), a64("E1"), 2.0 * WTOP, O.mult, O.add)
+    vts(R("ps", 0, 2), R("f3I", 0, 2), 16.0, C("f2"), O.mult, O.add)
+    vset(R("nf", 0, 160), 0.0)
+    vts(R("pa", 0, 8), R("gf", 0, 128, 16), C("gp"), None, O.add)
+    vts(R("PERM", 0, 8), R("pbase", 0, 8), C("ps"), None, O.add)
     vcopy(R("BL", 0, 32), R("bl", 0, 32))
-    vts(a128("biasd"), a128("identf"), C("f15"), None, O.mult)
-    vts(R("q25", 0, 16), R("reset", 0, 16), 0.25, None, O.mult)
-    vts(R("s0", 0, 16), R("reset", 0, 16), -1.0, 1.0, O.mult, O.add)
-    vts(a64("mm1"), a64("mask"), -1.0, None, O.add)
-    vscan(R("pwr", 0, 16), R("q25", 0, 16), R("s0", 0, 16), 0.0, O.mult, O.add)
-    vtt(a64("t1"), a64("thr"), a64("mask"), O.mult)
-    vtt(R("pm", 0, 16), R("pwr", 0, 16), R("mask", 0, 16), O.mult)
-    vts(a64("nmB"), a64("mask"), -float(2 ** 24), float(2 ** 24), O.mult, O.add)
-    vsum(C("pwc"), R("pm", 0, 16))
-    vtt(a64("thrM"), a64("t1"), a64("mm1"), O.add)
-    vcopy(R("c16f", 0, 4), R("c_c16", 0, 4))
-    vts(R("lane4", 0, 4), R("c16f", 0, 4), C("ff"), None, O.add)
-    for c in range(4):
-        vts(R("W4", 128 * c, 128 * c + 128), a128("blkf"), C("pwc"), 4.0 ** (32 - 16 * c), O.mult, O.mult)
-    vts(R("VL", 0, 4), R("lane4", 0, 4), 16.0, None, O.mult)
-    sact(a128("blkp"), a128("blkf"), AF.Copy, 2.0)
-    sact(a128("blkm"), a128("blkf"), AF.Copy, -2.0)
-    sact(a128("blkV"), a128("blkf"), AF.Copy, -float(2 ** 20))
-    sact(a128("idV"), a128("identf"), AF.Copy, -float(2 ** 20))
-    sact(a128("idN"), a128("identf"), AF.Copy, float(2 ** 70))
-    sact(a128("onesb"), a128("onesf"))
 
     def near(c):
         return topo.cores_of(c)
@@ -222,166 +200,192 @@ def rank_program(g, core, T, topo):
     def ones(m):
         return bin(m).count("1")
 
+    def halves(m):
+        es = [e for e in range(m.bit_length()) if m >> e & 1]
+        lo = sum(1 << e for e in es[:len(es) // 2])
+        return lo, m & ~lo
+
     def plan(s):
-        ds = [(d, T.cores[(T.rank_of(s) - d) % N]) for d in (1, 2, 3)]
+        ds = [T.cores[(T.rank_of(s) - d) % N] for d in (1, 2, 3)]
         rel = []
-        for (d, t) in ds:
-            twin = [(e, u) for (e, u) in ds if u != t and u in near(t)]
+        for t in ds:
+            twin = [u for u in ds if u != t and u in near(t)]
             if t not in near(s) and twin and topo.die(t) != topo.die(s):
-                rel.append((twin[0][1], twin[0][0], t, d))
-        far = [x[2] for x in rel]
-        lead = [x[0] for x in rel]
-        direct = [(d, t, t in lead) for (d, t) in ds if t not in far]
-        return sorted(direct, key=lambda x: not x[2]), rel
+                rel.append((twin[0], t))
+        direct = [t for t in ds if t not in [x[1] for x in rel]]
+        return sorted(direct, key=lambda t: t not in [x[0] for x in rel]), rel
     plans = {s: plan(s) for s in T.cores}
-    duty = [(e, t, d) for s in T.cores for (u, e, t, d) in plans[s][1] if u == core]
-
-    def targets(s):
-        return [t for (d, t, l) in plans[s][0]] + [t for p in plans.values() for (u, e, t, d) in p[1] if u == s]
-    writers = [s for s in T.cores if core in targets(s)]
-    tell = len(set(targets(core)))
-    come = []
-    for s in T.cores:
-        for (d, t, l) in plans[s][0]:
-            if t == core:
-                come.append(("b" if l else "a", d, ones(wmask(s, core))))
-        for (u, e, t, d) in plans[s][1]:
-            if t == core:
-                come.append(("a", d, ones(wmask(u, core))))
+    duty = [(s, t) for s in T.cores for (u, t) in plans[s][1] if u == core]
     nsl = [0]
-    block = lambda d: (OWN + 1024 + 256 * (d - 1), OWN + 1280 + 256 * (d - 1))
 
-    def put(dst, win, d, src, sem):
-        order("G", src[1], [])
-        rid, pid = topo.addr(dst, core)
-        a, b = block(d)
-        m = wmask(core, dst)
-        g.remote_dma(out_ap=T[win][:, a:b], in_ap=src[0], remote_sem=T.sem[sem], local_sem=T.sem.sl, pid=pid, routing_id=rid,
-                     dma_engine_mask=m)
-        nsl[0] += ones(m)
+    def block(s, t):
+        d = (T.rank_of(s) - T.rank_of(t)) % N
+        return OWN + 1024 + 256 * (d - 1), OWN + 1280 + 256 * (d - 1)
 
-    Zown, Zall = ("ZW", OWN, OWN + 1024), ("ZW", OWN, OWN + 1792)
-    Yown, Yall = ("YW", OWN, OWN + 1024), ("YW", OWN, OWN + 1792)
+    def calls(s, e):
+        lead, other = plans[s][0]
+        ml_, mo_ = wmask(s, lead), wmask(s, other)
+        if ml_ & mo_ == 0:
+            return [[(w, lead, ml_), (w, other, mo_)] for w in "ZY"]
+        if e == 0:
+            return [[(w, t, wmask(s, t))] for w in "ZY" for t in (lead, other)]
+        return [[(w, lead, ml_)] for w in "ZY"] + [[(w, other, m) for w, m in zip("ZY", halves(mo_))]]
+
+    def put(items):
+        ts = []
+        for (s, w, e, src, dst, m) in items:
+            order("G", src[1], [])
+            rid, pid = topo.addr(dst, core)
+            a, b = block(s, dst)
+            ts.append(RemoteDMATransfer(dst_ids=[DstId(rid=rid, pnc=pid)], dma_engine_mask=m, src=src[0],
+                                        remote_sem=T.sem["%s%d_%d" % (w, e, T.rank_of(s))], dst=T["%sW%d" % (w, e)][:, a:b]))
+            nsl[0] += ones(m)
+        g.remote_dma_fused(ts, local_sem=T.sem.sl)
 
     def borders(e):
-        vcopy(R("SY", 256 * e, 256 * e + 128), IND(*Yown, R("BL", 0, 8)))
-        sact(R("SY", 256 * e + 128, 256 * e + 256), IND(*Yown, R("BL", 8, 16)))
-        two = (("SZ", "ZW", "Z%d" % e), ("SY", "YW", "Y%d" % e))
-        todo = [(w, x) for x in plans[core][0] for w in two]
-        if e == 0:
-            todo = [(w, x) for w in two for x in plans[core][0]]
-        for (n, win, s), (d, t, l) in todo:
-            put(t, win, d, R(n, 256 * e, 256 * e + 256), ("b" if l else "a") + s)
-        for (n, win, s) in two:
-            for k in "ab":
-                v = sum(x[2] for x in come if x[0] == k)
-                total[k + s] = v
-                for x in come:
-                    if x[0] == k:
-                        record("A", [], [(win,) + block(x[1])], k + s, v)
-            for (b, t, d) in duty:
-                put(t, win, d, R(win, *block(b)), "a" + s)
+        vcopy(R("SY", 256 * e, 256 * e + 128), IND("YW%d" % e, OWN, OWN + 1024, R("BL", 0, 8)))
+        sact(R("SY", 256 * e + 128, 256 * e + 256), IND("YW%d" % e, OWN, OWN + 1024, R("BL", 8, 16)))
+        for c in calls(core, e):
+            put([(core, w, e, R("S" + w, 256 * e, 256 * e + 256), t, m) for (w, t, m) in c])
+        for w in "ZY":
+            win = "%sW%d" % (w, e)
+            for s in T.cores:
+                come = [m for c in calls(s, e) for (w2, t, m) in c if (w2, t) == (w, core)]
+                come += [wmask(u, t) for (u, t) in plans[s][1] if t == core]
+                for m in come:
+                    sem = "%s%d_%d" % (w, e, T.rank_of(s))
+                    total[sem] = ones(m)
+                    record("A" + sem, [], [(win,) + block(s, core) + (1,)], sem, ones(m))
+            for (s, t) in duty:
+                put([(s, w, e, R(win, *block(s, core)), t, wmask(core, t))])
 
-    sact(R("SZ", 0, 256), IND(*Zown, R("BL", 16, 32)))
-    mlp = lambda n, a: (T[n][0:64, a:a + 128], [(n, a, a + 128)], [])
-    id64 = (T.identf[0:64, 0:64], [("identf", 0, 128)], [])
+    def arrived(q, e):
+        for s, v in list(total.items()):
+            if s[:3] in ("Y%d_" % e, "Z%d_" % e):
+                need(q, s, v)
 
-    def mlist(a, bank):
-        vcopy(mlp("mlf", a), mlp("ml", a))
-        o, i = R(bank, 0, 64), mlp("mlf", a)
-        emit("P", [lambda: g.tensor.transpose(o[0], i[0], id64[0])], [o], [i, id64])
-        vcopy(R("ML", a // 2, a // 2 + 64), o)
-    mlist(0, "pb0")
-    vcopy(R("YW", OWN, OWN + 512), IND(*Zown, R("ML", 0, 32)))
-    sact(R("YW", OWN + 512, OWN + 1024), IND(*Zown, R("ML", 32, 64)))
+    sact(R("SZ", 0, 256), IND("ZW0", OWN, OWN + 1024, R("BL", 16, 32)))
+
+    def mlist(a):
+        vcopy(R("mlf", a, a + 64), R("ml", a, a + 64))
+        vtr(R("mlt", a, a + 64), R("mlf", a, a + 64))
+        vcopy(R("ML", a, a + 64), R("mlt", a, a + 64))
+    mlist(0)
+    vcopy(R("YW0", OWN, OWN + 512), IND("ZW0", OWN, OWN + 1024, R("ML", 0, 32)))
+    sact(R("YW0", OWN + 512, OWN + 1024), IND("ZW0", OWN, OWN + 1024, R("ML", 32, 64)))
     borders(0)
-    need("Y", "aZ0", total["aZ0"])
-    spread("ld_IM", "tIM", T.im)
-    spread("ld_M", "tM", T.m)
-    load("Y", "ld_x", R("tX", 0, 1024), T.x[:], 1)
-    vcopy(R("tNZM", OWN, OWN + 1024), IND("tNZ", 0, 1024, R("ML", 0, 64)))
-    mlist(128, "pb1")
-    vcopy(R("L1", 64, 128), R("tNZM", OWN, OWN + 1024, 16))
-    vcopy(R("L1", 0, 64), R("tNB", 0, 1024, 16))
-    vcopy(R("tNBI", OWN, OWN + 1024), IND("tNB", 0, 1024, R("ML", 64, 128)))
 
-    def step_lists():
-        vcopy(a128("nf"), a128("L1"))
-        vts(R("v5a", 0, 4), R("VL", 0, 4), 5.0, 1.0, O.mult, O.add)
-        vts(R("v5b", 0, 4), R("v5a", 0, 4), 1023, None, O.bitwise_and)
-        vcopy(R("V5", 0, 4), R("v5b", 0, 4))
-    step_lists()
+    sact(R("IOTA", 512, 1024), R("IOTA", 0, 512), AF.Identity, 1.0, 512.0)
+    sact(R("tM", OWN, OWN + 1024), IND("IOTA", 0, 1024, R("ML", 0, 64)))
+    vts(R("pb", 0, 8), R("pa", 0, 8), 1, None, O.bitwise_and)
+    vts(R("b16", 0, 8), R("gf", 0, 128, 16), 16.0, None, O.mult)
+    vtt(a128("identf"), a128("blkf"), a128("mask"), O.mult)
+    vts(R("fv", 0, 8), R("pb", 0, 8), 144.0, C("ff"), O.mult, O.add)
+    vts(C("n15"), C("ff"), 15.0, 999.0, O.is_equal, O.mult)
+    vtt(a64("wm"), a64("wrow"), a64("mask"), O.mult)
+    vtt(R("foldf", 0, 8), R("fv", 0, 8), R("b16", 0, 8), O.add)
+    vts(C("n16"), C("n15"), 1.0, None, O.add)
+    vset(R("TT", 288, 296), 0.0)
+    vcopy(R("FOLD", 0, 8), R("foldf", 0, 8))
+    vts(R("NEXT", 0, 8), R("foldf", 0, 8), C("n16"), 288.0, O.add, O.min)
+    vts(R("lane4", 0, 4), R("gf", 0, 64, 16), 16.0, C("ff"), O.mult, O.add)
+    vscan(a64("WL"), a64("reset"), a64("wm"), 0.0, O.mult, O.add)
+    vset(a128("reset32"), 1.0)
+    vset(a128("onesf"), 1.0)
+    vset(R("selfC", 0, 32), 0.0)
+    vset(R("s6a", 0, 12), 0.0)
+    vset(R("reset32", 0, 128, 32), 0.0)
+    vts(R("VL", 0, 4), R("lane4", 0, 4), 16.0, None, O.mult)
+    mlist(64)
 
+    def lane_lists(mrow):
+        vscan(a64("scv"), a64("reset"), a64("mkv"), 0.0, O.mult, O.add)
+        vcopy(R("mvl", 0, 4), ends("scv", 0, 4))
+        vcopy(R("nf", 80, 144), IND("tNZ", 0, 1024, R("mvl", 0, 4)))
+        vcopy(a128("L1"), IND("nf", 16, 144, R("PERM", 0, 8)))
+        vtr(R("TT", 0, 128), R("nf", 16, 144))
+        vtr(R("TT", 128, 288), R("nf", 0, 160))
+        sact(a128("Tn"), IND("TT", 0, 296, R("NEXT", 0, 8)))
+        vtt(a128("DL"), IND("TT", 0, 296, R("FOLD", 0, 8)), a128("Tn"), O.subtract)
+    vcopy(R("nf", 16, 80), R("tNB", 0, 1024, 16))
+    vtt(a64("mkv"), R("tM", OWN, OWN + 1024, 16), a64("mask"), O.mult)
+    sact(a128("identb"), a128("identf"))
+    for j, k in enumerate((16.0, 32.0, -16.0)):
+        sact(R("Es", 144 * j + 15, 144 * j + 143, 16), R("blkf", 0, 128, 16), AF.Copy, k)
+    lane_lists(None)
+    sact(R("tIM", OWN, OWN + 1024), IND("IOTA", 0, 1024, R("ML", 64, 128)))
+    sact(a128("identn"), a128("identf"), AF.Copy, -1.0)
+    sact(a128("blkp"), a128("blkf"), AF.Copy, 2.0)
+    sact(a128("blkm"), a128("blkf"), AF.Copy, -2.0)
+    sact(a128("blkH"), a128("blkf"), AF.Identity, -FAR, FAR)
+    sact(R("cst4", 0, 4), R("gf", 0, 64, 16), AF.Copy, -STEP)
+    sact(a64("stepG"), a64("gf"), AF.Copy, STEP)
+    sact(a64("offG"), a64("mask"), AF.Identity, FAR, -FAR)
+    for n, k in enumerate((0.5, -2.5)):
+        sact(R("offC", n, 128, 2), a64("mask"), AF.Identity, HUGE, -HUGE)
+        sact(R("thrC", n, 128, 2), a64("wm"), AF.Copy, k)
+    sact(R("selfC", 0, 32, 2), R("mask", 0, 16), AF.Copy, -3.0)
+
+    la, lq, lp, lw = [R("LL", 4 * n, 4 * n + 4) for n in range(4)]
+    fa, fq, fp, fw = [ends("SC", 64 * n, 4) for n in range(4)]
     for r in range(3):
-        mt = "tM" if r == 0 else "MF"
         more = r < 2
-        for (a, b) in CH:
-            sact(R("Zt", 16 * a, 16 * b), IND(*Zall, R("L1", 64 + a, 64 + b)))
-            b = min(b, 64 - YS)
-            if a < b:
-                vcopy(R("Yt", 16 * a, 16 * b), IND(*Yall, R("L1", a, b)))
-        sact(R("Yt", 1024 - 16 * YS, 1024), IND(*Yall, R("L1", 64 - YS, 64)))
-        for j, (a, b) in enumerate(CH):
-            o = R("pb%d" % j, 0, 16 * (b - a))
-            pe([mm(o, a128("identb"), R("Yt", 16 * a, 16 * b), True, False),
-                mm(o, a128("identn"), R("Zt", 16 * a, 16 * b), False, True)])
-        c0 = 16 * CH[0][1]
-        vts(R("ng", 0, c0), R("pb0", 0, c0), -1.0, None, O.mult)
-        vtt(R("AD", 0, c0), R("pb0", 0, c0), R("ng", 0, c0), O.max)
-        for j in (1, 2):
-            a, b = CH[j]
-            sact(R("AD", 16 * a, 16 * b), R("pb%d" % j, 0, 16 * (b - a)), AF.Abs)
-        K = R("pb3", 0, 64)
-        pe([mm(K, a128("biasd"), a64("ones64"), True, False)] +
-           [mm(K, R("Es", 15 - k, 143 - k), R("AD", k, 1024, 16), False, k == 15) for k in range(16)])
-        OH = R("pb5", 0, 64)
-        vtr(a64("KT"), K)
-        vscan(a64("Fs"), a64("reset"), a64("KT"), 0.0, O.mult, O.max)
-        for s in range(4):
-            vts(R("OHt", 16 * s, 16 * s + 16), R("KT", 16 * s, 16 * s + 16), C("Fs", 16 * s + 15), None, O.is_equal)
-        vtr(OH, a64("OHt"))
-        vtt(R("pr", 0, 64), OH, R("nf", 0, 64), O.mult)
-        vtt(R("pr", 64, 128), OH, R("nf", 64, 128), O.mult)
-        ROW = R("pb4", 0, 128)
-        pe([mm(ROW, a128("blkf"), a128("pr"), True, True)])
-        vts(a64("kz"), K, 16.0, None, O.is_lt)
-        vtt(a64("kz2"), a64("kz"), OH, O.mult)
-        vtt(a128("mk"), ROW, a128("mask"), O.mult)
-        vscan(a128("sc"), a128("reset"), a128("mk"), 0.0, O.mult, O.add)
-        vts(R("LAQ", 0, 8), R("sc", 15, 128, 16), 1023.0, None, O.min)
-        la, lq = R("LAQ", 0, 4), R("LAQ", 4, 8)
-        vcopy(R("L2", 0, 64), IND("tNZM", OWN, OWN + 1024, la))
-        vcopy(R("L2", 64, 128), IND("tNBI", OWN, OWN + 1024, lq))
-        vcopy(R("L2", 128, 192), IND("tNZ", 0, 1024, lq))
-        for n, c in (("Bt", 0), ("Bp", 128)):
+        Zn, Yn = "ZW%d" % r, "YW%d" % r
+        Zall, Yall, Zown = (Zn, OWN, OWN + 1792), (Yn, OWN, OWN + 1792), (Zn, OWN, OWN + 1024)
+        Mown, Iown = ("tM", OWN, OWN + 1024), ("tIM", OWN, OWN + 1024)
+        if more:
+            arrived("Y", r)
+            if r == 0:
+                dma("Y", "ld_x", R("tX", 0, 1024), T.x[:])
+            for w in "ZY":
+                dma("Y", "cp_%s%d" % (w, r), R("%sW%d" % (w, r + 1), OWN, OWN + 1024), R("%sW%d" % (w, r), OWN, OWN + 1024))
+        K = R("ps3", 0, 64)
+        pe([mm(K, a128("identb"), a64("brow"), True, False)])
+        for (a, b, who) in CH:
+            sact(R("Zt", 64 * a, 64 * b), IND(*Zall, R("L1", 64 + 4 * a, 64 + 4 * b)))
+        for (a, b, who) in CH:
+            vtt(R("Dt", 64 * a, 64 * b), IND(*Yall, R("L1", 4 * a, 4 * b)), R("Zt", 64 * a, 64 * b), O.subtract)
+        Es = lambda j, f: R("Es", 144 * j + 15 - f, 144 * j + 143 - f)
+        col = lambda n, f: R(n, 64 * f, 64 * f + 64)
+        for (a, b, who) in CH:
+            if who == "V":
+                pe([mm(K, Es(2, f), col("Dt", f), False, False) for f in range(a, b)])
+        for (a, b, who) in CH:
+            if who == "S":
+                sact(R("AD", 64 * a, 64 * b), R("Dt", 64 * a, 64 * b), AF.Abs)
+            else:
+                vts(R("AD", 64 * a, 64 * b), R("Dt", 64 * a, 64 * b), 0.0, None, O.max)
+            pe([mm(K, Es(0 if who == "S" else 1, f), col("AD", f), False, f == 15) for f in range(a, b)])
+        vscan(a64("Fs"), a64("reset"), K, 0.0, O.mult, O.max)
+        vtt(a64("ns"), K, a64("Fs"), O.is_lt)
+        vscan(R("SC", 64, 128), a64("ns"), R("DL", 64, 128), 0.0, O.mult, O.add)
+        vscan(R("SC", 0, 64), a64("ns"), R("DL", 0, 64), 0.0, O.mult, O.add)
+        vts(R("LL", 0, 8), ends("SC", 0, 8), 1023.0, None, O.min)
+        sact(R("rv", 8, 12), ends("Fs", 0, 4), AF.Relu, -VOID, 16.0 * VOID)
+        sact(R("rv", 0, 8), ends("SC", 0, 8), AF.Relu, VOID, -1023.0 * VOID)
+        vcopy(R("L2", 0, 64), IND("tNZ", 0, 1024, lq))
+        vcopy(R("L2", 64, 128), IND("tNB", 0, 1024, la))
+        vtt(R("mk2", 0, 64), IND(*Mown, la), a64("mask"), O.mult)
+        vtt(R("mk2", 64, 128), IND(*Iown, lq), a64("mask"), O.mult)
+        vd = R("ps4", 0, 4)
+        pe([mm(vd, a128("identb"), R("cst4", 0, 4), True, False)] +
+           [mm(vd, a128("identn"), R("rv", 4 * j, 4 * j + 4), False, j == 2) for j in range(3)])
+        vscan(R("SC", 128, 256), a128("reset"), a128("mk2"), 0.0, O.mult, O.add)
+        vcopy(R("LL", 8, 16), ends("SC", 128, 8))
+        vcopy(R("L2", 128, 192), IND("tNZ", 0, 1024, lp))
+        vcopy(R("L2", 192, 256), IND("tNB", 0, 1024, lw))
+        for n, c in (("Bp", 0), ("Bt", 128)):
             for h in (0, 1):
                 sact(R(n, 512 * h, 512 * h + 512), IND(*Zall, R("L2", c + 32 * h, c + 32 * h + 32)))
-        sact(R("At", 1024 - 16 * AS, 1024), IND(*Yall, R("L2", 128 - AS, 128)))
-        vcopy(R("At", 0, 1024 - 16 * AS), IND(*Yall, R("L2", 64, 128 - AS)))
-        vcopy(R("L2", 192, 256), IND("tNB", 0, 1024, la))
-        vcopy(R("WP", 0, 64), IND("tIM", OWN, OWN + 1024, lq))
-        vcopy(R("WP", 64, 128), IND(mt, OWN, OWN + 1024, la))
-        vts(a128("gh"), ROW, 1024.0, None, O.is_ge)
-        vtt(a128("mk2"), a128("WP"), MP, O.mult)
-        sact(a128("AQ"), ROW)
-        sact(R("NR", 0, 128, 2), R("AQ", 0, 64))
-        sact(R("NR", 1, 128, 2), R("WP", 0, 64))
-        vtt(R("T1", 0, 1024), IND(*Yall, R("L2", 192, 256)), R("Bt", 0, 1024), O.max)
-        vscan(a128("sc2"), a128("reset"), a128("mk2"), 0.0, O.mult, O.add)
-        vts(R("NLc", 0, 8), R("sc", 15, 128, 16), 1023.0, float(OWN), O.min, O.add)
-        vts(R("NLc", 8, 16), R("sc2", 15, 128, 16), float(OWN), None, O.add)
-        vcopy(R("LWP", 0, 8), R("sc2", 15, 128, 16))
-        vtt(R("T2", 0, 1024), IND(*Yall, R("L2", 192, 256)), R("Bp", 0, 1024), O.max)
-        if more:
-            need("G", "cv", cnt["cv"])
-            need("G", "cs", max(e[5] for w in ("ZW", "YW") for e in acc[w] if e[3] == "S"))
-            need("G", "sl", nsl[0])
-            for d in writers:
-                rid, pid = topo.addr(d, core)
-                g.remote_sem_update(T.sem["rdy%d" % (r + 1)], T.sem.sl, pid, rid, 1 << topo.engines(core, d)[0])
-                nsl[0] += 1
-            total["rdy%d" % (r + 1)] = tell
-        Gn = R("pb6", 0, 64)
+        if AS:
+            sact(R("At", 1024 - 16 * AS, 1024), IND(*Yall, R("L2", 256 - AS, 256)))
+        vcopy(R("At", 0, 512), IND(*Yall, R("L2", 192, 224)))
+        vtt(R("T2", 0, 1024), IND(*Yall, R("L2", 64, 128)), R("Bp", 0, 1024), O.max)
+        if AS < 32:
+            vcopy(R("At", 512, 1024 - 16 * AS), IND(*Yall, R("L2", 224, 256 - AS)))
+        vtt(R("T1", 0, 1024), IND(*Yall, R("L2", 64, 128)), R("Bt", 0, 1024), O.max)
+        Gn = R("ps6", 0, 64)
+        CS = R("ps7", 0, 128)
         dif = {}
 
         def diff(bk, src, h):
@@ -390,100 +394,96 @@ def rank_program(g, core, T, topo):
             pe([mm(o, a128("identb"), R(src, a, b), True, False), mm(o, a128("identn"), R("At", a, b), False, True)])
             dif[src, h] = o
 
-        def term(n, l):
-            pe([mm(Gn, a128(l), R(n, k, 1024, 16), False, n == "R2" and k == 15) for k in range(16)])
-        diff("pb0", "Bt", 0)
-        diff("pb2", "Bp", 0)
-        pe([mm(Gn, a128("idV"), R("gh", 0, 64), True, False), mm(Gn, a128("idV"), R("gh", 64, 128), False, False),
-            mm(Gn, a128("blkV"), a64("kz2"), False, False)])
-        term("T1", "blkp")
-        diff("pb1", "Bt", 1)
-        diff("pb5", "Bp", 1)
-        for (n, src, h) in (("R1", "Bt", 0), ("R2", "Bp", 0), ("R1", "Bt", 1), ("R2", "Bp", 1)):
+        def term(n, l, last=False):
+            pe([mm(Gn, a128(l), R(n, k, 1024, 16), False, last and k == 15) for k in range(16)])
+        pe([mm(Gn, a128("identb"), a64("offG"), True, False), mm(Gn, a128("identb"), a64("stepG"), False, False)])
+        pe([mm(CS, a128("identb"), a128("offC"), True, False), mm(CS, a128("identb"), a128("thrC"), False, False)])
+        diff("ps0", "Bp", 0)
+        diff("ps1", "Bt", 0)
+        term("T2", "blkm")
+        diff("ps2", "Bp", 1)
+        diff("ps5", "Bt", 1)
+        sact(R("NR", 0, 128, 2), IND(*Iown, lp))
+        sact(R("NR", 1, 128, 2), IND(*Iown, lq))
+        if r:
+            sact(ends("E1", 0, 4), vd, AF.Identity, 1.0, C("nth"))
+        else:
+            sact(ends("E1", 0, 4), vd)
+        for j, (n, src, h) in enumerate((("R2", "Bp", 0), ("R1", "Bt", 0), ("R2", "Bp", 1), ("R1", "Bt", 1))):
             o = R(n, 512 * h, 512 * h + 512)
-            if n == "R1" and h == 0:
+            if j >= 4 - RV:
                 vts(o, dif[src, h], 0.0, None, O.max)
             else:
                 sact(o, dif[src, h], AF.Relu)
-        term("T2", "blkm")
-        term("R1", "blkm")
+        term("T1", "blkp")
         term("R2", "blkp")
-        sact(R("zz", 0, 64), IND(*Zown, lq))
+        term("R1", "blkm", True)
+        sact(a128("zz"), IND(*Zown, R("LL", 4, 12)))
         sact(R("xx", 0, 64), IND("tX", 0, 1024, la))
-        sact(R("zz", 64, 128), IND(*Zown, R("LWP", 4, 8)))
-        sact(R("xx", 64, 128), IND("tX", 0, 1024, R("LWP", 0, 4)))
+        sact(R("xx", 64, 128), IND("tX", 0, 1024, lw))
         eqs, at = [], 0
         for c in range(4):
-            for col in (C("sc", 16 * c + 15), C("sc2", 16 * c + 15)):
+            for k in (16 * c + 15, 192 + 16 * c + 15):
                 w = 128 - 32 * c
-                vts(R("EQ", at, at + w), R("NR", 32 * c, 128), col, None, O.is_equal)
+                vts(R("EQ", at, at + w), R("NR", 32 * c, 128), C("SC", k), None, O.is_equal)
                 eqs.append((c, at, w))
                 at += w
-        vtt(a64("x1"), Gn, a64("TH") if r else a64("nmB"), O.is_gt)
-        vscan(a64("sp"), a64("reset"), a64("x1"), 0.0, O.mult, O.add)
-        for c in range(4):
-            vts(R("WT", 128 * c, 128 * c + 128), R("W4", 128 * c, 128 * c + 128), C("sp", 16 * c + 15), None, O.mult)
-        vts(a64("npr"), Gn, C("thc") if r else 0.0, None, O.is_le)
-        xz = R("pb4", 128, 256)
+        vts(R("NLc", 0, 16), ends("SC", 0, 16), float(OWN), None, O.add)
+        vscan(a64("GS"), Gn, a64("E1"), -4.0 * FAR, O.max, O.add)
+        xz = R("ps4", 128, 256)
         pe([mm(xz, a128("identb"), a128("xx"), True, False), mm(xz, a128("identn"), a128("zz"), False, True)])
-        vts(a128("cl"), xz, -1.0, 1.0, O.max, O.min)
-        CS = R("pb7", 0, 64)
+        sact(a128("cl"), xz, AF.Sign)
         for c in range(4):
-            pe([mm(R("pb7", 16 * c, 64), R("WT", 128 * c, 128 * c + 128), R("EQ", at + nm, at + w, 2),
-                   c == 0 and (at, nm) == (0, 0), False) for (c2, at, w) in eqs if c2 == c for nm in (0, 1)])
-        pe([mm(CS, a128("idN"), a64("npr"), False, True)])
-        nzp = R("pb3", 128, 256)
+            WT = R("WT", 128 * c, 128 * c + 128)
+            vts(WT, a128("blkH"), C("GS", 16 * c + 15), C("WL", 16 * c + 15), O.is_lt, O.mult)
+            pe([mm(R("ps7", 32 * c, 128), WT, R("EQ", at, at + w), False, False) for (c2, at, w) in eqs if c2 == c] +
+               [mm(R("ps7", 32 * c, 32 * c + 32), WT, R("selfC", 0, 32), False, c == 3)])
+        nzp = R("ps3", 128, 256)
         pe([mm(nzp, a128("identb"), a128("zz"), True, False), mm(nzp, a128("identb"), a128("cl"), False, True)])
         sact(a128("nzv"), nzp)
+        sact(R("QP", 0, 64), IND(*Mown, lw))
+        sact(R("QP", 64, 128), IND(*Mown, la))
         if more:
-            vts(R("oq", 0, 4), R("sc", 79, 128, 16), 1024.0, None, O.is_lt)
-            vtt(R("d1", 0, 4), R("sc2", 15, 64, 16), R("V5", 0, 4), O.subtract)
-            vtt(R("d2", 0, 4), R("d1", 0, 4), R("oq", 0, 4), O.mult)
-            vtt(R("alt", 0, 4), R("d2", 0, 4), R("V5", 0, 4), O.add)
-            vtt(R("da", 0, 4), R("sc", 15, 64, 16), R("alt", 0, 4), O.subtract)
-        vtt(a64("cm"), CS, a64("thrM"), O.is_le)
-        vscan(a64("cl2"), a64("reset"), a64("cm"), 0.0, O.mult, O.add)
+            vts(R("v5a", 0, 4), R("s6o", 2, 12, 3) if r else R("VL", 0, 4), 5.0, 1.0, O.mult, O.add)
+            vts(R("s6a", 1, 12, 3), fq, 1024.0, None, O.is_ge)
+        vscan(a128("BS"), a128("reset32"), CS, 0.0, O.mult, O.max)
         for c in range(4):
-            vts(R("OFF", c, 16, 4), R("NLc", c, 16, 4), C("cl2", 16 * c + 15), C("lane4", c), O.mult, O.max)
-        oa, oqq, ow, op = [R("OFF", 4 * n, 4 * n + 4) for n in range(4)]
+            vts(R("OFF", c, 16, 4), R("NLc", c, 16, 4), C("BS", 32 * c + 31), C("lane4", c), O.subtract, O.max)
+        oa, oq, op, ow = [R("OFF", 4 * n, 4 * n + 4) for n in range(4)]
         sca = lambda n, off, d: vcopy(IND(n, 0, OWN + 1024, off), d)
-        sca("ZW", oqq, R("nzv", 0, 64))
-        sca("ZW", op, R("nzv", 64, 128))
+        e = r + 1 if more else r
+        sca("ZW%d" % e, oq, R("nzv", 0, 64))
         if not more:
-            store("Y", "st_z", T.zo[:], R("ZW", OWN, OWN + 1024))
-            sca("MF", oa, R("AQ", 64, 128))
-            sca("MF", ow, R("WP", 64, 128))
-            store("Y", "st_m", T.mo[:], (T.MF[0:128:16, OWN:OWN + 1024], [("MF", OWN, OWN + 1024)], []))
+            sca("tM", oa, R("QP", 0, 64))
+            sca("ZW%d" % e, op, R("nzv", 64, 128))
+            dma("Y", "st_z", T.zo[:], R("ZW%d" % e, OWN, OWN + 1024))
+            sca("tM", ow, R("QP", 64, 128))
+            dma("S", "st_m", T.mo[:], (T.tM[0:128:16, OWN:OWN + 1024], [("tM", OWN, OWN + 1024, 1)], []))
             break
-        e = r + 1
-        sact(R("SZ", 256 * e, 256 * e + 256), IND(*Zown, R("BL", 16, 32)))
-        sca("YW", oa, R("nzv", 0, 64))
-        sca("YW", ow, R("nzv", 64, 128))
-        need("G", "rdy%d" % e, tell)
+        vts(R("s6a", 2, 12, 3), ends("BS", 0, 4, 32), 0.0, None, O.is_gt)
+        sca("ZW%d" % e, op, R("nzv", 64, 128))
+        sact(R("SZ", 256 * e, 256 * e + 256), IND("ZW%d" % e, OWN, OWN + 1024, R("BL", 16, 32)))
+        sca("YW%d" % e, oa, R("nzv", 0, 64))
+        vts(R("v5b", 0, 4), R("v5a", 0, 4), 1023, None, O.bitwise_and)
+        sca("YW%d" % e, ow, R("nzv", 64, 128))
         borders(e)
-        vtt(R("d3", 0, 4), R("da", 0, 4), R("cl2", 15, 64, 16), O.mult)
-        sca("tNZM", oa, R("L2", 128, 192))
-        sca("tNZM", ow, R("L2", 0, 64))
-        vtt(R("VL", 0, 4), R("d3", 0, 4), R("alt", 0, 4), O.add)
-        vsum(C("cn"), a64("cm"))
-        vcopy(R("vl", 0, 4), R("VL", 0, 4))
-        vcopy(C("cnt"), C("cn"))
-        vcopy(R("L1", 0, 64), IND("tNB", 0, 1024, R("vl", 0, 4)))
-        pe([mm(R("pb7", 256, 257), a128("onesb"), C("cnt"), True, True)])
-        vcopy(R("L1", 64, 128), IND("tNZM", OWN, OWN + 1024, R("vl", 0, 4)))
-        sca("tNBI", oqq, R("L2", 192, 256))
-        sca("tNBI", op, R("L2", 64, 128))
-        vcopy(C("thi"), R("pb7", 256, 257))
-        step_lists()
+        vtt(R("s6b", 0, 12, 3), R("v5b", 0, 4), fw, O.subtract)
+        vtt(R("s6b", 1, 12, 3), fw, fa, O.subtract)
+        vcopy(R("s6b", 2, 12, 3), fa)
+        sca("tM", oa, R("QP", 0, 64))
+        vscan(R("s6o", 0, 12), R("s6a", 0, 12), R("s6b", 0, 12), 0.0, O.mult, O.add)
+        sca("tM", ow, R("QP", 64, 128))
+        vcopy(R("vl", 0, 4), R("s6o", 2, 12, 3))
+        cn = R("ps4", 256, 257)
+        pe([mm(cn, a128("onesf"), C("s6a", 3 * c + 2), c == 0, c == 3) for c in range(4)])
+        sca("tIM", oq, R("NR", 0, 128, 2))
+        vtt(a64("mkv"), IND(*Mown, R("vl", 0, 4)), a64("mask"), O.mult)
+        vcopy(R("nf", 16, 80), IND("tNB", 0, 1024, R("vl", 0, 4)))
+        lane_lists(None)
+        sca("tIM", op, R("NR", 1, 128, 2))
+        vts(C("thi"), cn, -1.0, 512.0, O.mult, O.add)
         vts(C("thj"), C("thi"), 31, None, O.bitwise_and)
-        sca(mt, oa, R("AQ", 64, 128))
-        vcopy(C("thc"), C("thj"))
-        sca(mt, ow, R("WP", 64, 128))
-        vts(a64("TH"), a64("nmB"), C("thc"), None, O.add)
-        sca("tIM", oqq, R("AQ", 0, 64))
-        sca("tIM", op, R("WP", 0, 64))
-        if r == 0:
-            vcopy(R("MF", OWN, OWN + 1024), R("tM", OWN, OWN + 1024))
+        vts(C("nth"), C("thj"), -1.0, None, O.mult)
 
     total.update(cnt)
     total["sl"] = nsl[0]

@@ -7,25 +7,26 @@ _W = {
              At=1024, Bt=1024, Bp=1024, T1=1024, T2=1024, R1=1024, R2=1024, zz=128, xx=128, cl=128, nzv=128, EQ=640, rv=16,
              WT=512, identb=128, identn=128, blkp=128, blkm=128, blkH=128, Es=432, brow=64, cst4=4, offG=64, stepG=64,
              offC=128, thrC=128, selfC=32),
-    F4: dict(IOTA=1024, tM=1152, tIM=1152, mlf=128, mlt=128, nf=160, TT=296, Tn=128, DL=128, Fs=64, ns=64, SC=256, mk2=128,
-             E1=64, GS=64, BS=128, NR=128, QP=128, NLc=16, s6a=12, s6b=12, s6o=12, VL=4, mkv=64, scv=64, nth=2, onesf=128,
+    F4: dict(IOTA=1024, tM=1152, tIM=1152, mlf=96, mlt=160, pm=2, nf=160, TT=288, TH=576, sub1=128, sub2=128, bidi=128, DL=128, Fs=64, ns=64, SC=256, mk2=128,
+             E1=64, GS=64, BS=128, NR=128, QP=128, NLc=16, s6a=12, s6b=12, s6o=12, VL=4, mkv=64, scv=64, nth=16, onesf=128,
              itf=128, gf=128, ff=2, gp=2, mask=128, blkf=128, identf=128, reset=128, reset32=128, half=64, wrow=64, wm=64,
-             WL=64, lane4=4, pbase=8, f2=2, ps=2, fv=8, b16=8, foldf=8, n15=2, n16=2),
-    I4: dict(tNB=1024, tNZ=1024, ml=128, bl=32, v5a=4, v5b=4, thi=2, thj=2, c_p=2, fI=2, gI=2, f3I=2, f2I=2, pa=8, pb=8),
-    U2: dict(ML=128, BL=32, L1=128, LL=16, L2=256, OFF=16, vl=4, mvl=4, PERM=8, FOLD=8, NEXT=8),
+             WL=64, lane4=4, pbase=8, f2=2, ps=2, fv=8, b16=8, foldf=8),
+    I4: dict(tNB=1024, tNZ=1024, ml=128, bl=32, v5a=4, v5b=4, c_p=2, fI=2, gI=2, f3I=2, f2I=2, pa=8, pb=8, fg=2, fg1=2),
+    U2: dict(MF=4, ML=128, BL=32, L1=128, LL=16, L2=256, OFF=16, vl=4, mvl=4, PERM=8, FOLD=8, thl=2),
 }
 SCRATCH = {n: ("sbuf", [128, w], d) for d in _W for n, w in _W[d].items()}
 for _i in range(8):
     SCRATCH["ps%d" % _i] = ("psum", [128, 512], F4)
 N = 8
-SEMAPHORES = ["cv", "cs", "cp", "cg", "ld_z", "ld_b", "ld_m", "ld_im", "ld_nz", "ld_nb", "ld_x", "cp_Z0", "cp_Z1", "cp_Y0", "cp_Y1",
+SEMAPHORES = ["cv", "cs", "cp", "cg", "ld_z", "ld_bx", "ld_bz", "ld_m", "ld_im", "ld_nz", "ld_nb", "ld_x", "cp_Z0", "cp_Z1", "cp_Y0", "cp_Y1",
               "st_z", "st_m", "sl"] + ["%s%d_%d" % (w, e, s) for w in "YZ" for e in range(3) for s in range(N)]
 OWN = 128
 STEP, FAR, VOID = 2.0 ** 19, 2.0 ** 23, 2.0 ** 18
 WTOP, HUGE = 2.0 ** 75, 2.0 ** 80
-CFG = dict(CH=[(0, 2, "S"), (2, 6, "S"), (6, 11, "V"), (11, 16, "V")],
-           AS=16,
-           RV=1)
+CFG = dict(ZC=[(0, 8, "S"), (8, 16, "V")], FUSE=1, ZS=8, YS=5,
+           CH=[(12, 16, "S"), (8, 12, "V"), (5, 8, "V")],
+           ORD=0, AS=32,
+           RV=512)
 
 
 def rank_program(g, core, T, topo):
@@ -38,7 +39,7 @@ def rank_program(g, core, T, topo):
     total = {}
     seen = {q: {} for q in QUEUE}
     acc = {}
-    CH, AS, RV = CFG["CH"], CFG["AS"], CFG["RV"]
+    CH, AS, RV, ZS, YS = CFG["CH"], CFG["AS"], CFG["RV"], CFG["ZS"], CFG["YS"]
 
     def need(q, sem, val):
         if seen[q].get(sem, 0) < val:
@@ -147,44 +148,40 @@ def rank_program(g, core, T, topo):
     a64 = lambda n: R(n, 0, 64)
     ends = lambda n, a, k, s=16: R(n, a + s - 1, a + s * k, s)
 
-    def lists(a, sem, src):
-        for h in (0, 1):
-            for b in (0, 1):
-                c = a + 32 * b + 16 * h
-                dma("Y", sem, R("ml", c, c + 16), src[h:8:2, 512 * b:512 * b + 512], 4)
-    dma("S", "ld_b", R("bl", 0, 16), T.bx[:], 2)
-    dma("S", "ld_b", R("bl", 16, 32), T.bz[:], 2)
-    lists(0, "ld_m", T.m)
-    dma("S", "ld_z", R("ZW0", OWN, OWN + 1024), T.z[:])
+    dma("Y", "ld_m", R("ml", 0, 64), T.m[:])
+    dma("S", "ld_bz", R("bl", 16, 32), T.bz[:])
+    dma("Y", "ld_z", R("ZW0", OWN, OWN + 1024), T.z[:])
+    dma("S", "ld_bx", R("bl", 0, 16), T.bx[:])
     dma("Y", "ld_nz", R("tNZ", 0, 1024), T.nz[:])
     dma("Y", "ld_nb", R("tNB", 0, 1024), T.nb[:])
-    lists(64, "ld_im", T.im)
+    dma("Y", "ld_im", R("ml", 64, 128), T.im[:])
 
     emit("G", [lambda: g.iota(T.c_p[:, 0:2], [[0, 2]], 0, 1)], [R("c_p", 0, 2)], [])
+    giota(R("pbase", 0, 8), [[64, 2], [4, 4]], 0, 0)
     giota(a128("itf"), [[0, 8], [1, 16]], 0, 0)
     giota(a128("gf"), [[1, 8], [0, 16]], 0, 0)
-    giota(R("pbase", 0, 8), [[64, 2], [4, 4]], 0, 0)
     giota(a64("brow"), [[0, 4], [-1, 16]], 15, 0)
     giota(R("IOTA", 0, 512), [[1, 512]], 0, 0)
+    vset(R("mlf", 0, 96), 0.0)
     vset(a64("E1"), 0.0)
-    vset(a64("half"), 0.5)
     vts(R("fI", 0, 2), R("c_p", 0, 2), 15, None, O.bitwise_and)
     vts(R("gI", 0, 2), R("c_p", 0, 2), 4, None, O.arith_shift_right)
-    vset(R("Es", 0, 432), 0.0)
-    vcopy(R("ff", 0, 2), R("fI", 0, 2))
-    vcopy(R("gp", 0, 2), R("gI", 0, 2))
+    vset(a64("half"), 0.5)
     vts(R("f3I", 0, 2), R("fI", 0, 2), 3, None, O.bitwise_and)
     vts(R("f2I", 0, 2), R("fI", 0, 2), 2, None, O.arith_shift_right)
-    vts(a128("mask"), a128("itf"), C("ff"), None, O.is_equal)
-    vts(a128("reset"), a128("itf"), 0.0, None, O.is_gt)
+    vtt(R("fg", 0, 2), R("fI", 0, 2), R("gI", 0, 2), O.add)
+    vcopy(R("ff", 0, 2), R("fI", 0, 2))
     vcopy(R("f2", 0, 2), R("f2I", 0, 2))
-    vts(a128("blkf"), a128("gf"), C("gp"), None, O.is_equal)
-    vscan(a64("wrow"), a64("half"), a64("E1"), 2.0 * WTOP, O.mult, O.add)
+    vts(R("fg1", 0, 2), R("fg", 0, 2), 1, None, O.bitwise_and)
     vts(R("ps", 0, 2), R("f3I", 0, 2), 16.0, C("f2"), O.mult, O.add)
-    vset(R("nf", 0, 160), 0.0)
-    vts(R("pa", 0, 8), R("gf", 0, 128, 16), C("gp"), None, O.add)
+    vcopy(R("gp", 0, 2), R("gI", 0, 2))
+    vts(R("pm", 0, 2), R("fg1", 0, 2), 80.0, C("ps"), O.mult, O.add)
+    vts(a128("mask"), a128("itf"), C("ff"), None, O.is_equal)
+    vts(R("MF", 0, 4), R("pbase", 0, 4), C("pm"), None, O.add)
+    vts(a128("reset"), a128("itf"), 0.0, None, O.is_gt)
+    vts(a128("blkf"), a128("gf"), C("gp"), None, O.is_equal)
     vts(R("PERM", 0, 8), R("pbase", 0, 8), C("ps"), None, O.add)
-    vcopy(R("BL", 0, 32), R("bl", 0, 32))
+    vcopy(R("BL", 16, 32), R("bl", 16, 32))
 
     def near(c):
         return topo.cores_of(c)
@@ -229,7 +226,9 @@ def rank_program(g, core, T, topo):
             return [[(w, lead, ml_), (w, other, mo_)] for w in "ZY"]
         if e == 0:
             return [[(w, t, wmask(s, t))] for w in "ZY" for t in (lead, other)]
-        return [[(w, lead, ml_)] for w in "ZY"] + [[(w, other, m) for w, m in zip("ZY", halves(mo_))]]
+        if CFG["FUSE"]:
+            return [[(w, lead, ml_)] for w in "ZY"] + [[(w, other, m) for w, m in zip("ZY", halves(mo_))]]
+        return [[(w, t, wmask(s, t))] for t in (lead, other) for w in "ZY"]
 
     def put(items):
         ts = []
@@ -264,30 +263,36 @@ def rank_program(g, core, T, topo):
             if s[:3] in ("Y%d_" % e, "Z%d_" % e):
                 need(q, s, v)
 
-    sact(R("SZ", 0, 256), IND("ZW0", OWN, OWN + 1024, R("BL", 16, 32)))
-
     def mlist(a):
-        vcopy(R("mlf", a, a + 64), R("ml", a, a + 64))
-        vtr(R("mlt", a, a + 64), R("mlf", a, a + 64))
-        vcopy(R("ML", a, a + 64), R("mlt", a, a + 64))
+        vcopy(R("mlf", 16, 80), R("ml", a, a + 64))
+        vtr(R("mlt", 0, 64), R("mlf", 16, 80))
+        vtr(R("mlt", 64, 160), R("mlf", 0, 96))
+        vcopy(R("ML", a, a + 64), IND("mlt", 0, 160, R("MF", 0, 4)))
     mlist(0)
+    vcopy(R("SZ", 0, 128), IND("ZW0", OWN, OWN + 1024, R("BL", 16, 24)))
+    sact(R("SZ", 128, 256), IND("ZW0", OWN, OWN + 1024, R("BL", 24, 32)))
+    vcopy(R("BL", 0, 16), R("bl", 0, 16))
     vcopy(R("YW0", OWN, OWN + 512), IND("ZW0", OWN, OWN + 1024, R("ML", 0, 32)))
     sact(R("YW0", OWN + 512, OWN + 1024), IND("ZW0", OWN, OWN + 1024, R("ML", 32, 64)))
     borders(0)
 
+    giota(R("TH", 0, 576), [[0, 18], [1, 32]], -31, 0)
     sact(R("IOTA", 512, 1024), R("IOTA", 0, 512), AF.Identity, 1.0, 512.0)
     sact(R("tM", OWN, OWN + 1024), IND("IOTA", 0, 1024, R("ML", 0, 64)))
+    vset(R("Es", 0, 432), 0.0)
+    vscan(a64("wrow"), a64("half"), a64("E1"), 2.0 * WTOP, O.mult, O.add)
+    vset(R("nf", 0, 160), 0.0)
+    vts(R("pa", 0, 8), R("gf", 0, 128, 16), C("gp"), None, O.add)
     vts(R("pb", 0, 8), R("pa", 0, 8), 1, None, O.bitwise_and)
     vts(R("b16", 0, 8), R("gf", 0, 128, 16), 16.0, None, O.mult)
     vtt(a128("identf"), a128("blkf"), a128("mask"), O.mult)
     vts(R("fv", 0, 8), R("pb", 0, 8), 144.0, C("ff"), O.mult, O.add)
-    vts(C("n15"), C("ff"), 15.0, 999.0, O.is_equal, O.mult)
+    vts(a128("sub1"), a128("itf"), 1.0, C("ff"), O.add, O.is_equal)
     vtt(a64("wm"), a64("wrow"), a64("mask"), O.mult)
     vtt(R("foldf", 0, 8), R("fv", 0, 8), R("b16", 0, 8), O.add)
-    vts(C("n16"), C("n15"), 1.0, None, O.add)
-    vset(R("TT", 288, 296), 0.0)
+    vtt(a128("sub2"), a128("mask"), a128("sub1"), O.subtract)
     vcopy(R("FOLD", 0, 8), R("foldf", 0, 8))
-    vts(R("NEXT", 0, 8), R("foldf", 0, 8), C("n16"), 288.0, O.add, O.min)
+    vtt(a128("bidi"), a128("sub2"), a128("blkf"), O.mult)
     vts(R("lane4", 0, 4), R("gf", 0, 64, 16), 16.0, C("ff"), O.mult, O.add)
     vscan(a64("WL"), a64("reset"), a64("wm"), 0.0, O.mult, O.add)
     vset(a128("reset32"), 1.0)
@@ -298,21 +303,20 @@ def rank_program(g, core, T, topo):
     vts(R("VL", 0, 4), R("lane4", 0, 4), 16.0, None, O.mult)
     mlist(64)
 
-    def lane_lists(mrow):
+    def lane_lists():
         vscan(a64("scv"), a64("reset"), a64("mkv"), 0.0, O.mult, O.add)
         vcopy(R("mvl", 0, 4), ends("scv", 0, 4))
         vcopy(R("nf", 80, 144), IND("tNZ", 0, 1024, R("mvl", 0, 4)))
+        pe([mm(R("ps5", 0, 160), a128("bidi"), R("nf", 0, 160), True, True)])
         vcopy(a128("L1"), IND("nf", 16, 144, R("PERM", 0, 8)))
-        vtr(R("TT", 0, 128), R("nf", 16, 144))
-        vtr(R("TT", 128, 288), R("nf", 0, 160))
-        sact(a128("Tn"), IND("TT", 0, 296, R("NEXT", 0, 8)))
-        vtt(a128("DL"), IND("TT", 0, 296, R("FOLD", 0, 8)), a128("Tn"), O.subtract)
+        vtr(R("TT", 0, 128), R("ps5", 16, 144))
+        vtr(R("TT", 128, 288), R("ps5", 0, 160))
     vcopy(R("nf", 16, 80), R("tNB", 0, 1024, 16))
     vtt(a64("mkv"), R("tM", OWN, OWN + 1024, 16), a64("mask"), O.mult)
     sact(a128("identb"), a128("identf"))
     for j, k in enumerate((16.0, 32.0, -16.0)):
         sact(R("Es", 144 * j + 15, 144 * j + 143, 16), R("blkf", 0, 128, 16), AF.Copy, k)
-    lane_lists(None)
+    lane_lists()
     sact(R("tIM", OWN, OWN + 1024), IND("IOTA", 0, 1024, R("ML", 64, 128)))
     sact(a128("identn"), a128("identf"), AF.Copy, -1.0)
     sact(a128("blkp"), a128("blkf"), AF.Copy, 2.0)
@@ -328,6 +332,8 @@ def rank_program(g, core, T, topo):
 
     la, lq, lp, lw = [R("LL", 4 * n, 4 * n + 4) for n in range(4)]
     fa, fq, fp, fw = [ends("SC", 64 * n, 4) for n in range(4)]
+    oa, oq, op, ow = [R("OFF", 4 * n, 4 * n + 4) for n in range(4)]
+    sca = lambda n, off, d: vcopy(IND(n, 0, OWN + 1024, off), d)
     for r in range(3):
         more = r < 2
         Zn, Yn = "ZW%d" % r, "YW%d" % r
@@ -341,26 +347,48 @@ def rank_program(g, core, T, topo):
                 dma("Y", "cp_%s%d" % (w, r), R("%sW%d" % (w, r + 1), OWN, OWN + 1024), R("%sW%d" % (w, r), OWN, OWN + 1024))
         K = R("ps3", 0, 64)
         pe([mm(K, a128("identb"), a64("brow"), True, False)])
-        for (a, b, who) in CH:
-            sact(R("Zt", 64 * a, 64 * b), IND(*Zall, R("L1", 64 + 4 * a, 64 + 4 * b)))
-        for (a, b, who) in CH:
-            vtt(R("Dt", 64 * a, 64 * b), IND(*Yall, R("L1", 4 * a, 4 * b)), R("Zt", 64 * a, 64 * b), O.subtract)
+        part = lambda n, a, b: R(n, 64 * a, 64 * b)
         Es = lambda j, f: R("Es", 144 * j + 15 - f, 144 * j + 143 - f)
-        col = lambda n, f: R(n, 64 * f, 64 * f + 64)
+        left = [16]
+
+        def keys(j, n, a, b):
+            left[0] -= (b - a) * (j != 2)
+            pe([mm(K, Es(j, f), part(n, f, f + 1), False, left[0] == 0 and f == b - 1) for f in range(a, b)])
+        for (a, b, who) in CFG["ZC"]:
+            (sact if who == "S" else vcopy)(part("Zt", a, b), IND(*Zall, R("L1", 64 + 4 * a, 64 + 4 * b)))
+        if YS:
+            sact(part("Dt", 0, YS), IND(*Yall, R("L1", 0, 4 * YS)))
+        for (a, b, who) in CH:
+            vtt(part("Dt", a, b), IND(*Yall, R("L1", 4 * a, 4 * b)), part("Zt", a, b), O.subtract)
+        dS = R("ps0", 0, 64 * YS)
+        if YS:
+            pe([mm(dS, a128("identb"), part("Dt", 0, YS), True, False), mm(dS, a128("identn"), part("Zt", 0, YS), False, True)])
         for (a, b, who) in CH:
             if who == "V":
-                pe([mm(K, Es(2, f), col("Dt", f), False, False) for f in range(a, b)])
-        for (a, b, who) in CH:
-            if who == "S":
-                sact(R("AD", 64 * a, 64 * b), R("Dt", 64 * a, 64 * b), AF.Abs)
+                keys(2, "Dt", a, b)
+        for (a, b, who) in CH[:1] + [(0, YS, "P")] * (YS > 0) + CH[1:]:
+            if who == "V":
+                vts(part("AD", a, b), part("Dt", a, b), 0.0, None, O.max)
             else:
-                vts(R("AD", 64 * a, 64 * b), R("Dt", 64 * a, 64 * b), 0.0, None, O.max)
-            pe([mm(K, Es(0 if who == "S" else 1, f), col("AD", f), False, f == 15) for f in range(a, b)])
+                sact(part("AD", a, b), part("Dt", a, b) if who == "S" else dS, AF.Abs)
+            keys(int(who == "V"), "AD", a, b)
+        sact(a128("DL"), IND("TT", 0, 288, R("FOLD", 0, 8)))
+        if r:
+            sca("tIM", oq, R("NR", 0, 128, 2))
+            sca("tIM", op, R("NR", 1, 128, 2))
         vscan(a64("Fs"), a64("reset"), K, 0.0, O.mult, O.max)
+        if more:
+            vts(R("v5a", 0, 4), R("s6o", 2, 12, 3) if r else R("VL", 0, 4), 5.0, 1.0, O.mult, O.add)
         vtt(a64("ns"), K, a64("Fs"), O.is_lt)
+        if more:
+            vts(R("v5b", 0, 4), R("v5a", 0, 4), 1023, None, O.bitwise_and)
         vscan(R("SC", 64, 128), a64("ns"), R("DL", 64, 128), 0.0, O.mult, O.add)
         vscan(R("SC", 0, 64), a64("ns"), R("DL", 0, 64), 0.0, O.mult, O.add)
         vts(R("LL", 0, 8), ends("SC", 0, 8), 1023.0, None, O.min)
+        if more:
+            vts(R("s6a", 1, 12, 3), fq, 1024.0, None, O.is_ge)
+        if r:
+            sact(R("nth", 0, 16), IND("TH", 0, 576, C("thl")))
         sact(R("rv", 8, 12), ends("Fs", 0, 4), AF.Relu, -VOID, 16.0 * VOID)
         sact(R("rv", 0, 8), ends("SC", 0, 8), AF.Relu, VOID, -1023.0 * VOID)
         vcopy(R("L2", 0, 64), IND("tNZ", 0, 1024, lq))
@@ -372,51 +400,59 @@ def rank_program(g, core, T, topo):
            [mm(vd, a128("identn"), R("rv", 4 * j, 4 * j + 4), False, j == 2) for j in range(3)])
         vscan(R("SC", 128, 256), a128("reset"), a128("mk2"), 0.0, O.mult, O.add)
         vcopy(R("LL", 8, 16), ends("SC", 128, 8))
+        if more:
+            vtt(R("s6b", 0, 12, 3), R("v5b", 0, 4), fw, O.subtract)
         vcopy(R("L2", 128, 192), IND("tNZ", 0, 1024, lp))
         vcopy(R("L2", 192, 256), IND("tNB", 0, 1024, lw))
-        for n, c in (("Bp", 0), ("Bt", 128)):
-            for h in (0, 1):
-                sact(R(n, 512 * h, 512 * h + 512), IND(*Zall, R("L2", c + 32 * h, c + 32 * h + 32)))
-        if AS:
-            sact(R("At", 1024 - 16 * AS, 1024), IND(*Yall, R("L2", 256 - AS, 256)))
-        vcopy(R("At", 0, 512), IND(*Yall, R("L2", 192, 224)))
-        vtt(R("T2", 0, 1024), IND(*Yall, R("L2", 64, 128)), R("Bp", 0, 1024), O.max)
-        if AS < 32:
-            vcopy(R("At", 512, 1024 - 16 * AS), IND(*Yall, R("L2", 224, 256 - AS)))
-        vtt(R("T1", 0, 1024), IND(*Yall, R("L2", 64, 128)), R("Bt", 0, 1024), O.max)
         Gn = R("ps6", 0, 64)
         CS = R("ps7", 0, 128)
-        dif = {}
+        hf = lambda n, h: R(n, 512 * h, 512 * h + 512)
+        lst = lambda j, h: R("L2", 64 * j + 32 * h, 64 * j + 32 * h + 32)
+        bank = {("Bp", 0): "ps0", ("Bp", 1): "ps2", ("Bt", 0): "ps1", ("Bt", 1): "ps5"}
 
-        def diff(bk, src, h):
-            a, b = 512 * h, 512 * h + 512
-            o = R(bk, 0, 512)
-            pe([mm(o, a128("identb"), R(src, a, b), True, False), mm(o, a128("identn"), R("At", a, b), False, True)])
-            dif[src, h] = o
+        def diff(src, h):
+            o = R(bank[src, h], 0, 512)
+            pe([mm(o, a128("identb"), hf(src, h), True, False), mm(o, a128("identn"), hf("At", h), False, True)])
 
         def term(n, l, last=False):
             pe([mm(Gn, a128(l), R(n, k, 1024, 16), False, last and k == 15) for k in range(16)])
+
+        def relu(q, n, src, a, b):
+            i = R(bank[src, a // 512], a % 512, a % 512 + b - a)
+            if q == "V":
+                vts(R(n, a, b), i, 0.0, None, O.max)
+            else:
+                sact(R(n, a, b), i, AF.Relu)
         pe([mm(Gn, a128("identb"), a64("offG"), True, False), mm(Gn, a128("identb"), a64("stepG"), False, False)])
         pe([mm(CS, a128("identb"), a128("offC"), True, False), mm(CS, a128("identb"), a128("thrC"), False, False)])
-        diff("ps0", "Bp", 0)
-        diff("ps1", "Bt", 0)
+        sact(hf("Bp", 0), IND(*Zall, lst(0, 0)))
+        sact(hf("Bp", 1), IND(*Zall, lst(0, 1)))
+        sact(R("At", 1024 - 16 * AS, 1024), IND(*Yall, R("L2", 256 - AS, 256)))
+        vcopy(R("At", 0, 1024 - 16 * AS), IND(*Yall, R("L2", 192, 256 - AS)))
+        sact(hf("Bt", 0), IND(*Zall, lst(2, 0)))
+        sact(hf("Bt", 1), IND(*Zall, lst(2, 1)))
+        vtt(R("T2", 0, 1024), IND(*Yall, R("L2", 64, 128)), R("Bp", 0, 1024), O.max)
+        diff("Bp", 0)
+        diff("Bp", 1)
+        diff("Bt", 0)
         term("T2", "blkm")
-        diff("ps2", "Bp", 1)
-        diff("ps5", "Bt", 1)
+        diff("Bt", 1)
+        relu("V", "R2", "Bp", 0, RV)
+        vtt(hf("T1", 0), IND(*Yall, lst(1, 0)), hf("Bt", 0), O.max)
+        vtt(hf("T1", 1), IND(*Yall, lst(1, 1)), hf("Bt", 1), O.max)
         sact(R("NR", 0, 128, 2), IND(*Iown, lp))
         sact(R("NR", 1, 128, 2), IND(*Iown, lq))
+        if RV < 512:
+            relu("S", "R2", "Bp", RV, 512)
+        relu("S", "R2", "Bp", 512, 1024)
+        relu("S", "R1", "Bt", 0, 512)
+        relu("S", "R1", "Bt", 512, 1024)
         if r:
             sact(ends("E1", 0, 4), vd, AF.Identity, 1.0, C("nth"))
         else:
             sact(ends("E1", 0, 4), vd)
-        for j, (n, src, h) in enumerate((("R2", "Bp", 0), ("R1", "Bt", 0), ("R2", "Bp", 1), ("R1", "Bt", 1))):
-            o = R(n, 512 * h, 512 * h + 512)
-            if j >= 4 - RV:
-                vts(o, dif[src, h], 0.0, None, O.max)
-            else:
-                sact(o, dif[src, h], AF.Relu)
-        term("T1", "blkp")
         term("R2", "blkp")
+        term("T1", "blkp")
         term("R1", "blkm", True)
         sact(a128("zz"), IND(*Zown, R("LL", 4, 12)))
         sact(R("xx", 0, 64), IND("tX", 0, 1024, la))
@@ -444,13 +480,11 @@ def rank_program(g, core, T, topo):
         sact(R("QP", 0, 64), IND(*Mown, lw))
         sact(R("QP", 64, 128), IND(*Mown, la))
         if more:
-            vts(R("v5a", 0, 4), R("s6o", 2, 12, 3) if r else R("VL", 0, 4), 5.0, 1.0, O.mult, O.add)
-            vts(R("s6a", 1, 12, 3), fq, 1024.0, None, O.is_ge)
+            vtt(R("s6b", 1, 12, 3), fw, fa, O.subtract)
+            vcopy(R("s6b", 2, 12, 3), fa)
         vscan(a128("BS"), a128("reset32"), CS, 0.0, O.mult, O.max)
         for c in range(4):
             vts(R("OFF", c, 16, 4), R("NLc", c, 16, 4), C("BS", 32 * c + 31), C("lane4", c), O.subtract, O.max)
-        oa, oq, op, ow = [R("OFF", 4 * n, 4 * n + 4) for n in range(4)]
-        sca = lambda n, off, d: vcopy(IND(n, 0, OWN + 1024, off), d)
         e = r + 1 if more else r
         sca("ZW%d" % e, oq, R("nzv", 0, 64))
         if not more:
@@ -464,26 +498,18 @@ def rank_program(g, core, T, topo):
         sca("ZW%d" % e, op, R("nzv", 64, 128))
         sact(R("SZ", 256 * e, 256 * e + 256), IND("ZW%d" % e, OWN, OWN + 1024, R("BL", 16, 32)))
         sca("YW%d" % e, oa, R("nzv", 0, 64))
-        vts(R("v5b", 0, 4), R("v5a", 0, 4), 1023, None, O.bitwise_and)
-        sca("YW%d" % e, ow, R("nzv", 64, 128))
-        borders(e)
-        vtt(R("s6b", 0, 12, 3), R("v5b", 0, 4), fw, O.subtract)
-        vtt(R("s6b", 1, 12, 3), fw, fa, O.subtract)
-        vcopy(R("s6b", 2, 12, 3), fa)
-        sca("tM", oa, R("QP", 0, 64))
         vscan(R("s6o", 0, 12), R("s6a", 0, 12), R("s6b", 0, 12), 0.0, O.mult, O.add)
-        sca("tM", ow, R("QP", 64, 128))
+        sca("YW%d" % e, ow, R("nzv", 64, 128))
         vcopy(R("vl", 0, 4), R("s6o", 2, 12, 3))
+        borders(e)
         cn = R("ps4", 256, 257)
         pe([mm(cn, a128("onesf"), C("s6a", 3 * c + 2), c == 0, c == 3) for c in range(4)])
-        sca("tIM", oq, R("NR", 0, 128, 2))
-        vtt(a64("mkv"), IND(*Mown, R("vl", 0, 4)), a64("mask"), O.mult)
+        sca("tM", oa, R("QP", 0, 64))
         vcopy(R("nf", 16, 80), IND("tNB", 0, 1024, R("vl", 0, 4)))
-        lane_lists(None)
-        sca("tIM", op, R("NR", 1, 128, 2))
-        vts(C("thi"), cn, -1.0, 512.0, O.mult, O.add)
-        vts(C("thj"), C("thi"), 31, None, O.bitwise_and)
-        vts(C("nth"), C("thj"), -1.0, None, O.mult)
+        sca("tM", ow, R("QP", 64, 128))
+        vts(C("thl"), cn, 31.0, None, O.add)
+        vtt(a64("mkv"), IND(*Mown, R("vl", 0, 4)), a64("mask"), O.mult)
+        lane_lists()
 
     total.update(cnt)
     total["sl"] = nsl[0]

@@ -5,15 +5,16 @@ F4, B2, I4, U2 = "float32", "bfloat16", "int32", "uint16"
 _W = {
     B2: dict(ZW0=1920, ZW1=1920, ZW2=1920, YW0=1920, YW1=1920, YW2=1920, tX=1024, SY=768, SZ=768, Zt=1024, Dt=1024, AD=1024,
              At=1024, Bt=1024, Bp=1024, T1=1024, T2=1024, R1=1024, R2=1024, zz=128, xx=128, cl=128, nzv=128, EQ=640, rv=16,
-             WT=512, identb=128, identn=128, blkp=128, blkm=128, blkH=128, Es=432, brow=64, cst4=4, offG=64, stepG=64,
-             offC=128, thrC=128, selfC=32),
-    F4: dict(IOTA=1024, tM=1152, tIM=1152, mlf=96, mlt=160, pm=2, nf=160, TT=288, TH=576, sub1=128, sub2=128, bidi=128, DL=128, Fs=64, ns=64, SC=256, mk2=128,
-             E1=64, GS=64, BS=128, NR=128, QP=128, NLc=16, s6a=12, s6b=12, s6o=12, VL=4, mkv=64, scv=64, nth=16, onesf=128,
-             itf=128, gf=128, ff=2, gp=2, mask=128, blkf=128, identf=128, reset=128, reset32=128, half=64, wrow=64, wm=64,
-             WL=64, lane4=4, pbase=8, f2=2, ps=2, fv=8, b16=8, foldf=8),
-    I4: dict(tNB=1024, tNZ=1024, ml=128, bl=32, v5a=4, v5b=4, c_p=2, fI=2, gI=2, f3I=2, f2I=2, pa=8, pb=8, fg=2, fg1=2),
+             WT=512, identb=128, identn=128, blkp=128, blkm=128, blkH=128, zeroB=464, brow=64, cst4=4, offG=64, stepG=64,
+             offC=128, thrC=128),
+    F4: dict(IOTA=1024, tM=1152, tIM=1152, zeroF=336, mlt=160, TT=288, TH=576, sub1=128, bidi=128, DL=128, Fs=64, ns=64, SC=256,
+             mk2=128, GS=64, BS=128, NR=128, QP=128, NLc=16, v5=16, identg=128, s6o=12, VL=4, mkv=64, scv=64, nth=16, onesf=128,
+             itf=128, gf=128, ff=2, gp=2, pf=2, up=2, mask=64, blkf=128, identf=128, reset=128, reset32=128, half=64, wrow=64,
+             wm=64, WL=64, lane4=4, pbase=8, fv=8, foldf=8, rows=64, cols=64),
+    I4: dict(tNB=1024, tNZ=1024, ml=128, bl=32, c_p=2, fI=2, gI=2, pa=8, pb=8),
     U2: dict(MF=4, ML=128, BL=32, L1=128, LL=16, L2=256, OFF=16, vl=4, mvl=4, PERM=8, FOLD=8, thl=2),
 }
+PART = dict(mlf=("zeroF", 0), E1=("zeroF", 96), nf=("zeroF", 160), s6a=("zeroF", 320), Es=("zeroB", 0), selfC=("zeroB", 432))
 SCRATCH = {n: ("sbuf", [128, w], d) for d in _W for n, w in _W[d].items()}
 for _i in range(8):
     SCRATCH["ps%d" % _i] = ("psum", [128, 512], F4)
@@ -22,10 +23,11 @@ SEMAPHORES = ["cv", "cs", "cp", "cg", "ld_z", "ld_bx", "ld_bz", "ld_m", "ld_im",
               "st_z", "st_m", "sl"] + ["%s%d_%d" % (w, e, s) for w in "YZ" for e in range(3) for s in range(N)]
 OWN = 128
 STEP, FAR, VOID = 2.0 ** 19, 2.0 ** 23, 2.0 ** 18
+ROUND = 1.5 * 2.0 ** 23
 WTOP, HUGE = 2.0 ** 75, 2.0 ** 80
-CFG = dict(ZC=[(0, 8, "S"), (8, 16, "V")], FUSE=1, ZS=8, YS=5,
-           CH=[(12, 16, "S"), (8, 12, "V"), (5, 8, "V")],
-           ORD=0, AS=32,
+CFG = dict(ZC=[(0, 10, "S"), (10, 16, "V")], SYV=0, ZS=8, YS=4,
+           CH=[(12, 16, "S"), (7, 12, "V"), (4, 7, "V")],
+           HM=[], ODD=0, IMQ=1, KO=[1, -2, 4, -3, 2, 3], ORD=0, XL=32, AV=0, TO=("T1", "R1"), AS=32,
            RV=512)
 
 
@@ -38,13 +40,15 @@ def rank_program(g, core, T, topo):
     cnt = {"cv": 0, "cs": 0, "cp": 0, "cg": 0}
     total = {}
     seen = {q: {} for q in QUEUE}
-    acc = {}
+    acc, past = {}, {}
     CH, AS, RV, ZS, YS = CFG["CH"], CFG["AS"], CFG["RV"], CFG["ZS"], CFG["YS"]
 
     def need(q, sem, val):
         if seen[q].get(sem, 0) < val:
             QUEUE[q].wait_ge(T.sem[sem], val)
             seen[q][sem] = val
+            for s, v in past.get((sem, val), {}).items():
+                seen[q][s] = max(seen[q].get(s, 0), v)
 
     def meet(a, b, s, a2, b2, s2):
         if b2 <= a or b <= a2:
@@ -55,7 +59,7 @@ def rank_program(g, core, T, topo):
         w = {}
         for kind, regs in (("r", reads), ("w", writes)):
             for (n, a, b, s) in regs:
-                ps = n[:2] == "ps" and n != "ps"
+                ps = n[:2] == "ps"
                 for (a2, b2, st2, k2, q2, s2, v2) in acc.get(n, ()):
                     if ps:
                         if q2 == q and (q == "P" or (kind == "r" and k2 == "r")):
@@ -63,7 +67,7 @@ def rank_program(g, core, T, topo):
                     elif (kind == "r" and k2 == "r") or not meet(a, b, s, a2, b2, st2):
                         continue
                     w[s2] = max(w.get(s2, 0), v2)
-        for s, v in w.items():
+        for s, v in sorted(w.items(), key=lambda x: -len(past.get(x, ()))):
             need(q, s, v)
 
     def record(q, reads, writes, sem, val):
@@ -82,16 +86,20 @@ def rank_program(g, core, T, topo):
         s = SEM[q]
         cnt[s] += 1
         last.then_inc(T.sem[s], 1)
+        past[s, cnt[s]] = dict(seen[q])
         record(q, reads, writes, s, cnt[s])
 
     def R(n, a, b, s=1):
+        n, o = PART.get(n, (n, 0))
+        a, b = a + o, b + o
         return (T[n][:, a:b] if s == 1 else T[n][:, a:b:s], [(n, a, b, s)], [])
 
     def C(n, c=0):
         return R(n, c, c + 1)
 
     def IND(n, a, b, off):
-        return (T[n][:, a:b].indirect(off[0]), [(n, a, b, 1)], off[1])
+        w = R(n, a, b)
+        return (w[0].indirect(off[0]), w[1], off[1])
 
     def tup(*xs):
         return [x for x in xs if isinstance(x, tuple)]
@@ -148,40 +156,41 @@ def rank_program(g, core, T, topo):
     a64 = lambda n: R(n, 0, 64)
     ends = lambda n, a, k, s=16: R(n, a + s - 1, a + s * k, s)
 
-    dma("Y", "ld_m", R("ml", 0, 64), T.m[:])
-    dma("S", "ld_bz", R("bl", 16, 32), T.bz[:])
     dma("Y", "ld_z", R("ZW0", OWN, OWN + 1024), T.z[:])
+    dma("S", "ld_bz", R("bl", 16, 32), T.bz[:])
+    dma("Y", "ld_m", R("ml", 0, 64), T.m[:])
     dma("S", "ld_bx", R("bl", 0, 16), T.bx[:])
     dma("Y", "ld_nz", R("tNZ", 0, 1024), T.nz[:])
     dma("Y", "ld_nb", R("tNB", 0, 1024), T.nb[:])
     dma("Y", "ld_im", R("ml", 64, 128), T.im[:])
 
     emit("G", [lambda: g.iota(T.c_p[:, 0:2], [[0, 2]], 0, 1)], [R("c_p", 0, 2)], [])
+    giota(R("IOTA", 0, 128), [[1, 128]], 0, 0)
+    giota(R("rows", 0, 32), [[0, 2], [1, 4], [16, 4]], 0, 0)
+    giota(R("rows", 32, 48), [[1, 4], [32, 2], [96, 2]], 0, 0)
+    giota(R("rows", 48, 64), [[1, 4], [32, 2], [-64, 2]], 80, 0)
     giota(R("pbase", 0, 8), [[64, 2], [4, 4]], 0, 0)
-    giota(a128("itf"), [[0, 8], [1, 16]], 0, 0)
     giota(a128("gf"), [[1, 8], [0, 16]], 0, 0)
-    giota(a64("brow"), [[0, 4], [-1, 16]], 15, 0)
-    giota(R("IOTA", 0, 512), [[1, 512]], 0, 0)
-    vset(R("mlf", 0, 96), 0.0)
-    vset(a64("E1"), 0.0)
+    giota(a128("itf"), [[0, 8], [1, 16]], 0, 0)
+    vset(R("zeroF", 0, 336), 0.0)
     vts(R("fI", 0, 2), R("c_p", 0, 2), 15, None, O.bitwise_and)
     vts(R("gI", 0, 2), R("c_p", 0, 2), 4, None, O.arith_shift_right)
-    vset(a64("half"), 0.5)
-    vts(R("f3I", 0, 2), R("fI", 0, 2), 3, None, O.bitwise_and)
-    vts(R("f2I", 0, 2), R("fI", 0, 2), 2, None, O.arith_shift_right)
-    vtt(R("fg", 0, 2), R("fI", 0, 2), R("gI", 0, 2), O.add)
+    vcopy(R("pf", 0, 2), R("c_p", 0, 2))
     vcopy(R("ff", 0, 2), R("fI", 0, 2))
-    vcopy(R("f2", 0, 2), R("f2I", 0, 2))
-    vts(R("fg1", 0, 2), R("fg", 0, 2), 1, None, O.bitwise_and)
-    vts(R("ps", 0, 2), R("f3I", 0, 2), 16.0, C("f2"), O.mult, O.add)
     vcopy(R("gp", 0, 2), R("gI", 0, 2))
-    vts(R("pm", 0, 2), R("fg1", 0, 2), 80.0, C("ps"), O.mult, O.add)
-    vts(a128("mask"), a128("itf"), C("ff"), None, O.is_equal)
-    vts(R("MF", 0, 4), R("pbase", 0, 4), C("pm"), None, O.add)
-    vts(a128("reset"), a128("itf"), 0.0, None, O.is_gt)
-    vts(a128("blkf"), a128("gf"), C("gp"), None, O.is_equal)
-    vts(R("PERM", 0, 8), R("pbase", 0, 8), C("ps"), None, O.add)
+    vts(a128("identf"), R("IOTA", 0, 128), C("pf"), None, O.is_equal)
+    vts(R("up", 0, 2), R("ff", 0, 2), 0.0, C("pf"), O.is_gt, O.mult)
+    vtr(a64("cols"), a64("rows"))
+    vts(a128("sub1"), R("IOTA", 0, 128), 1.0, C("up"), O.add, O.is_equal)
+    vts(R("MF", 0, 4), R("pbase", 0, 4), C("cols", 32), None, O.add)
+    vts(R("PERM", 0, 8), R("pbase", 0, 8), C("cols", 0), None, O.add)
+    vset(R("zeroB", 0, 464), 0.0)
     vcopy(R("BL", 16, 32), R("bl", 16, 32))
+    vts(a128("blkf"), a128("gf"), C("gp"), None, O.is_equal)
+    for k in (128, 256, 512):
+        sact(R("IOTA", k, 2 * k), R("IOTA", 0, k), AF.Identity, 1.0, float(k))
+    sact(a128("identb"), a128("identf"))
+    sact(a128("identn"), a128("identf"), AF.Copy, -1.0)
 
     def near(c):
         return topo.cores_of(c)
@@ -207,11 +216,12 @@ def rank_program(g, core, T, topo):
         rel = []
         for t in ds:
             twin = [u for u in ds if u != t and u in near(t)]
-            if t not in near(s) and twin and topo.die(t) != topo.die(s):
+            if twin and topo.die(t) != topo.die(s) and not any(u in near(s) for u in ds):
                 rel.append((twin[0], t))
         direct = [t for t in ds if t not in [x[1] for x in rel]]
         return sorted(direct, key=lambda t: t not in [x[0] for x in rel]), rel
     plans = {s: plan(s) for s in T.cores}
+    late = [t for s in T.cores for (u, t) in plans[s][1]]
     duty = [(s, t) for s in T.cores for (u, t) in plans[s][1] if u == core]
     nsl = [0]
 
@@ -220,115 +230,120 @@ def rank_program(g, core, T, topo):
         return OWN + 1024 + 256 * (d - 1), OWN + 1280 + 256 * (d - 1)
 
     def calls(s, e):
-        lead, other = plans[s][0]
-        ml_, mo_ = wmask(s, lead), wmask(s, other)
-        if ml_ & mo_ == 0:
-            return [[(w, lead, ml_), (w, other, mo_)] for w in "ZY"]
-        if e == 0:
-            return [[(w, t, wmask(s, t))] for w in "ZY" for t in (lead, other)]
-        if CFG["FUSE"]:
-            return [[(w, lead, ml_)] for w in "ZY"] + [[(w, other, m) for w, m in zip("ZY", halves(mo_))]]
-        return [[(w, t, wmask(s, t))] for t in (lead, other) for w in "ZY"]
+        if plans[s][1]:
+            return [[(w, [t], wmask(s, t))] for t in plans[s][0] for w in "ZY"]
+        far = sorted([t for t in plans[s][0] if t not in near(s)], key=lambda t: t in late)
+        by = [t for t in plans[s][0] if t in near(s)]
+        if CFG["ODD"] == 2:
+            return [[(w, ts, wmask(s, far[0]))] for ts in (far[:1] + by, far[1:]) for w in "ZY"]
+        if CFG["ODD"] == 3:
+            z, y = [[(w, [t], wmask(s, t)) for t in far[:1] + by + far[1:]] for w in "ZY"]
+            h = halves(z[1][2])
+            return [z[:2], y[:2], z[2:], y[2:]] if e else [z[:1], y[:1], z[2:], y[2:], [z[1][:2] + h[:1], y[1][:2] + h[1:]]]
+        if CFG["ODD"]:
+            z, y = [[(w, [t], wmask(s, t)) for t in far[:1] + by + far[1:]] for w in "ZY"]
+            return ([z[:2]] if e else [z[:1], z[1:2]]) + [y[:2], z[2:], y[2:]]
+        z, y = [[(w, ts, wmask(s, ts[0])) for ts in (far, by)] for w in "ZY"]
+        return [z, y] if e else [z[:1], z[1:], y]
+
+    def hmask(u, t, s, w, e):
+        return topo.mask(u, s) if (w, e) in CFG["HM"] else wmask(u, t)
 
     def put(items):
         ts = []
-        for (s, w, e, src, dst, m) in items:
+        for (s, w, e, src, dsts, m) in items:
             order("G", src[1], [])
-            rid, pid = topo.addr(dst, core)
-            a, b = block(s, dst)
-            ts.append(RemoteDMATransfer(dst_ids=[DstId(rid=rid, pnc=pid)], dma_engine_mask=m, src=src[0],
-                                        remote_sem=T.sem["%s%d_%d" % (w, e, T.rank_of(s))], dst=T["%sW%d" % (w, e)][:, a:b]))
+            ids = [DstId(rid=topo.addr(d, core)[0], pnc=topo.addr(d, core)[1]) for d in dsts]
+            ts.append(RemoteDMATransfer(dst_ids=ids, dma_engine_mask=m, srcs=[src[0]],
+                                        dsts=[R("%sW%d" % (w, e), *block(s, d))[0] for d in dsts],
+                                        remote_sem=T.sem["%s%d_%d" % (w, e, T.rank_of(s))]))
             nsl[0] += ones(m)
         g.remote_dma_fused(ts, local_sem=T.sem.sl)
 
     def borders(e):
-        vcopy(R("SY", 256 * e, 256 * e + 128), IND("YW%d" % e, OWN, OWN + 1024, R("BL", 0, 8)))
-        sact(R("SY", 256 * e + 128, 256 * e + 256), IND("YW%d" % e, OWN, OWN + 1024, R("BL", 8, 16)))
+        k = CFG["SYV"] if e else 8
+        if k:
+            vcopy(R("SY", 256 * e, 256 * e + 16 * k), IND("YW%d" % e, OWN, OWN + 1024, R("BL", 0, k)))
+        sact(R("SY", 256 * e + 16 * k, 256 * e + 256), IND("YW%d" % e, OWN, OWN + 1024, R("BL", k, 16)))
         for c in calls(core, e):
             put([(core, w, e, R("S" + w, 256 * e, 256 * e + 256), t, m) for (w, t, m) in c])
         for w in "ZY":
             win = "%sW%d" % (w, e)
             for s in T.cores:
-                come = [m for c in calls(s, e) for (w2, t, m) in c if (w2, t) == (w, core)]
-                come += [wmask(u, t) for (u, t) in plans[s][1] if t == core]
+                come = [m for c in calls(s, e) for (w2, ts, m) in c if w2 == w and core in ts]
+                come += [hmask(u, t, s, w, e) for (u, t) in plans[s][1] if t == core]
                 for m in come:
                     sem = "%s%d_%d" % (w, e, T.rank_of(s))
                     total[sem] = ones(m)
                     record("A" + sem, [], [(win,) + block(s, core) + (1,)], sem, ones(m))
             for (s, t) in duty:
-                put([(s, w, e, R(win, *block(s, core)), t, wmask(core, t))])
-
-    def arrived(q, e):
-        for s, v in list(total.items()):
-            if s[:3] in ("Y%d_" % e, "Z%d_" % e):
-                need(q, s, v)
+                put([(s, w, e, R(win, *block(s, core)), [t], hmask(core, t, s, w, e))])
 
     def mlist(a):
         vcopy(R("mlf", 16, 80), R("ml", a, a + 64))
         vtr(R("mlt", 0, 64), R("mlf", 16, 80))
         vtr(R("mlt", 64, 160), R("mlf", 0, 96))
         vcopy(R("ML", a, a + 64), IND("mlt", 0, 160, R("MF", 0, 4)))
-    mlist(0)
     vcopy(R("SZ", 0, 128), IND("ZW0", OWN, OWN + 1024, R("BL", 16, 24)))
     sact(R("SZ", 128, 256), IND("ZW0", OWN, OWN + 1024, R("BL", 24, 32)))
+    for j, k in enumerate((16.0, 32.0, -16.0)):
+        sact(R("Es", 144 * j + 15, 144 * j + 143, 16), R("blkf", 0, 128, 16), AF.Copy, k)
+    sact(a64("brow"), a64("itf"), AF.Identity, -1.0, 15.0)
+    mlist(0)
     vcopy(R("BL", 0, 16), R("bl", 0, 16))
     vcopy(R("YW0", OWN, OWN + 512), IND("ZW0", OWN, OWN + 1024, R("ML", 0, 32)))
     sact(R("YW0", OWN + 512, OWN + 1024), IND("ZW0", OWN, OWN + 1024, R("ML", 32, 64)))
     borders(0)
 
     giota(R("TH", 0, 576), [[0, 18], [1, 32]], -31, 0)
-    sact(R("IOTA", 512, 1024), R("IOTA", 0, 512), AF.Identity, 1.0, 512.0)
     sact(R("tM", OWN, OWN + 1024), IND("IOTA", 0, 1024, R("ML", 0, 64)))
-    vset(R("Es", 0, 432), 0.0)
-    vscan(a64("wrow"), a64("half"), a64("E1"), 2.0 * WTOP, O.mult, O.add)
-    vset(R("nf", 0, 160), 0.0)
+    vset(a64("half"), 0.5)
+    vts(a64("mask"), a64("itf"), C("ff"), None, O.is_equal)
+    vts(a128("reset"), a128("itf"), 0.0, None, O.is_gt)
     vts(R("pa", 0, 8), R("gf", 0, 128, 16), C("gp"), None, O.add)
+    vscan(a64("wrow"), a64("half"), a64("E1"), 2.0 * WTOP, O.mult, O.add)
     vts(R("pb", 0, 8), R("pa", 0, 8), 1, None, O.bitwise_and)
-    vts(R("b16", 0, 8), R("gf", 0, 128, 16), 16.0, None, O.mult)
-    vtt(a128("identf"), a128("blkf"), a128("mask"), O.mult)
+    vtt(a128("bidi"), a128("identf"), a128("sub1"), O.subtract)
     vts(R("fv", 0, 8), R("pb", 0, 8), 144.0, C("ff"), O.mult, O.add)
-    vts(a128("sub1"), a128("itf"), 1.0, C("ff"), O.add, O.is_equal)
     vtt(a64("wm"), a64("wrow"), a64("mask"), O.mult)
-    vtt(R("foldf", 0, 8), R("fv", 0, 8), R("b16", 0, 8), O.add)
-    vtt(a128("sub2"), a128("mask"), a128("sub1"), O.subtract)
-    vcopy(R("FOLD", 0, 8), R("foldf", 0, 8))
-    vtt(a128("bidi"), a128("sub2"), a128("blkf"), O.mult)
-    vts(R("lane4", 0, 4), R("gf", 0, 64, 16), 16.0, C("ff"), O.mult, O.add)
-    vscan(a64("WL"), a64("reset"), a64("wm"), 0.0, O.mult, O.add)
-    vset(a128("reset32"), 1.0)
-    vset(a128("onesf"), 1.0)
-    vset(R("selfC", 0, 32), 0.0)
-    vset(R("s6a", 0, 12), 0.0)
-    vset(R("reset32", 0, 128, 32), 0.0)
-    vts(R("VL", 0, 4), R("lane4", 0, 4), 16.0, None, O.mult)
+    vtt(R("foldf", 0, 8), R("fv", 0, 8), R("IOTA", 0, 128, 16), O.add)
     mlist(64)
 
-    def lane_lists():
+    def lane_lists(nbv):
+        vcopy(R("nf", 16, 80), nbv)
         vscan(a64("scv"), a64("reset"), a64("mkv"), 0.0, O.mult, O.add)
         vcopy(R("mvl", 0, 4), ends("scv", 0, 4))
         vcopy(R("nf", 80, 144), IND("tNZ", 0, 1024, R("mvl", 0, 4)))
         pe([mm(R("ps5", 0, 160), a128("bidi"), R("nf", 0, 160), True, True)])
         vcopy(a128("L1"), IND("nf", 16, 144, R("PERM", 0, 8)))
+        if nbv[2] and CFG["IMQ"]:
+            vcopy(IND("tIM", 0, OWN + 1024, R("OFF", 4, 8)), R("NR", 0, 128, 2))
         vtr(R("TT", 0, 128), R("ps5", 16, 144))
         vtr(R("TT", 128, 288), R("ps5", 0, 160))
-    vcopy(R("nf", 16, 80), R("tNB", 0, 1024, 16))
+    vcopy(R("FOLD", 0, 8), R("foldf", 0, 8))
     vtt(a64("mkv"), R("tM", OWN, OWN + 1024, 16), a64("mask"), O.mult)
-    sact(a128("identb"), a128("identf"))
-    for j, k in enumerate((16.0, 32.0, -16.0)):
-        sact(R("Es", 144 * j + 15, 144 * j + 143, 16), R("blkf", 0, 128, 16), AF.Copy, k)
-    lane_lists()
+    lane_lists(R("tNB", 0, 1024, 16))
     sact(R("tIM", OWN, OWN + 1024), IND("IOTA", 0, 1024, R("ML", 64, 128)))
-    sact(a128("identn"), a128("identf"), AF.Copy, -1.0)
-    sact(a128("blkp"), a128("blkf"), AF.Copy, 2.0)
-    sact(a128("blkm"), a128("blkf"), AF.Copy, -2.0)
+
+    vts(R("lane4", 0, 4), R("gf", 0, 64, 16), 16.0, C("ff"), O.mult, O.add)
+    vts(a128("blkp"), a128("blkf"), 2.0, None, O.mult)
+    vts(R("VL", 0, 4), R("lane4", 0, 4), 16.0, None, O.mult)
+
+    def late_constants():
+        vscan(a64("WL"), a64("reset"), a64("wm"), 0.0, O.mult, O.add)
+        vts(a128("blkm"), a128("blkf"), -2.0, None, O.mult)
+        sact(R("cst4", 0, 4), R("gf", 0, 64, 16), AF.Copy, -STEP)
+        sact(a64("stepG"), a64("gf"), AF.Copy, STEP)
+        sact(a64("offG"), a64("mask"), AF.Identity, FAR, -FAR)
+        for n, k in enumerate((0.5, -2.5)):
+            sact(R("offC", n, 128, 2), a64("mask"), AF.Identity, HUGE, -HUGE)
+            sact(R("thrC", n, 128, 2), a64("wm"), AF.Copy, k)
+
+    def last_constants():
+        sact(a128("reset32"), a128("TH"), AF.Sign, 1.0, 31.0)
     sact(a128("blkH"), a128("blkf"), AF.Identity, -FAR, FAR)
-    sact(R("cst4", 0, 4), R("gf", 0, 64, 16), AF.Copy, -STEP)
-    sact(a64("stepG"), a64("gf"), AF.Copy, STEP)
-    sact(a64("offG"), a64("mask"), AF.Identity, FAR, -FAR)
-    for n, k in enumerate((0.5, -2.5)):
-        sact(R("offC", n, 128, 2), a64("mask"), AF.Identity, HUGE, -HUGE)
-        sact(R("thrC", n, 128, 2), a64("wm"), AF.Copy, k)
     sact(R("selfC", 0, 32, 2), R("mask", 0, 16), AF.Copy, -3.0)
+    sact(a128("identg"), a128("identf"), AF.Copy, -1.0)
 
     la, lq, lp, lw = [R("LL", 4 * n, 4 * n + 4) for n in range(4)]
     fa, fq, fp, fw = [ends("SC", 64 * n, 4) for n in range(4)]
@@ -339,12 +354,6 @@ def rank_program(g, core, T, topo):
         Zn, Yn = "ZW%d" % r, "YW%d" % r
         Zall, Yall, Zown = (Zn, OWN, OWN + 1792), (Yn, OWN, OWN + 1792), (Zn, OWN, OWN + 1024)
         Mown, Iown = ("tM", OWN, OWN + 1024), ("tIM", OWN, OWN + 1024)
-        if more:
-            arrived("Y", r)
-            if r == 0:
-                dma("Y", "ld_x", R("tX", 0, 1024), T.x[:])
-            for w in "ZY":
-                dma("Y", "cp_%s%d" % (w, r), R("%sW%d" % (w, r + 1), OWN, OWN + 1024), R("%sW%d" % (w, r), OWN, OWN + 1024))
         K = R("ps3", 0, 64)
         pe([mm(K, a128("identb"), a64("brow"), True, False)])
         part = lambda n, a, b: R(n, 64 * a, 64 * b)
@@ -363,10 +372,12 @@ def rank_program(g, core, T, topo):
         dS = R("ps0", 0, 64 * YS)
         if YS:
             pe([mm(dS, a128("identb"), part("Dt", 0, YS), True, False), mm(dS, a128("identn"), part("Zt", 0, YS), False, True)])
-        for (a, b, who) in CH:
-            if who == "V":
+        parts = CH + [(0, YS, "P")]
+        for i in CFG["KO"]:
+            a, b, who = parts[abs(i) - 1]
+            if i < 0:
                 keys(2, "Dt", a, b)
-        for (a, b, who) in CH[:1] + [(0, YS, "P")] * (YS > 0) + CH[1:]:
+                continue
             if who == "V":
                 vts(part("AD", a, b), part("Dt", a, b), 0.0, None, O.max)
             else:
@@ -374,36 +385,44 @@ def rank_program(g, core, T, topo):
             keys(int(who == "V"), "AD", a, b)
         sact(a128("DL"), IND("TT", 0, 288, R("FOLD", 0, 8)))
         if r:
-            sca("tIM", oq, R("NR", 0, 128, 2))
+            if not CFG["IMQ"]:
+                sca("tIM", oq, R("NR", 0, 128, 2))
             sca("tIM", op, R("NR", 1, 128, 2))
+        else:
+            late_constants()
         vscan(a64("Fs"), a64("reset"), K, 0.0, O.mult, O.max)
         if more:
-            vts(R("v5a", 0, 4), R("s6o", 2, 12, 3) if r else R("VL", 0, 4), 5.0, 1.0, O.mult, O.add)
+            need("Y", "cv", cnt["cv"])
+            if r == 0:
+                dma("Y", "ld_x", R("tX", 0, 1024), T.x[:])
+            for w in "ZY":
+                dma("Y", "cp_%s%d" % (w, r), R("%sW%d" % (w, r + 1), OWN, OWN + 1024), R("%sW%d" % (w, r), OWN, OWN + 1024))
         vtt(a64("ns"), K, a64("Fs"), O.is_lt)
-        if more:
-            vts(R("v5b", 0, 4), R("v5a", 0, 4), 1023, None, O.bitwise_and)
         vscan(R("SC", 64, 128), a64("ns"), R("DL", 64, 128), 0.0, O.mult, O.add)
         vscan(R("SC", 0, 64), a64("ns"), R("DL", 0, 64), 0.0, O.mult, O.add)
-        vts(R("LL", 0, 8), ends("SC", 0, 8), 1023.0, None, O.min)
-        if more:
-            vts(R("s6a", 1, 12, 3), fq, 1024.0, None, O.is_ge)
+        vts(lq, fq, 1023.0, None, O.min)
+        vts(la, fa, 1023.0, None, O.min)
         if r:
             sact(R("nth", 0, 16), IND("TH", 0, 576, C("thl")))
+        if more:
+            v = R("s6o", 2, 12, 3) if r else R("VL", 0, 4)
+            sact(R("v5", 0, 4), v, AF.Identity, 5.0, 1.0)
+            sact(R("v5", 4, 8), v, AF.Identity, 5.0, -510.5)
+            sact(R("v5", 8, 12), R("v5", 4, 8), AF.Identity, 1.0 / 1024, ROUND)
+            sact(R("v5", 12, 16), R("v5", 8, 12), AF.Identity, -1024.0, 1024.0 * ROUND)
         sact(R("rv", 8, 12), ends("Fs", 0, 4), AF.Relu, -VOID, 16.0 * VOID)
         sact(R("rv", 0, 8), ends("SC", 0, 8), AF.Relu, VOID, -1023.0 * VOID)
         vcopy(R("L2", 0, 64), IND("tNZ", 0, 1024, lq))
-        vcopy(R("L2", 64, 128), IND("tNB", 0, 1024, la))
-        vtt(R("mk2", 0, 64), IND(*Mown, la), a64("mask"), O.mult)
         vtt(R("mk2", 64, 128), IND(*Iown, lq), a64("mask"), O.mult)
+        vtt(R("mk2", 0, 64), IND(*Mown, la), a64("mask"), O.mult)
+        vcopy(R("L2", 64, 128), IND("tNB", 0, 1024, la))
         vd = R("ps4", 0, 4)
         pe([mm(vd, a128("identb"), R("cst4", 0, 4), True, False)] +
            [mm(vd, a128("identn"), R("rv", 4 * j, 4 * j + 4), False, j == 2) for j in range(3)])
         vscan(R("SC", 128, 256), a128("reset"), a128("mk2"), 0.0, O.mult, O.add)
         vcopy(R("LL", 8, 16), ends("SC", 128, 8))
-        if more:
-            vtt(R("s6b", 0, 12, 3), R("v5b", 0, 4), fw, O.subtract)
-        vcopy(R("L2", 128, 192), IND("tNZ", 0, 1024, lp))
         vcopy(R("L2", 192, 256), IND("tNB", 0, 1024, lw))
+        vcopy(R("L2", 128, 192), IND("tNZ", 0, 1024, lp))
         Gn = R("ps6", 0, 64)
         CS = R("ps7", 0, 128)
         hf = lambda n, h: R(n, 512 * h, 512 * h + 512)
@@ -425,38 +444,74 @@ def rank_program(g, core, T, topo):
                 sact(R(n, a, b), i, AF.Relu)
         pe([mm(Gn, a128("identb"), a64("offG"), True, False), mm(Gn, a128("identb"), a64("stepG"), False, False)])
         pe([mm(CS, a128("identb"), a128("offC"), True, False), mm(CS, a128("identb"), a128("thrC"), False, False)])
-        sact(hf("Bp", 0), IND(*Zall, lst(0, 0)))
-        sact(hf("Bp", 1), IND(*Zall, lst(0, 1)))
-        sact(R("At", 1024 - 16 * AS, 1024), IND(*Yall, R("L2", 256 - AS, 256)))
-        vcopy(R("At", 0, 1024 - 16 * AS), IND(*Yall, R("L2", 192, 256 - AS)))
-        sact(hf("Bt", 0), IND(*Zall, lst(2, 0)))
-        sact(hf("Bt", 1), IND(*Zall, lst(2, 1)))
-        vtt(R("T2", 0, 1024), IND(*Yall, R("L2", 64, 128)), R("Bp", 0, 1024), O.max)
-        diff("Bp", 0)
-        diff("Bp", 1)
-        diff("Bt", 0)
-        term("T2", "blkm")
-        diff("Bt", 1)
-        relu("V", "R2", "Bp", 0, RV)
-        vtt(hf("T1", 0), IND(*Yall, lst(1, 0)), hf("Bt", 0), O.max)
-        vtt(hf("T1", 1), IND(*Yall, lst(1, 1)), hf("Bt", 1), O.max)
-        sact(R("NR", 0, 128, 2), IND(*Iown, lp))
-        sact(R("NR", 1, 128, 2), IND(*Iown, lq))
-        if RV < 512:
-            relu("S", "R2", "Bp", RV, 512)
-        relu("S", "R2", "Bp", 512, 1024)
-        relu("S", "R1", "Bt", 0, 512)
-        relu("S", "R1", "Bt", 512, 1024)
-        if r:
-            sact(ends("E1", 0, 4), vd, AF.Identity, 1.0, C("nth"))
+        def e1():
+            if r:
+                sact(ends("E1", 0, 4), vd, AF.Identity, 1.0, C("nth"))
+            else:
+                sact(ends("E1", 0, 4), vd)
+        if CFG["ORD"] == 0:
+            sact(hf("Bp", 0), IND(*Zall, lst(0, 0)))
+            sact(hf("Bp", 1), IND(*Zall, lst(0, 1)))
+            sact(R("At", 1024 - 16 * AS, 1024), IND(*Yall, R("L2", 256 - AS, 256)))
+            vcopy(R("At", 0, 1024 - 16 * AS), IND(*Yall, R("L2", 192, 256 - AS)))
+            sact(hf("Bt", 0), IND(*Zall, lst(2, 0)))
+            sact(hf("Bt", 1), IND(*Zall, lst(2, 1)))
+            vtt(R("T2", 0, 1024), IND(*Yall, R("L2", 64, 128)), R("Bp", 0, 1024), O.max)
+            diff("Bp", 0)
+            diff("Bp", 1)
+            diff("Bt", 0)
+            term("T2", "blkm")
+            diff("Bt", 1)
+            relu("V", "R2", "Bp", 0, RV)
+            vtt(hf("T1", 0), IND(*Yall, lst(1, 0)), hf("Bt", 0), O.max)
+            vtt(hf("T1", 1), IND(*Yall, lst(1, 1)), hf("Bt", 1), O.max)
+            sact(R("NR", 0, 128, 2), IND(*Iown, lp))
+            sact(R("NR", 1, 128, 2), IND(*Iown, lq))
+            if RV < 512:
+                relu("S", "R2", "Bp", RV, 512)
+            relu("S", "R2", "Bp", 512, 1024)
+            relu("S", "R1", "Bt", 0, 512)
+            relu("S", "R1", "Bt", 512, 1024)
+            e1()
+            term("R2", "blkp")
+            term("T1", "blkp")
+            term("R1", "blkm", True)
         else:
-            sact(ends("E1", 0, 4), vd)
-        term("R2", "blkp")
-        term("T1", "blkp")
-        term("R1", "blkm", True)
+            cols = lambda n, a, b: R(n, 16 * a, 16 * b)
+            names = lambda j, a, b: R("L2", 64 * j + a, 64 * j + b)
+            held = {}
+            for st in CFG["SEQ"]:
+                k, n = st[0], st[1]
+                if k in "SV" and n in ("Bp", "Bt", "At"):
+                    a, b = st[2:]
+                    i = IND(*(Yall if n == "At" else Zall), names({"Bp": 0, "Bt": 2, "At": 3}[n], a, b))
+                    (sact if k == "S" else vcopy)(cols(n, a, b), i)
+                elif n in ("T1", "T2") and k == "V":
+                    a, b = st[2:]
+                    vtt(cols(n, a, b), IND(*Yall, names(1, a, b)), cols("Bt" if n == "T1" else "Bp", a, b), O.max)
+                elif k == "D":
+                    a, b, bk = st[2:]
+                    held[n, a] = o = R("ps%d" % bk, 0, 16 * (b - a))
+                    pe([mm(o, a128("identb"), cols(n, a, b), True, False), mm(o, a128("identn"), cols("At", a, b), False, True)])
+                elif k == "P":
+                    term(n, "blkp" if n in ("T1", "R2") else "blkm", st == CFG["SEQ"][-1])
+                elif n == "NR":
+                    sact(R("NR", 0, 128, 2), IND(*Iown, lp))
+                    sact(R("NR", 1, 128, 2), IND(*Iown, lq))
+                elif n == "E1":
+                    e1()
+                else:
+                    a, b = st[2:]
+                    i = held["Bt" if n == "R1" else "Bp", a]
+                    if k == "V":
+                        vts(cols(n, a, b), i, 0.0, None, O.max)
+                    else:
+                        sact(cols(n, a, b), i, AF.Relu)
         sact(a128("zz"), IND(*Zown, R("LL", 4, 12)))
         sact(R("xx", 0, 64), IND("tX", 0, 1024, la))
         sact(R("xx", 64, 128), IND("tX", 0, 1024, lw))
+        if r == 0:
+            last_constants()
         eqs, at = [], 0
         for c in range(4):
             for k in (16 * c + 15, 192 + 16 * c + 15):
@@ -464,7 +519,7 @@ def rank_program(g, core, T, topo):
                 vts(R("EQ", at, at + w), R("NR", 32 * c, 128), C("SC", k), None, O.is_equal)
                 eqs.append((c, at, w))
                 at += w
-        vts(R("NLc", 0, 16), ends("SC", 0, 16), float(OWN), None, O.add)
+        sact(R("NLc", 0, 16), ends("SC", 0, 16), AF.Identity, 1.0, float(OWN))
         vscan(a64("GS"), Gn, a64("E1"), -4.0 * FAR, O.max, O.add)
         xz = R("ps4", 128, 256)
         pe([mm(xz, a128("identb"), a128("xx"), True, False), mm(xz, a128("identn"), a128("zz"), False, True)])
@@ -479,9 +534,13 @@ def rank_program(g, core, T, topo):
         sact(a128("nzv"), nzp)
         sact(R("QP", 0, 64), IND(*Mown, lw))
         sact(R("QP", 64, 128), IND(*Mown, la))
+        if r == 0:
+            sact(a128("onesf"), a128("blkf"), AF.Identity, 0.0, 1.0)
         if more:
-            vtt(R("s6b", 1, 12, 3), fw, fa, O.subtract)
-            vcopy(R("s6b", 2, 12, 3), fa)
+            sact(R("s6a", 1, 12, 3), R("rv", 4, 8), AF.Sign)
+            for j, ts in enumerate(((("identf", R("v5", 0, 4)), ("identf", R("v5", 12, 16)), ("identg", fw)),
+                                    (("identf", fw), ("identg", fa)), (("identf", fa),))):
+                pe([mm(R("ps0", j, 12, 3), a128(l), x, i == 0, i == len(ts) - 1) for i, (l, x) in enumerate(ts)])
         vscan(a128("BS"), a128("reset32"), CS, 0.0, O.mult, O.max)
         for c in range(4):
             vts(R("OFF", c, 16, 4), R("NLc", c, 16, 4), C("BS", 32 * c + 31), C("lane4", c), O.subtract, O.max)
@@ -498,18 +557,17 @@ def rank_program(g, core, T, topo):
         sca("ZW%d" % e, op, R("nzv", 64, 128))
         sact(R("SZ", 256 * e, 256 * e + 256), IND("ZW%d" % e, OWN, OWN + 1024, R("BL", 16, 32)))
         sca("YW%d" % e, oa, R("nzv", 0, 64))
-        vscan(R("s6o", 0, 12), R("s6a", 0, 12), R("s6b", 0, 12), 0.0, O.mult, O.add)
+        vscan(R("s6o", 0, 12), R("s6a", 0, 12), R("ps0", 0, 12), 0.0, O.mult, O.add)
         sca("YW%d" % e, ow, R("nzv", 64, 128))
-        vcopy(R("vl", 0, 4), R("s6o", 2, 12, 3))
         borders(e)
         cn = R("ps4", 256, 257)
         pe([mm(cn, a128("onesf"), C("s6a", 3 * c + 2), c == 0, c == 3) for c in range(4)])
         sca("tM", oa, R("QP", 0, 64))
-        vcopy(R("nf", 16, 80), IND("tNB", 0, 1024, R("vl", 0, 4)))
+        vcopy(R("vl", 0, 4), R("s6o", 2, 12, 3))
         sca("tM", ow, R("QP", 64, 128))
         vts(C("thl"), cn, 31.0, None, O.add)
         vtt(a64("mkv"), IND(*Mown, R("vl", 0, 4)), a64("mask"), O.mult)
-        lane_lists()
+        lane_lists(IND("tNB", 0, 1024, R("vl", 0, 4)))
 
     total.update(cnt)
     total["sl"] = nsl[0]

from concourse.bass import DstId, RemoteDMATransfer
from concourse.mybir import AluOpType as O, ActivationFunctionType as AF

F4, B2, I4, U2 = "float32", "bfloat16", "int32", "uint16"
_W = {
    B2: dict(ZW0=1920, ZW1=1920, ZW2=1920, YW0=1920, YW1=1920, YW2=1920, tX=1024, SY=768, SZ=768, Zt=1024, Dt=1024, AD=1024,
             At=1024, Bt=1024, Bp=1024, T1=1024, T2=1024, R1=1024, R2=1024, zz=128, xx=128, cl=128, nzv=128, EQ=640, rv=16,
             WT=512, identb=128, identn=128, blkp=128, blkm=128, blkH=128, zeroB=464, brow=64, cst4=4, offG=64, stepG=64,
             offC=128, thrC=128),
    F4: dict(IOTA=1024, tM=1152, tIM=1152, zeroF=336, mlt=160, TT=288, TH=576, sub1=128, bidi=128, DL=128, Fs=64, ns=64, SC=256,
             mk2=128, GS=64, BS=128, NR=128, QP=128, NLc=16, v5=16, identg=128, s6o=12, VL=4, mkv=64, scv=64, nth=16, onesf=128,
             itf=128, gf=128, ff=2, gp=2, pf=2, up=2, mask=64, blkf=128, identf=128, reset=128, reset32=128, half=64, wrow=64,
             wm=64, WL=64, lane4=4, pbase=8, fv=8, foldf=8, rows=64, cols=64),
    I4: dict(tNB=1024, tNZ=1024, ml=128, bl=32, c_p=2, fI=2, gI=2, pa=8, pb=8),
    U2: dict(MF=4, ML=128, BL=32, L1=128, LL=16, L2=256, OFF=16, vl=4, mvl=4, PERM=8, FOLD=8, thl=2),
}
PART = dict(mlf=("zeroF", 0), E1=("zeroF", 96), nf=("zeroF", 160), s6a=("zeroF", 320), Es=("zeroB", 0), selfC=("zeroB", 432))
SCRATCH = {n: ("sbuf", [128, w], d) for d in _W for n, w in _W[d].items()}
for _i in range(8):
    SCRATCH["ps%d" % _i] = ("psum", [128, 512], F4)
N = 8
SEMAPHORES = ["cv", "cs", "cp", "cg", "ld_z", "ld_bx", "ld_bz", "ld_m", "ld_im", "ld_nz", "ld_nb", "ld_x", "cp_Z0", "cp_Z1", "cp_Y0", "cp_Y1",
              "st_z", "st_m", "sl"] + ["%s%d_%d" % (w, e, s) for w in "YZ" for e in range(3) for s in range(N)]
OWN = 128
STEP, FAR, VOID = 2.0 ** 19, 2.0 ** 23, 2.0 ** 18
ROUND = 1.5 * 2.0 ** 23
WTOP, HUGE = 2.0 ** 75, 2.0 ** 80
CFG = dict(ZC=[(0, 10, "S"), (10, 16, "V")], SYV=0, ZS=8, YS=4,
           CH=[(12, 16, "S"), (7, 12, "V"), (4, 7, "V")],
           HM=[], ODD=0, IMQ=1, KO=[1, -2, 4, -3, 2, 3], ORD=0, XL=32, AV=0, TO=("T1", "R1"), AS=32,
           RV=512)


def rank_program(g, core, T, topo):
    rank = T.rank_of(core)
    if rank is None:
        return
    QUEUE = {"V": g.vector, "S": g.scalar, "P": g.tensor, "G": g, "Y": g.sync}
    SEM = {"V": "cv", "S": "cs", "P": "cp", "G": "cg"}
    cnt = {"cv": 0, "cs": 0, "cp": 0, "cg": 0}
    total = {}
    seen = {q: {} for q in QUEUE}
    acc, past = {}, {}
    CH, AS, RV, ZS, YS = CFG["CH"], CFG["AS"], CFG["RV"], CFG["ZS"], CFG["YS"]

    def need(q, sem, val):
        if seen[q].get(sem, 0) < val:
            QUEUE[q].wait_ge(T.sem[sem], val)
            seen[q][sem] = val
            for s, v in past.get((sem, val), {}).items():
                seen[q][s] = max(seen[q].get(s, 0), v)

    def meet(a, b, s, a2, b2, s2):
        if b2 <= a or b <= a2:
            return False
        return s != s2 or (a - a2) % s == 0

    def order(q, reads, writes):
        w = {}
        for kind, regs in (("r", reads), ("w", writes)):
            for (n, a, b, s) in regs:
                ps = n[:2] == "ps"
                for (a2, b2, st2, k2, q2, s2, v2) in acc.get(n, ()):
                    if ps:
                        if q2 == q and (q == "P" or (kind == "r" and k2 == "r")):
                            continue
                    elif (kind == "r" and k2 == "r") or not meet(a, b, s, a2, b2, st2):
                        continue
                    w[s2] = max(w.get(s2, 0), v2)
        for s, v in sorted(w.items(), key=lambda x: -len(past.get(x, ()))):
            need(q, s, v)

    def record(q, reads, writes, sem, val):
        for kind, regs in (("r", reads), ("w", writes)):
            for (n, a, b, s) in regs:
                l = [e for e in acc.get(n, []) if e[:5] != (a, b, s, kind, q)]
                l.append((a, b, s, kind, q, sem, val))
                acc[n] = l

    def emit(q, calls, outs, ins):
        reads = [r for i in ins for r in i[1] + i[2]] + [r for o in outs for r in o[2]]
        writes = [r for o in outs for r in o[1]]
        order(q, reads, writes)
        for c in calls:
            last = c()
        s = SEM[q]
        cnt[s] += 1
        last.then_inc(T.sem[s], 1)
        past[s, cnt[s]] = dict(seen[q])
        record(q, reads, writes, s, cnt[s])

    def R(n, a, b, s=1):
        n, o = PART.get(n, (n, 0))
        a, b = a + o, b + o
        return (T[n][:, a:b] if s == 1 else T[n][:, a:b:s], [(n, a, b, s)], [])

    def C(n, c=0):
        return R(n, c, c + 1)

    def IND(n, a, b, off):
        w = R(n, a, b)
        return (w[0].indirect(off[0]), w[1], off[1])

    def tup(*xs):
        return [x for x in xs if isinstance(x, tuple)]

    def raw(x):
        return x[0] if isinstance(x, tuple) else x

    def vcopy(o, i):
        emit("V", [lambda: g.vector.tensor_copy(out=o[0], in_=i[0])], [o], [i])

    def vtt(o, a, b, op):
        emit("V", [lambda: g.vector.tensor_tensor(out=o[0], in0=a[0], in1=b[0], op=op)], [o], [a, b])

    def vts(o, a, s1, s2, op0, op1=None):
        if op1 is None:
            f = lambda: g.vector.tensor_scalar(out=o[0], in0=a[0], scalar1=raw(s1), scalar2=None, op0=op0)
        else:
            f = lambda: g.vector.tensor_scalar(out=o[0], in0=a[0], scalar1=raw(s1), scalar2=raw(s2), op0=op0, op1=op1)
        emit("V", [f], [o], [a] + tup(s1, s2))

    def vscan(o, d0, d1, init, op0, op1):
        emit("V", [lambda: g.vector.tensor_tensor_scan(out=o[0], data0=d0[0], data1=d1[0], initial=init, op0=op0, op1=op1)],
             [o], [d0, d1])

    def vset(o, c):
        emit("V", [lambda: g.vector.memset(o[0], c)], [o], [])

    def vtr(o, i):
        emit("V", [lambda: g.vector.transpose(out=o[0], in_=i[0])], [o], [i])

    def sact(o, i, func=AF.Copy, scale=1.0, bias=None):
        if bias is None:
            f = lambda: g.scalar.activation(out=o[0], in_=i[0], func=func, scale=scale)
        else:
            f = lambda: g.scalar.activation(out=o[0], in_=i[0], func=func, scale=scale, bias=raw(bias))
        emit("S", [f], [o], [i] + tup(bias))

    def mm(o, l, r, st, sp):
        return (lambda: g.tensor.matmul(o[0], l[0], r[0], st, sp)), o, l, r

    def pe(ms):
        emit("P", [m[0] for m in ms], [m[1] for m in ms], [x for m in ms for x in (m[2], m[3])])

    def giota(o, pat, base, ch):
        emit("G", [lambda: g.iota(o[0], pat, base, ch, allow_small_or_imprecise_dtypes=True)], [o], [])

    def dma(q, sem, o, i, tot=1):
        order(q, i[1] if tup(i) else [], o[1] if tup(o) else [])
        QUEUE[q].dma_start(out=raw(o), in_=raw(i)).then_inc(T.sem[sem], 16)
        total[sem] = 16 * tot
        record("D" + sem, i[1] if tup(i) else [], o[1] if tup(o) else [], sem, 16 * tot)

    a128 = lambda n: R(n, 0, 128)
    a64 = lambda n: R(n, 0, 64)
    ends = lambda n, a, k, s=16: R(n, a + s - 1, a + s * k, s)

    dma("Y", "ld_z", R("ZW0", OWN, OWN + 1024), T.z[:])
    dma("S", "ld_bz", R("bl", 16, 32), T.bz[:])
    dma("Y", "ld_m", R("ml", 0, 64), T.m[:])
    dma("S", "ld_bx", R("bl", 0, 16), T.bx[:])
    dma("Y", "ld_nz", R("tNZ", 0, 1024), T.nz[:])
    dma("Y", "ld_nb", R("tNB", 0, 1024), T.nb[:])
    dma("Y", "ld_im", R("ml", 64, 128), T.im[:])

    emit("G", [lambda: g.iota(T.c_p[:, 0:2], [[0, 2]], 0, 1)], [R("c_p", 0, 2)], [])
    giota(R("IOTA", 0, 128), [[1, 128]], 0, 0)
    giota(R("rows", 0, 32), [[0, 2], [1, 4], [16, 4]], 0, 0)
    giota(R("rows", 32, 48), [[1, 4], [32, 2], [96, 2]], 0, 0)
    giota(R("rows", 48, 64), [[1, 4], [32, 2], [-64, 2]], 80, 0)
    giota(R("pbase", 0, 8), [[64, 2], [4, 4]], 0, 0)
    giota(a128("gf"), [[1, 8], [0, 16]], 0, 0)
    giota(a128("itf"), [[0, 8], [1, 16]], 0, 0)
    vset(R("zeroF", 0, 336), 0.0)
    vts(R("fI", 0, 2), R("c_p", 0, 2), 15, None, O.bitwise_and)
    vts(R("gI", 0, 2), R("c_p", 0, 2), 4, None, O.arith_shift_right)
    vcopy(R("pf", 0, 2), R("c_p", 0, 2))
    vcopy(R("ff", 0, 2), R("fI", 0, 2))
    vcopy(R("gp", 0, 2), R("gI", 0, 2))
    vts(a128("identf"), R("IOTA", 0, 128), C("pf"), None, O.is_equal)
    vts(R("up", 0, 2), R("ff", 0, 2), 0.0, C("pf"), O.is_gt, O.mult)
    vtr(a64("cols"), a64("rows"))
    vts(a128("sub1"), R("IOTA", 0, 128), 1.0, C("up"), O.add, O.is_equal)
    vts(R("MF", 0, 4), R("pbase", 0, 4), C("cols", 32), None, O.add)
    vts(R("PERM", 0, 8), R("pbase", 0, 8), C("cols", 0), None, O.add)
    vset(R("zeroB", 0, 464), 0.0)
    vcopy(R("BL", 16, 32), R("bl", 16, 32))
    vts(a128("blkf"), a128("gf"), C("gp"), None, O.is_equal)
    for k in (128, 256, 512):
        sact(R("IOTA", k, 2 * k), R("IOTA", 0, k), AF.Identity, 1.0, float(k))
    sact(a128("identb"), a128("identf"))
    sact(a128("identn"), a128("identf"), AF.Copy, -1.0)

    def near(c):
        return topo.cores_of(c)

    def wmask(c, d):
        m = topo.mask(c, d)
        if d in near(c):
            for o in T.cores:
                if o not in near(c):
                    m &= ~topo.mask(c, o)
        return m

    def ones(m):
        return bin(m).count("1")

    def halves(m):
        es = [e for e in range(m.bit_length()) if m >> e & 1]
        lo = sum(1 << e for e in es[:len(es) // 2])
        return lo, m & ~lo

    def plan(s):
        ds = [T.cores[(T.rank_of(s) - d) % N] for d in (1, 2, 3)]
        rel = []
        for t in ds:
            twin = [u for u in ds if u != t and u in near(t)]
            if twin and topo.die(t) != topo.die(s) and not any(u in near(s) for u in ds):
                rel.append((twin[0], t))
        direct = [t for t in ds if t not in [x[1] for x in rel]]
        return sorted(direct, key=lambda t: t not in [x[0] for x in rel]), rel
    plans = {s: plan(s) for s in T.cores}
    late = [t for s in T.cores for (u, t) in plans[s][1]]
    duty = [(s, t) for s in T.cores for (u, t) in plans[s][1] if u == core]
    nsl = [0]

    def block(s, t):
        d = (T.rank_of(s) - T.rank_of(t)) % N
        return OWN + 1024 + 256 * (d - 1), OWN + 1280 + 256 * (d - 1)

    def calls(s, e):
        if plans[s][1]:
            return [[(w, [t], wmask(s, t))] for t in plans[s][0] for w in "ZY"]
        far = sorted([t for t in plans[s][0] if t not in near(s)], key=lambda t: t in late)
        by = [t for t in plans[s][0] if t in near(s)]
        if CFG["ODD"] == 2:
            return [[(w, ts, wmask(s, far[0]))] for ts in (far[:1] + by, far[1:]) for w in "ZY"]
        if CFG["ODD"] == 3:
            z, y = [[(w, [t], wmask(s, t)) for t in far[:1] + by + far[1:]] for w in "ZY"]
            h = halves(z[1][2])
            return [z[:2], y[:2], z[2:], y[2:]] if e else [z[:1], y[:1], z[2:], y[2:], [z[1][:2] + h[:1], y[1][:2] + h[1:]]]
        if CFG["ODD"]:
            z, y = [[(w, [t], wmask(s, t)) for t in far[:1] + by + far[1:]] for w in "ZY"]
            return ([z[:2]] if e else [z[:1], z[1:2]]) + [y[:2], z[2:], y[2:]]
        z, y = [[(w, ts, wmask(s, ts[0])) for ts in (far, by)] for w in "ZY"]
        return [z, y] if e else [z[:1], z[1:], y]

    def hmask(u, t, s, w, e):
        return topo.mask(u, s) if (w, e) in CFG["HM"] else wmask(u, t)

    def put(items):
        ts = []
        for (s, w, e, src, dsts, m) in items:
            order("G", src[1], [])
            ids = [DstId(rid=topo.addr(d, core)[0], pnc=topo.addr(d, core)[1]) for d in dsts]
            ts.append(RemoteDMATransfer(dst_ids=ids, dma_engine_mask=m, srcs=[src[0]],
                                        dsts=[R("%sW%d" % (w, e), *block(s, d))[0] for d in dsts],
                                        remote_sem=T.sem["%s%d_%d" % (w, e, T.rank_of(s))]))
            nsl[0] += ones(m)
        g.remote_dma_fused(ts, local_sem=T.sem.sl)

    def borders(e):
        k = CFG["SYV"] if e else 8
        if k:
            vcopy(R("SY", 256 * e, 256 * e + 16 * k), IND("YW%d" % e, OWN, OWN + 1024, R("BL", 0, k)))
        sact(R("SY", 256 * e + 16 * k, 256 * e + 256), IND("YW%d" % e, OWN, OWN + 1024, R("BL", k, 16)))
        for c in calls(core, e):
            put([(core, w, e, R("S" + w, 256 * e, 256 * e + 256), t, m) for (w, t, m) in c])
        for w in "ZY":
            win = "%sW%d" % (w, e)
            for s in T.cores:
                come = [m for c in calls(s, e) for (w2, ts, m) in c if w2 == w and core in ts]
                come += [hmask(u, t, s, w, e) for (u, t) in plans[s][1] if t == core]
                for m in come:
                    sem = "%s%d_%d" % (w, e, T.rank_of(s))
                    total[sem] = ones(m)
                    record("A" + sem, [], [(win,) + block(s, core) + (1,)], sem, ones(m))
            for (s, t) in duty:
                put([(s, w, e, R(win, *block(s, core)), [t], hmask(core, t, s, w, e))])

    def mlist(a):
        vcopy(R("mlf", 16, 80), R("ml", a, a + 64))
        vtr(R("mlt", 0, 64), R("mlf", 16, 80))
        vtr(R("mlt", 64, 160), R("mlf", 0, 96))
        vcopy(R("ML", a, a + 64), IND("mlt", 0, 160, R("MF", 0, 4)))
    vcopy(R("SZ", 0, 128), IND("ZW0", OWN, OWN + 1024, R("BL", 16, 24)))
    sact(R("SZ", 128, 256), IND("ZW0", OWN, OWN + 1024, R("BL", 24, 32)))
    for j, k in enumerate((16.0, 32.0, -16.0)):
        sact(R("Es", 144 * j + 15, 144 * j + 143, 16), R("blkf", 0, 128, 16), AF.Copy, k)
    sact(a64("brow"), a64("itf"), AF.Identity, -1.0, 15.0)
    mlist(0)
    vcopy(R("BL", 0, 16), R("bl", 0, 16))
    vcopy(R("YW0", OWN, OWN + 512), IND("ZW0", OWN, OWN + 1024, R("ML", 0, 32)))
    sact(R("YW0", OWN + 512, OWN + 1024), IND("ZW0", OWN, OWN + 1024, R("ML", 32, 64)))
    borders(0)

    giota(R("TH", 0, 576), [[0, 18], [1, 32]], -31, 0)
    sact(R("tM", OWN, OWN + 1024), IND("IOTA", 0, 1024, R("ML", 0, 64)))
    vset(a64("half"), 0.5)
    vts(a64("mask"), a64("itf"), C("ff"), None, O.is_equal)
    vts(a128("reset"), a128("itf"), 0.0, None, O.is_gt)
    vts(R("pa", 0, 8), R("gf", 0, 128, 16), C("gp"), None, O.add)
    vscan(a64("wrow"), a64("half"), a64("E1"), 2.0 * WTOP, O.mult, O.add)
    vts(R("pb", 0, 8), R("pa", 0, 8), 1, None, O.bitwise_and)
    vtt(a128("bidi"), a128("identf"), a128("sub1"), O.subtract)
    vts(R("fv", 0, 8), R("pb", 0, 8), 144.0, C("ff"), O.mult, O.add)
    vtt(a64("wm"), a64("wrow"), a64("mask"), O.mult)
    vtt(R("foldf", 0, 8), R("fv", 0, 8), R("IOTA", 0, 128, 16), O.add)
    mlist(64)

    def lane_lists(nbv):
        vcopy(R("nf", 16, 80), nbv)
        vscan(a64("scv"), a64("reset"), a64("mkv"), 0.0, O.mult, O.add)
        vcopy(R("mvl", 0, 4), ends("scv", 0, 4))
        vcopy(R("nf", 80, 144), IND("tNZ", 0, 1024, R("mvl", 0, 4)))
        pe([mm(R("ps5", 0, 160), a128("bidi"), R("nf", 0, 160), True, True)])
        vcopy(a128("L1"), IND("nf", 16, 144, R("PERM", 0, 8)))
        if nbv[2] and CFG["IMQ"]:
            vcopy(IND("tIM", 0, OWN + 1024, R("OFF", 4, 8)), R("NR", 0, 128, 2))
        vtr(R("TT", 0, 128), R("ps5", 16, 144))
        vtr(R("TT", 128, 288), R("ps5", 0, 160))
    vcopy(R("FOLD", 0, 8), R("foldf", 0, 8))
    vtt(a64("mkv"), R("tM", OWN, OWN + 1024, 16), a64("mask"), O.mult)
    lane_lists(R("tNB", 0, 1024, 16))
    sact(R("tIM", OWN, OWN + 1024), IND("IOTA", 0, 1024, R("ML", 64, 128)))

    vts(R("lane4", 0, 4), R("gf", 0, 64, 16), 16.0, C("ff"), O.mult, O.add)
    vts(a128("blkp"), a128("blkf"), 2.0, None, O.mult)
    vts(R("VL", 0, 4), R("lane4", 0, 4), 16.0, None, O.mult)

    def late_constants():
        vscan(a64("WL"), a64("reset"), a64("wm"), 0.0, O.mult, O.add)
        vts(a128("blkm"), a128("blkf"), -2.0, None, O.mult)
        sact(R("cst4", 0, 4), R("gf", 0, 64, 16), AF.Copy, -STEP)
        sact(a64("stepG"), a64("gf"), AF.Copy, STEP)
        sact(a64("offG"), a64("mask"), AF.Identity, FAR, -FAR)
        for n, k in enumerate((0.5, -2.5)):
            sact(R("offC", n, 128, 2), a64("mask"), AF.Identity, HUGE, -HUGE)
            sact(R("thrC", n, 128, 2), a64("wm"), AF.Copy, k)

    def last_constants():
        sact(a128("reset32"), a128("TH"), AF.Sign, 1.0, 31.0)
    sact(a128("blkH"), a128("blkf"), AF.Identity, -FAR, FAR)
    sact(R("selfC", 0, 32, 2), R("mask", 0, 16), AF.Copy, -3.0)
    sact(a128("identg"), a128("identf"), AF.Copy, -1.0)

    la, lq, lp, lw = [R("LL", 4 * n, 4 * n + 4) for n in range(4)]
    fa, fq, fp, fw = [ends("SC", 64 * n, 4) for n in range(4)]
    oa, oq, op, ow = [R("OFF", 4 * n, 4 * n + 4) for n in range(4)]
    sca = lambda n, off, d: vcopy(IND(n, 0, OWN + 1024, off), d)
    for r in range(3):
        more = r < 2
        Zn, Yn = "ZW%d" % r, "YW%d" % r
        Zall, Yall, Zown = (Zn, OWN, OWN + 1792), (Yn, OWN, OWN + 1792), (Zn, OWN, OWN + 1024)
        Mown, Iown = ("tM", OWN, OWN + 1024), ("tIM", OWN, OWN + 1024)
        K = R("ps3", 0, 64)
        pe([mm(K, a128("identb"), a64("brow"), True, False)])
        part = lambda n, a, b: R(n, 64 * a, 64 * b)
        Es = lambda j, f: R("Es", 144 * j + 15 - f, 144 * j + 143 - f)
        left = [16]

        def keys(j, n, a, b):
            left[0] -= (b - a) * (j != 2)
            pe([mm(K, Es(j, f), part(n, f, f + 1), False, left[0] == 0 and f == b - 1) for f in range(a, b)])
        for (a, b, who) in CFG["ZC"]:
            (sact if who == "S" else vcopy)(part("Zt", a, b), IND(*Zall, R("L1", 64 + 4 * a, 64 + 4 * b)))
        if YS:
            sact(part("Dt", 0, YS), IND(*Yall, R("L1", 0, 4 * YS)))
        for (a, b, who) in CH:
            vtt(part("Dt", a, b), IND(*Yall, R("L1", 4 * a, 4 * b)), part("Zt", a, b), O.subtract)
        dS = R("ps0", 0, 64 * YS)
        if YS:
            pe([mm(dS, a128("identb"), part("Dt", 0, YS), True, False), mm(dS, a128("identn"), part("Zt", 0, YS), False, True)])
        parts = CH + [(0, YS, "P")]
        for i in CFG["KO"]:
            a, b, who = parts[abs(i) - 1]
            if i < 0:
                keys(2, "Dt", a, b)
                continue
            if who == "V":
                vts(part("AD", a, b), part("Dt", a, b), 0.0, None, O.max)
            else:
                sact(part("AD", a, b), part("Dt", a, b) if who == "S" else dS, AF.Abs)
            keys(int(who == "V"), "AD", a, b)
        sact(a128("DL"), IND("TT", 0, 288, R("FOLD", 0, 8)))
        if r:
            if not CFG["IMQ"]:
                sca("tIM", oq, R("NR", 0, 128, 2))
            sca("tIM", op, R("NR", 1, 128, 2))
        else:
            late_constants()
        vscan(a64("Fs"), a64("reset"), K, 0.0, O.mult, O.max)
        if more:
            need("Y", "cv", cnt["cv"])
            if r == 0:
                dma("Y", "ld_x", R("tX", 0, 1024), T.x[:])
            for w in "ZY":
                dma("Y", "cp_%s%d" % (w, r), R("%sW%d" % (w, r + 1), OWN, OWN + 1024), R("%sW%d" % (w, r), OWN, OWN + 1024))
        vtt(a64("ns"), K, a64("Fs"), O.is_lt)
        vscan(R("SC", 64, 128), a64("ns"), R("DL", 64, 128), 0.0, O.mult, O.add)
        vscan(R("SC", 0, 64), a64("ns"), R("DL", 0, 64), 0.0, O.mult, O.add)
        vts(lq, fq, 1023.0, None, O.min)
        vts(la, fa, 1023.0, None, O.min)
        if r:
            sact(R("nth", 0, 16), IND("TH", 0, 576, C("thl")))
        if more:
            v = R("s6o", 2, 12, 3) if r else R("VL", 0, 4)
            sact(R("v5", 0, 4), v, AF.Identity, 5.0, 1.0)
            sact(R("v5", 4, 8), v, AF.Identity, 5.0, -510.5)
            sact(R("v5", 8, 12), R("v5", 4, 8), AF.Identity, 1.0 / 1024, ROUND)
            sact(R("v5", 12, 16), R("v5", 8, 12), AF.Identity, -1024.0, 1024.0 * ROUND)
        sact(R("rv", 8, 12), ends("Fs", 0, 4), AF.Relu, -VOID, 16.0 * VOID)
        sact(R("rv", 0, 8), ends("SC", 0, 8), AF.Relu, VOID, -1023.0 * VOID)
        vcopy(R("L2", 0, 64), IND("tNZ", 0, 1024, lq))
        vtt(R("mk2", 64, 128), IND(*Iown, lq), a64("mask"), O.mult)
        vtt(R("mk2", 0, 64), IND(*Mown, la), a64("mask"), O.mult)
        vcopy(R("L2", 64, 128), IND("tNB", 0, 1024, la))
        vd = R("ps4", 0, 4)
        pe([mm(vd, a128("identb"), R("cst4", 0, 4), True, False)] +
           [mm(vd, a128("identn"), R("rv", 4 * j, 4 * j + 4), False, j == 2) for j in range(3)])
        vscan(R("SC", 128, 256), a128("reset"), a128("mk2"), 0.0, O.mult, O.add)
        vcopy(R("LL", 8, 16), ends("SC", 128, 8))
        vcopy(R("L2", 192, 256), IND("tNB", 0, 1024, lw))
        vcopy(R("L2", 128, 192), IND("tNZ", 0, 1024, lp))
        Gn = R("ps6", 0, 64)
        CS = R("ps7", 0, 128)
        hf = lambda n, h: R(n, 512 * h, 512 * h + 512)
        lst = lambda j, h: R("L2", 64 * j + 32 * h, 64 * j + 32 * h + 32)
        bank = {("Bp", 0): "ps0", ("Bp", 1): "ps2", ("Bt", 0): "ps1", ("Bt", 1): "ps5"}

        def diff(src, h):
            o = R(bank[src, h], 0, 512)
            pe([mm(o, a128("identb"), hf(src, h), True, False), mm(o, a128("identn"), hf("At", h), False, True)])

        def term(n, l, last=False):
            pe([mm(Gn, a128(l), R(n, k, 1024, 16), False, last and k == 15) for k in range(16)])

        def relu(q, n, src, a, b):
            i = R(bank[src, a // 512], a % 512, a % 512 + b - a)
            if q == "V":
                vts(R(n, a, b), i, 0.0, None, O.max)
            else:
                sact(R(n, a, b), i, AF.Relu)
        pe([mm(Gn, a128("identb"), a64("offG"), True, False), mm(Gn, a128("identb"), a64("stepG"), False, False)])
        pe([mm(CS, a128("identb"), a128("offC"), True, False), mm(CS, a128("identb"), a128("thrC"), False, False)])
        def e1():
            if r:
                sact(ends("E1", 0, 4), vd, AF.Identity, 1.0, C("nth"))
            else:
                sact(ends("E1", 0, 4), vd)
        if CFG["ORD"] == 0:
            sact(hf("Bp", 0), IND(*Zall, lst(0, 0)))
            sact(hf("Bp", 1), IND(*Zall, lst(0, 1)))
            sact(R("At", 1024 - 16 * AS, 1024), IND(*Yall, R("L2", 256 - AS, 256)))
            vcopy(R("At", 0, 1024 - 16 * AS), IND(*Yall, R("L2", 192, 256 - AS)))
            sact(hf("Bt", 0), IND(*Zall, lst(2, 0)))
            sact(hf("Bt", 1), IND(*Zall, lst(2, 1)))
            vtt(R("T2", 0, 1024), IND(*Yall, R("L2", 64, 128)), R("Bp", 0, 1024), O.max)
            diff("Bp", 0)
            diff("Bp", 1)
            diff("Bt", 0)
            term("T2", "blkm")
            diff("Bt", 1)
            relu("V", "R2", "Bp", 0, RV)
            vtt(hf("T1", 0), IND(*Yall, lst(1, 0)), hf("Bt", 0), O.max)
            vtt(hf("T1", 1), IND(*Yall, lst(1, 1)), hf("Bt", 1), O.max)
            sact(R("NR", 0, 128, 2), IND(*Iown, lp))
            sact(R("NR", 1, 128, 2), IND(*Iown, lq))
            if RV < 512:
                relu("S", "R2", "Bp", RV, 512)
            relu("S", "R2", "Bp", 512, 1024)
            relu("S", "R1", "Bt", 0, 512)
            relu("S", "R1", "Bt", 512, 1024)
            e1()
            term("R2", "blkp")
            term("T1", "blkp")
            term("R1", "blkm", True)
        else:
            cols = lambda n, a, b: R(n, 16 * a, 16 * b)
            names = lambda j, a, b: R("L2", 64 * j + a, 64 * j + b)
            held = {}
            for st in CFG["SEQ"]:
                k, n = st[0], st[1]
                if k in "SV" and n in ("Bp", "Bt", "At"):
                    a, b = st[2:]
                    i = IND(*(Yall if n == "At" else Zall), names({"Bp": 0, "Bt": 2, "At": 3}[n], a, b))
                    (sact if k == "S" else vcopy)(cols(n, a, b), i)
                elif n in ("T1", "T2") and k == "V":
                    a, b = st[2:]
                    vtt(cols(n, a, b), IND(*Yall, names(1, a, b)), cols("Bt" if n == "T1" else "Bp", a, b), O.max)
                elif k == "D":
                    a, b, bk = st[2:]
                    held[n, a] = o = R("ps%d" % bk, 0, 16 * (b - a))
                    pe([mm(o, a128("identb"), cols(n, a, b), True, False), mm(o, a128("identn"), cols("At", a, b), False, True)])
                elif k == "P":
                    term(n, "blkp" if n in ("T1", "R2") else "blkm", st == CFG["SEQ"][-1])
                elif n == "NR":
                    sact(R("NR", 0, 128, 2), IND(*Iown, lp))
                    sact(R("NR", 1, 128, 2), IND(*Iown, lq))
                elif n == "E1":
                    e1()
                else:
                    a, b = st[2:]
                    i = held["Bt" if n == "R1" else "Bp", a]
                    if k == "V":
                        vts(cols(n, a, b), i, 0.0, None, O.max)
                    else:
                        sact(cols(n, a, b), i, AF.Relu)
        sact(a128("zz"), IND(*Zown, R("LL", 4, 12)))
        sact(R("xx", 0, 64), IND("tX", 0, 1024, la))
        sact(R("xx", 64, 128), IND("tX", 0, 1024, lw))
        if r == 0:
            last_constants()
        eqs, at = [], 0
        for c in range(4):
            for k in (16 * c + 15, 192 + 16 * c + 15):
                w = 128 - 32 * c
                vts(R("EQ", at, at + w), R("NR", 32 * c, 128), C("SC", k), None, O.is_equal)
                eqs.append((c, at, w))
                at += w
        sact(R("NLc", 0, 16), ends("SC", 0, 16), AF.Identity, 1.0, float(OWN))
        vscan(a64("GS"), Gn, a64("E1"), -4.0 * FAR, O.max, O.add)
        xz = R("ps4", 128, 256)
        pe([mm(xz, a128("identb"), a128("xx"), True, False), mm(xz, a128("identn"), a128("zz"), False, True)])
        sact(a128("cl"), xz, AF.Sign)
        for c in range(4):
            WT = R("WT", 128 * c, 128 * c + 128)
            vts(WT, a128("blkH"), C("GS", 16 * c + 15), C("WL", 16 * c + 15), O.is_lt, O.mult)
            pe([mm(R("ps7", 32 * c, 128), WT, R("EQ", at, at + w), False, False) for (c2, at, w) in eqs if c2 == c] +
               [mm(R("ps7", 32 * c, 32 * c + 32), WT, R("selfC", 0, 32), False, c == 3)])
        nzp = R("ps3", 128, 256)
        pe([mm(nzp, a128("identb"), a128("zz"), True, False), mm(nzp, a128("identb"), a128("cl"), False, True)])
        sact(a128("nzv"), nzp)
        sact(R("QP", 0, 64), IND(*Mown, lw))
        sact(R("QP", 64, 128), IND(*Mown, la))
        if r == 0:
            sact(a128("onesf"), a128("blkf"), AF.Identity, 0.0, 1.0)
        if more:
            sact(R("s6a", 1, 12, 3), R("rv", 4, 8), AF.Sign)
            for j, ts in enumerate(((("identf", R("v5", 0, 4)), ("identf", R("v5", 12, 16)), ("identg", fw)),
                                    (("identf", fw), ("identg", fa)), (("identf", fa),))):
                pe([mm(R("ps0", j, 12, 3), a128(l), x, i == 0, i == len(ts) - 1) for i, (l, x) in enumerate(ts)])
        vscan(a128("BS"), a128("reset32"), CS, 0.0, O.mult, O.max)
        for c in range(4):
            vts(R("OFF", c, 16, 4), R("NLc", c, 16, 4), C("BS", 32 * c + 31), C("lane4", c), O.subtract, O.max)
        e = r + 1 if more else r
        sca("ZW%d" % e, oq, R("nzv", 0, 64))
        if not more:
            sca("tM", oa, R("QP", 0, 64))
            sca("ZW%d" % e, op, R("nzv", 64, 128))
            dma("Y", "st_z", T.zo[:], R("ZW%d" % e, OWN, OWN + 1024))
            sca("tM", ow, R("QP", 64, 128))
            dma("S", "st_m", T.mo[:], (T.tM[0:128:16, OWN:OWN + 1024], [("tM", OWN, OWN + 1024, 1)], []))
            break
        vts(R("s6a", 2, 12, 3), ends("BS", 0, 4, 32), 0.0, None, O.is_gt)
        sca("ZW%d" % e, op, R("nzv", 64, 128))
        sact(R("SZ", 256 * e, 256 * e + 256), IND("ZW%d" % e, OWN, OWN + 1024, R("BL", 16, 32)))
        sca("YW%d" % e, oa, R("nzv", 0, 64))
        vscan(R("s6o", 0, 12), R("s6a", 0, 12), R("ps0", 0, 12), 0.0, O.mult, O.add)
        sca("YW%d" % e, ow, R("nzv", 64, 128))
        borders(e)
        cn = R("ps4", 256, 257)
        pe([mm(cn, a128("onesf"), C("s6a", 3 * c + 2), c == 0, c == 3) for c in range(4)])
        sca("tM", oa, R("QP", 0, 64))
        vcopy(R("vl", 0, 4), R("s6o", 2, 12, 3))
        sca("tM", ow, R("QP", 64, 128))
        vts(C("thl"), cn, 31.0, None, O.add)
        vtt(a64("mkv"), IND(*Mown, R("vl", 0, 4)), a64("mask"), O.mult)
        lane_lists(IND("tNB", 0, 1024, R("vl", 0, 4)))

    total.update(cnt)
    total["sl"] = nsl[0]
    for s, v in total.items():
        if max(seen[q].get(s, 0) for q in seen) < v:
            g.wait_ge(T.sem[s], v)
